import numpy as np, ml_dtypes
CORES = [24,25,26,27,28,29,30,31]
N = 8
import mx_ref
BF = ml_dtypes.bfloat16
def gcols(t, e):
    v = np.concatenate([t.reshape(8, 16, -1, 4), np.zeros((8, 16, 1, 4), BF)], axis=2)
    return np.ascontiguousarray(np.stack([v[g][:, e[g]] for g in range(8)])).reshape(128, -1)
def tile(rs):
    return np.stack(rs, axis=2).reshape(128, -1).astype(BF)
def pick(q, e):
    c = np.concatenate([q[0].reshape(128, -1, 4), np.zeros((128, 1, 4), np.uint8)], axis=1); s = np.concatenate([q[1], np.ones((16, 1), np.uint8)], axis=1)
    return (np.ascontiguousarray(c[:, e].reshape(128, -1)), np.ascontiguousarray(s[:, e]))
def join(*qs):
    return (np.concatenate([q[0] for q in qs], axis=1), np.concatenate([q[1] for q in qs], axis=1))
def put(q, e, v):
    c, s = q[0].reshape(128, -1, 4).copy(), q[1].copy(); c[:, e] = v[0].reshape(128, -1, 4); s[:, e] = v[1]
    return (c.reshape(128, -1), s)
def pk(c, s):
    return (np.ascontiguousarray(c), mx_ref.live(s))
def emit(q):
    return q[0], q[1]
def packed(v, rng):
    q = [mx_ref.quantize(np.ascontiguousarray(v[r])) for r in range(N)]
    return np.stack([a for a, b in q]), np.stack([mx_ref.plane(b, rng) for a, b in q])
def values_of_codes():
    e, c = np.zeros((128, 128, 4), np.float32), np.zeros((128, 2, 4), np.uint8)
    e[np.arange(128), np.arange(128), 0] = 1
    c[:127, :, 0] = np.arange(256).reshape(2, 128).T[:127]
    return mx_ref.matmul(mx_ref.quantize(e.reshape(128, 512).astype(BF)), (c.reshape(128, 8), np.full((16, 2), 127, np.uint8))).T.reshape(-1).astype(np.float64)
CODE_VALUE, SCALE_VALUE = values_of_codes(), 2.0 ** (np.arange(256) - 127.0)
def decode(q):
    return (CODE_VALUE[q[0]].reshape(16, 8, -1, 4) * SCALE_VALUE[q[1]][:, None, :, None] + 0.0).reshape(128, -1).astype(np.float32)
def f(rng, *shape):
    return mx_ref.flush((rng.standard_normal(shape, dtype=np.float32) * np.exp2(rng.integers(-2, 3, shape[:-1] + (1,)))).astype(BF))
def wide(rng, *shape, cols=0):
    v = rng.standard_normal(shape, dtype=np.float32) * np.exp2(rng.integers(-12, 13, shape)).astype(np.float32)
    if cols: v *= np.repeat(np.exp2(rng.integers(-cols, cols + 1, shape[:-2] + (1, shape[-1] // 4))) * (rng.random(shape[:-2] + (1, shape[-1] // 4)) > 0.0625), 4, axis=-1).astype(np.float32)
    return mx_ref.flush(v.astype(BF))
C, R = 320, 2
def alike(w):
    return np.stack([w] * N)
def layers(rng):
    return f(rng, N, 128, 4096)
def weights(rng, w, still=()):
    w = np.array(w).reshape(N, 8, 16, 8, 8, 16, 4)
    for i in still:
        w[:, :, i] = 0
        w[:, :, :, :, :, i] = 0
    c, p = packed(w.reshape(N, 128, 4096), rng)
    return {"wc": c, "ws": p}
def numbers_of(rng):
    return {"x": np.array(f(rng, N, 128, 4 * C)), "u": alike(f(rng, 128, 512)), "v": np.array(f(rng, N, 128, 512))}
def unscored(rng):
    a = np.array(f(rng, 128, 512)).reshape(128, 128, 4)
    a[:, ::16] = 0
    a[:, 1::16] = 0
    return a
def setup_inputs(rng):
    return {**numbers_of(rng), **weights(rng, layers(rng))}
def setup_inputs_ties(rng):
    d = numbers_of(rng)
    o = rng.permutation(N)
    k = rng.integers(0, 3, (N, 8, C))
    m = np.where((o % 2 == 0)[:, None, None], k, rng.integers(-2, 3, (N, 8, C)))
    k[o == 0] = 0
    m[o == 0] = 0
    k[o == 1] *= -1
    x = d["x"].reshape(N, 8, 16, C, 4)
    x[:, :, 0] = 0
    x[:, :, 0, :, 0] = k.astype(np.float32).astype(BF)
    x[:, :, 0, :, 1] = m.astype(np.float32).astype(BF)
    a = unscored(rng)
    for h in range(0, 128, 16):
        a[h, h, 0] = 1
        a[h, h + 1, 1] = 1
    return {"x": x.reshape(N, 128, 4 * C), "u": alike(a.reshape(128, 512)), "v": d["v"], **weights(rng, layers(rng), [0])}
def setup_inputs_near(rng):
    d = numbers_of(rng)
    x = d["x"].astype(np.float32).reshape(N, 8, 16, C, 4)
    x[:, :, 0] = 0
    x[:, :, 8:] = 0
    a = unscored(rng)
    o = rng.permutation(8) % 4
    for g in range(8):
        h = 16 * g
        for m in range(2):
            s = rng.integers(0, 16, (N, C))
            c = rng.integers(0, 2, (N, C)) * 2.0 - 1.0
            if o[g] < 3: x[:, g, 8 + m] = ((s[:, :, None] >> np.arange(4)) & 1) * np.exp2(np.arange(4) - 23.0)
            if o[g] < 2:
                k = 1.0 if o[g] == 0 else 2.0 ** -30
                x[:, g, 0, :, m] = c
                x[:, g, 11, :, 0] = 2.0 ** -10
                a[h, h + m, m] = k
                a[h + 8 + m, h + m] = k
                a[h + 11, h + m, 0] = k
            elif o[g] == 2:
                for r in range(N): x[r, g, 0, rng.permutation(C)[:2], m] = [1.0, -1.0]
                a[h, h + m, m] = 2.0 ** 30
                a[h + 8 + m, h + m] = 2.0 ** -30
            else:
                x[:, g, 10, :, m] = np.where(s % 2 == 0, 1.125 * 2.0 ** -30 * c, 0.0)
                x[:, g, 12, :, m] = np.where(s % 2 == 0, 0.0, 1.25 * 2.0 ** -30 * c)
                a[h + 10, h + m, m] = 1.125 * 2.0 ** -30
                a[h + 12, h + m, m] = 2.0 ** -30
    return {"x": x.reshape(N, 128, 4 * C).astype(BF), "u": alike(a.reshape(128, 512)), "v": d["v"], **weights(rng, layers(rng), [0, 8, 9, 10, 11, 12, 13, 14, 15])}
def setup_inputs_odd(rng):
    d = numbers_of(rng)
    a = (1.0 + (2 * rng.integers(0, 64, (N, 16, 8, C, 4)) + 1) * 2.0 ** -7) * np.exp2(-rng.integers(8, 15, (N, 16, 8, C, 4)).astype(np.float64))
    a = np.where(np.arange(8)[:, None, None] * 4 + np.arange(4) == rng.integers(0, 32, (N, 16, 1, C, 1)), 1.96875, a)
    a = a * (rng.integers(0, 2, a.shape) * 2.0 - 1.0) * np.exp2(rng.integers(-2, 3, (N, 16, 1, C, 1)).astype(np.float64))
    return {"x": a.astype(np.float32).reshape(N, 128, 4 * C).astype(BF), "u": d["u"], "v": d["v"], **weights(rng, layers(rng), [8, 9, 10, 11, 12, 13, 14, 15])}
def setup_inputs_ends(rng):
    d = numbers_of(rng)
    o = rng.permutation(N) % 4
    x = np.zeros((N, 8, 16, C, 4), np.float32)
    x[:, :, 8:12] = f(rng, N, 8, 4, C, 4).astype(np.float32) * np.float32(1024)
    for r in range(N):
        c = rng.integers(0, 2, C) * 2.0 - 1.0
        w = rng.choice([1.375, 1.5], (8, C))
        a, b = rng.permutation(C)[:2]
        w[:, b] = 1.625
        if o[r] == 0:
            w[:, a] = 1.625
            c[a], c[b] = 1.0, -1.0
        else: w[:, a] = 1.25
        if o[r] == 1: c[:] = -1.0
        if o[r] == 2: c[:] = 1.0
        e = w * c * 2.0 ** 29 if o[r] < 2 else np.ones((8, 1)) * c * 2.0 ** -30
        x[r, :, :8] = e[:, None, :, None]
        k = (rng.integers(0, 2, (128, 512)) * 2.0 - 1.0).astype(np.float32)
        if o[r] == 1: d["v"][r] = (k * np.float32(2.0 ** 30)).astype(BF)
        if o[r] == 2: d["v"][r] = (k * np.float32(2.0 ** -30)).astype(BF)
    u = unscored(rng).reshape(8, 16, 128, 4)
    p = rng.permutation(8)
    for g in range(8):
        k = (2.0 ** 30 if p[g] < 4 else 2.0 ** -29) * (1.0 if p[g] % 2 == 0 else -1.0)
        for m in range(2):
            u[:, :8, 16 * g + m] = 0.75 * k * (1 - 2 * m)
            u[g, :8, 16 * g + m] = k * (1 - 2 * m)
    w = ((rng.integers(0, 2, (N, 128, 4096)) * 2.0 - 1.0) * 2.0 ** -11).astype(np.float32).astype(BF)
    return {"x": x.reshape(N, 128, 4 * C).astype(BF), "u": alike(u.reshape(128, 512)), "v": d["v"], **weights(rng, w, [0, 1, 2, 3, 4, 5, 6, 7])}
def setup_inputs_spread(rng):
    d = numbers_of(rng)
    w = np.array(mx_ref.flush((layers(rng).astype(np.float32) * np.float32(2.0 ** -7)).astype(BF)))
    x = np.array(wide(rng, N, 128, 4 * C, cols=3))
    e = int(rng.integers(N))
    x[e] = ((1.0 + 0.25 * rng.random((128, 4 * C))) * 2.0 ** 24).astype(np.float32).astype(BF)
    w[e ^ 1] = (-0.1875 - 0.0625 * rng.random((128, 4096))).astype(np.float32).astype(BF)
    return {"x": x, "u": d["u"], "v": d["v"], **weights(rng, w)}
def check_inputs(d):
    b = []
    for k in ("x", "u", "v"):
        a = np.abs(d[k].astype(np.float32))
        if not (np.isfinite(a).all() and ((a == 0) | (a >= 2.0 ** -30) & (a <= 2.0 ** 30)).all()): b.append("a value of " + k)
    if (d["u"] != d["u"][:1]).any(): b.append("u isn't the same on all ranks")
    none, least, most = [emit(mx_ref.quantize(np.full((128, 16), k, np.float32).astype(BF)))[1][0, 0] for k in (0.0, 2.0 ** -30, 2.0 ** 30)]
    size = 0.0
    for r in range(N):
        if ((d["wc"][r] == 0x7F) | (d["wc"][r] == 0xFF)).any(): b.append("wc: a code that is no number")
        s = mx_ref.live(d["ws"][r])
        if ((s != none) & ((s < least) | (s > most))).any(): b.append("ws: a scale out of range")
        if (((d["wc"][r].reshape(16, 8, -1, 4) & 0x7F) != 0) & (s == none)[:, None, :, None]).any(): b.append("wc: a code other than zero where the scale is that of zeros")
        size = max(size, float(np.abs(decode(pk(d["wc"][r], d["ws"][r]))).max()))
    if not float(np.abs(d["x"].astype(np.float32)).max()) * (1.0 + 20.0 * size) * (1.0 + 20.0 * size) <= 900000000.0: b.append("the sizes of x and W together")
    return b
def places(s):
    o = np.argsort(-s, axis=1, kind="stable")
    i = np.zeros(s.shape, np.int64)
    np.put_along_axis(i, o, np.broadcast_to(np.arange(C), s.shape), axis=1)
    return o, i
def reference(x, u, v, wc, ws):
    qu = [mx_ref.quantize(u[r]) for r in range(N)]
    lay = [pk(wc[r], ws[r]) for r in range(N)]
    now = [x[r] for r in range(N)]
    total = np.zeros((N, C), np.int64)
    for t in range(R):
        q = [mx_ref.quantize(now[r]) for r in range(N)]
        full = [decode(q[r]).astype(BF) for r in range(N)]
        s = [mx_ref.matmul(qu[r], q[r]) + np.float32(0.0) for r in range(N)]
        first = [places(s[r][::16]) for r in range(N)]
        second = [places(s[r][1::16])[1] for r in range(N)]
        made = [None] * N
        for r in range(N):
            e = r ^ (1 << t)
            total[r] = first[r][1][0]
            took = np.zeros((8, C), np.int64)
            for g in range(8):
                turn = places(total[r][None])[1][0]
                took[g] = first[e][0][g][turn]
                total[r] = total[r] + second[e][g][took[g]]
            z = mx_ref.quantize(gcols(full[e], took))
            p = [mx_ref.matmul(pick(lay[r], np.arange(128 * b, 128 * b + 128)), z) for b in range(8)]
            y = tile([np.maximum(p[b], p[b + 4]) * np.float32(0.03125) for b in range(4)])
            back = gcols(decode(mx_ref.quantize(y)).astype(BF), np.argsort(took, axis=1))
            made[e] = (full[e].astype(np.float32) + back.astype(np.float32)).astype(BF)
        now = made
    y, tot = np.zeros((N, 128, C), np.float32), np.zeros((N, 1, C), np.float32)
    oc, osc = np.zeros((N, 128, 4 * C), np.uint8), np.zeros((N, 16, C), np.uint8)
    for r in range(N):
        q = mx_ref.quantize(now[r])
        y[r] = mx_ref.matmul(mx_ref.quantize(v[r]), q)
        tot[r, 0] = total[r]
        oc[r], osc[r] = emit(q)
    return {"y": y, "tot": tot, "oc": oc, "osc": osc}

@@ -1,0 +1,545 @@
+from concourse.mybir import dt, AluOpType as A, AxisListType, ActivationFunctionType as F
+
+NC = 320
+NG = 8
+NM = 20
+TILE = ((0, 128), (128, 128), (256, 192), (448, 320), (768, 320))
+BY_VECTOR, BY_SCALAR = (4, 1, 0), (2, 3)
+PIECE = (0, 128, 192)
+
+F32, BF, I32, U16, FP8, U8 = "float32", "bfloat16", "int32", "uint16", "float8_e4m3fn_x4", "uint8"
+SCRATCH = {"ps": ("psum", [128, 4096], F32)}
+
+
+def _sb(name, cols, dtype):
+    SCRATCH[name] = ("sbuf", [128, cols], dtype)
+
+
+def _mx(name, cols):
+    _sb(name + "c", cols, FP8)
+    _sb(name + "s", cols, U8)
+
+
+for _n, _c in (("tab0", NC), ("tier", NC), ("iot", NC), ("hcol", 1), ("pif", 1), ("trib", NC), ("ramp", NM),
+               ("mask8", 8), ("mask8n", 8), ("h8", 8), ("tiec", 4), ("triv", 128), ("lf", 48),
+               ("a0", 4), ("d0", 4), ("dg", 2 * NC), ("sc", 2 * NC), ("sx", 2 * NC), ("sg", 2 * NC), ("row", 2 * NC), ("cs", 2 * NC),
+               ("accA", NM), ("accB", NM), ("owA", NM), ("owB", NM), ("plA", NM), ("plB", NM),
+               ("bx", NC), ("cx", NC), ("ir", NC), ("di", NC), ("si", NC),
+               ("xn", 24), ("kr0", NC), ("kr1", NC), ("pk", 4), ("cnt", 4), ("ogd", 48), ("os1", 48),
+               ("sr", NC), ("rkd", NC), ("rks", NC), ("cc", 4 * NC), ("ysb", NC), ("tsb", NC), ("cw", NG * NC)):
+    _sb(_n, _c, F32)
+for _n, _c in (("ipr", NC), ("diag", NC), ("rst", NC), ("bdi", 512), ("gob", 512), ("go", 512), ("xt0", 4 * NC), ("xt1", 4 * NC),
+               ("ut", 512), ("vt", 512), ("ones", 512), ("ident", 128), ("et", 2048), ("wg", 4096), ("bd", 512), ("bg", 960), ("tri128", 128),
+               ("a0c", 3 * 448), ("eqb", 128), ("eq", 2 * NC), ("ee", 2 * NC), ("gt", 2 * NC), ("gg", 2 * NC), ("mtA", 4352), ("mtB", 4352),
+               ("junk", 4 * 448), ("cb", 328), ("ct", 4 * NC), ("nt", 512), ("zt", 4 * NC), ("yt", 4 * NC),
+               ("fp", 4 * NC), ("fs", 4 * NC), ("yp", 4 * NC)):
+    _sb(_n, _c, BF)
+_sb("pi_i", 4, I32)
+for _n, _c in (("l15", NM), ("lm", NM), ("lu", 24), ("aoff", NM), ("inva", NM), ("off", NM), ("offo", 4), ("noff", NM), ("koff", NM)):
+    _sb(_n, _c, U16)
+KE, KW, KB, KG, KO = 0, 512, 1536, 1664, 1904
+for _n, _c in (("xq0", NC), ("xq1", NC), ("xq2", NC), ("px0", NC), ("px1", NC), ("py0", NC), ("py1", NC), ("uq", 128), ("up", 384), ("vq", 128),
+               ("kq", 2032), ("mq", 2176), ("nq", 128), ("cq", NC), ("zq", NC), ("yq0", NC), ("yq1", NC), ("ww", 1024)):
+    _mx(_n, _c)
+
+SEMAPHORES = ["v", "s", "t", "gp", "ls"] + ["d%d" % k for k in range(16)] + ["rx%d" % k for k in range(8)]
+
+MG16 = 1.5 * 2.0 ** 27
+MG32 = 1.5 * 2.0 ** 28
+
+
+def rank_program(g, core, T, topo):
+    rank = T.rank_of(core)
+    if rank is None:
+        return
+    V, S, PE = g.vector, g.scalar, g.tensor
+    queues = {"v": V, "s": S, "t": PE, "gp": g, "sy": g.sync}
+    known = {q: {} for q in queues}
+    count = {"v": 0, "s": 0, "t": 0, "gp": 0}
+    state = {}
+    tally = {"dma": 0, "ls": 0, "junk": 0}
+
+    def st(k):
+        if k not in state:
+            state[k] = {"w": [], "r": [], "b": []}
+        return state[k]
+
+    def waits(eng, r, w, p):
+        deps = []
+        for k in r:
+            x = st(k)
+            deps += x["w"] + x["b"]
+            if k[:2] == "ps":
+                deps += [d for d in x["r"] if d[0] != eng]
+        for k in w:
+            x = st(k)
+            deps += x["w"] + x["r"] + x["b"]
+        for k in p:
+            x = st(k)
+            if x["r"]:
+                x["b"] = x["w"] + x["r"] + x["b"]
+                x["w"], x["r"] = [], []
+            deps += [d for d in x["b"] if not (eng == "t" and d[0] == "t")]
+        kn = known[eng]
+        best = {}
+        for d in deps:
+            if kn.get(d[0], 0) < d[1] and (d[0] not in best or best[d[0]][1] < d[1]):
+                best[d[0]] = d
+        items = list(best.values())
+        for d in items:
+            if any(o is not d and o[2].get(d[0], 0) >= d[1] for o in items):
+                continue
+            if kn.get(d[0], 0) < d[1]:
+                queues[eng].wait_ge(T.sem[d[0]], d[1])
+            for s, n in list(d[2].items()) + [(d[0], d[1])]:
+                if kn.get(s, 0) < n:
+                    kn[s] = n
+
+    def record(ev, r, w, p):
+        for k in r:
+            st(k)["r"].append(ev)
+        for k in w:
+            x = st(k)
+            x["w"], x["r"], x["b"] = [ev], [], [ev]
+        for k in p:
+            st(k)["w"].append(ev)
+
+    def do(eng, fn, r=(), w=(), p=()):
+        waits(eng, r, w, p)
+        count[eng] += 1
+        fn().then_inc(T.sem[eng], 1)
+        record((eng, count[eng], dict(known[eng])), r, w, p)
+
+    def dma(eng, out, in_, r=(), w=(), p=()):
+        waits(eng, r, w, p)
+        s = "d%d" % tally["dma"]
+        tally["dma"] += 1
+        queues[eng].dma_start(out, in_).then_inc(T.sem[s], 16)
+        record((s, 16, dict(known[eng])), r, w, p)
+
+    def engines_between(a, b):
+        return len(topo.engines(a, b))
+
+    def send(dst, rx, out, in_, r):
+        waits("gp", r, (), ())
+        rid, pid, _ = topo.addr(dst)
+        g.remote_dma(out, in_, T.sem["rx%d" % rx], T.sem["ls"], pid, rid, topo.mask(core, dst))
+        tally["ls"] += engines_between(core, dst)
+
+    def send_tile(t, rx, land, name):
+        q = partner(t)
+        send(q, rx, codes(land, 0, NC), codes(name, 0, NC), [name])
+        send(q, rx + 1, T[land + "s"][:, 0:NC], T[name + "s"][:, 0:NC], [name])
+        n = engines_between(q, core)
+        st(land)["w"] = [("rx%d" % rx, n, {}), ("rx%d" % (rx + 1), n, {})]
+
+    def partner(t):
+        return T.cores[rank ^ (1 << t)]
+
+    def codes(name, a, b):
+        return T[name + "c"][:, a:b].bitcast(dt.uint8)
+
+    def bank(k, a=0, b=NC):
+        return T.ps[:, 512 * k + a:512 * k + b]
+
+    def ps(k):
+        return "ps%d" % k
+
+    def plane(name, k, a=0, b=NC):
+        return T[name][:, k * NC + a:k * NC + b]
+
+    def half(name, n, a=0, b=NC, step=1):
+        o = NC if n == "B" else 0
+        return T[name][:, o + a:o + b:step]
+
+    def lasts(name, n):
+        return half(name, n, 15, NC, 16)
+
+    def junk(n):
+        k = tally["junk"] % 4
+        tally["junk"] += 1
+        return T.junk[:, 448 * k:448 * k + n], "junk%d" % k
+
+    def quant(name, a, b, tile, ta, r):
+        do("v", lambda: V.quantize_mx(T[name + "c"][:, a:b], T[name + "s"][:, a:b], T[tile][:, ta:ta + 4 * (b - a)]), r=r, p=[name])
+
+    def mm(k, n, left, la, right, ra, start=True, stop=True, key=None):
+        kw = {"w": [ps(k)]} if start else {"p": [ps(k)]}
+        do("t", lambda: PE.matmul_mx(bank(k, 0, n), T[left + "c"][:, la:la + 128], T[left + "s"][:, la:la + 128],
+                                     T[right + "c"][:, ra:ra + n], T[right + "s"][:, ra:ra + n], start, stop), r=[left, key or right], **kw)
+
+    def ts(out, in0, s1, s2, op0, op1=None, **k):
+        if op1 is None:
+            do("v", lambda: V.tensor_scalar(out, in0, s1, s2, op0), **k)
+        else:
+            do("v", lambda: V.tensor_scalar(out, in0, s1, s2, op0, op1), **k)
+
+    def tt(out, a, b, op, **k):
+        do("v", lambda: V.tensor_tensor(out, a, b, op), **k)
+
+    def vcopy(out, in_, **k):
+        do("v", lambda: V.tensor_copy(out, in_), **k)
+
+    def scopy(out, in_, scale=1.0, **k):
+        do("s", lambda: S.activation(out, in_, F.Copy, scale=scale), **k)
+
+    def ssum(in_, n, col, key, r):
+        j, jk = junk(n)
+        do("s", lambda: S.activation(j, in_, F.Copy, accum_out=col), r=r, w=[jk], p=[key])
+
+    def scan(out, d1, n=NC, **k):
+        do("v", lambda: V.tensor_tensor_scan(out, T.rst[:, 0:n], d1, 0.0, A.mult, A.add), **k)
+
+    def fill(ap, c, key):
+        do("v", lambda: V.memset(ap, c), w=[key])
+
+    def iota(name, a, b, pattern, base, cm):
+        ap = T[name][:, a:b]
+        if name == "pi_i":
+            do("gp", lambda: g.iota(ap, pattern, base, cm), p=[name])
+        else:
+            do("gp", lambda: g.iota(ap, pattern, base, cm, allow_small_or_imprecise_dtypes=True), p=[name])
+
+    dma("sy", T.xt0[:, :], T.x[:, :], p=["xt0"])
+    dma("s", T.ut[:, :], T.u[:, :], w=["ut"])
+    dma("sy", codes("ww", 0, 1024), T.wc[:, :], p=["ww"])
+    dma("sy", T.wws[:, :], T.ws[:, :], p=["ww"])
+    dma("sy", T.vt[:, :], T.v[:, :], w=["vt"])
+
+    iota("lf", 0, 8, [[16, 8]], 0, 0)
+    iota("lf", 8, 16, [[16, 8]], 1, 0)
+    iota("lf", 16, 24, [[0, 8]], 0, 0)
+    iota("triv", 0, 128, [[1, 128]], 0, -1)
+    iota("pi_i", 0, 1, [[0, 1]], 0, 1)
+    iota("h8", 0, 8, [[1, 8]], 0, 0)
+    iota("tiec", 0, 2, [[-128, 2]], 511, -1)
+    iota("tiec", 2, 3, [[0, 1]], 511 - PIECE[2], -1)
+    fill(T.ones[:], 1.0, "ones")
+    fill(T.et[:], 0.0, "et")
+    fill(T.nt[:], 0.0, "ntz")
+    vcopy(T.lu[:], T.lf[:, 0:24], r=["lf"], w=["lu"])
+    ts(T.tri128[:], T.triv[:], 0.0, None, A.is_lt, r=["triv"], w=["tri128"])
+    ts(T.ident[:], T.triv[:], 0.0, None, A.is_equal, r=["triv"], w=["ident"])
+    fill(T.cb[:, NC:328], -40.0, "cbz")
+    fill(T.bg[:], 0.0, "bg")
+    for n in "BA":
+        fill(T["acc" + n][:, 0:1], 0.0, "acc0" + n)
+        for u, (o, w) in enumerate(TILE):
+            a, b = 4 * o + 256 * u, 4 * (o + w)
+            scopy(T["mt" + n][:, a:b], T.ones[:, 0:b - a], 0.0, r=["ones"], w=["mz%s%d" % (n, u)])
+
+    quant("xq0", 0, NC, "xt0", 0, ["xt0"])
+    quant("uq", 0, 128, "ut", 0, ["ut"])
+    do("v", lambda: V.tensor_copy(T.upc[:, 0:384].bitcast(dt.uint32), T.uqc[:, 0:128].bitcast(dt.uint32).indirect(T.lu[:, 0:24])), r=["uq", "lu"], p=["up"])
+    do("s", lambda: S.activation(T.ups[:, 0:384], T.uqs[:, 0:128].indirect(T.lu[:, 0:24]), F.Copy), r=["uq", "lu"], p=["up"])
+    send_tile(0, 0, "px0", "xq0")
+
+    def early_constants():
+        iota("ipr", 0, NC, [[0, NM], [1, 16]], 0, 0)
+        iota("bdi", 0, 512, [[0, 8], [1, 16], [0, 4]], 0, 0)
+        iota("lf", 24, 44, [[16, NM]], 15, 0)
+        iota("gob", 0, 512, [[1, 8], [0, 64]], 0, 0)
+        iota("tier", 0, NC, [[-1, NC]], 511, 0)
+        iota("tab0", 0, NC, [[-1, NC]], 319, 0)
+        iota("iot", 0, NC, [[1, NC]], 0, 0)
+        ts(T.pi_i[:, 1:2], T.pi_i[:, 0:1], 15, None, A.bitwise_and, r=["pi_i"], w=["pi1"])
+        ts(T.pi_i[:, 2:3], T.pi_i[:, 0:1], 4, None, A.arith_shift_right, r=["pi_i"], w=["pi2"])
+        ts(T.tiec[:, 0:3], T.tiec[:, 0:3], 1.0 / 512, 1.0 / 1024, A.mult, A.add, w=["tiec"])
+        vcopy(T.hcol[:], T.pi_i[:, 2:3], r=["pi2"], w=["hcol"])
+        vcopy(T.pif[:], T.pi_i[:, 1:2], r=["pi1"], w=["pif"])
+        ts(T.mask8[:], T.h8[:], T.hcol[:, 0:1], None, A.is_equal, r=["h8", "hcol"], w=["mask8"])
+        ts(T.mask8n[:], T.h8[:], T.hcol[:, 0:1], -0.5, A.is_equal, A.mult, r=["h8", "hcol"], w=["mask8n"])
+        for b in range(4):
+            scopy(T.et[:, 512 * b + b:512 * (b + 1):4], T.ident[:], r=["ident", "et"], w=["et%d" % b])
+
+    def middle_constants():
+        for h in range(NG):
+            scopy(T.wg[:, 512 * h:512 * h + 512], T.ones[:], T.mask8[:, h:h + 1], r=["ones", "mask8"], p=["wg%d" % (h // 4)])
+        scopy(T.tier[:], T.tier[:], 1.0 / 512, w=["tier"])
+        ts(T.diag[:], T.ipr[:], T.pif[:, 0:1], None, A.is_equal, r=["ipr", "pif"], w=["diag"])
+        ts(T.rst[:], T.ipr[:], 0.0, None, A.is_gt, r=["ipr"], w=["rst"])
+        ts(T.bd[:], T.bdi[:], T.pif[:, 0:1], None, A.is_equal, r=["bdi", "pif"], w=["bd"])
+        vcopy(T.l15[:], T.lf[:, 24:44], r=["lf"], w=["l15"])
+        quant("kq", KB, KB + 128, "bd", 0, ["bd"])
+        vcopy(T.bg[:, 448:512], T.bd[:, 0:64], r=["bd"], w=["bg"])
+        ts(T.go[:], T.gob[:], T.hcol[:, 0:1], None, A.is_equal, r=["gob", "hcol"], w=["go"])
+        quant("kq", KG, KG + 240, "bg", 0, ["bg"])
+        ts(T.lm[:], T.lf[:, 24:44], -15.0, 0.0625, A.add, A.mult, r=["lf"], w=["lm"])
+        ts(T.ramp[:], T.lf[:, 24:44], -15.0, None, A.add, r=["lf"], w=["ramp"])
+        quant("kq", KO, KO + 128, "go", 0, ["go"])
+        ts(T.trib[:], T.ipr[:], T.pif[:, 0:1], 1e29, A.is_ge, A.mult, r=["ipr", "pif"], w=["trib"])
+
+    def own_places(X):
+        mm(0, NC, "up", 256, X, 0)
+        for c in range(3):
+            mm(1 + c, 128, X, PIECE[c], "uq", 0)
+        for c in range(3):
+            o, sc, k, rr = PIECE[c], bank(1 + c, 0, 1), 448 * c, [ps(0), ps(1 + c)]
+            key = "a0c%d" % c
+            ts(T.eqb[:], bank(0, o, o + 128), sc, None, A.is_equal, r=rr, w=["eqb"])
+            if o:
+                ts(T.a0c[:, k:k + o], bank(0, 0, o), sc, None, A.is_ge, r=rr, p=[key])
+            ts(T.a0c[:, k + o:k + NC], bank(0, o, NC), sc, None, A.is_gt, r=rr, p=[key])
+            tt(T.a0c[:, k + NC:k + NC + 128], T.eqb[:], T.tri128[:], A.mult, r=["eqb", "tri128"], p=[key])
+            ssum(T.a0c[:, k:k + 448], 448, T.a0[:, c:c + 1], "a0", [key])
+
+    def block_of(c):
+        return (8 * c, 8 * c + 8, 0, 8) if c < 2 else (16, 20, 4, 8)
+
+    def digits_high():
+        ts(T.nt[:, 0:4 * NM:4], T.xn[:, 0:NM], MG16, MG16, A.add, A.subtract, r=["xn", "ntz"], w=["nthi"])
+
+    def digits_low_and_spread(h):
+        tt(T.nt[:, 1:4 * NM:4], T.xn[:, 0:NM], T.nt[:, 0:4 * NM:4], A.subtract, r=["xn", "nthi", "ntz"], w=["ntlo"])
+        do("v", lambda: V.quantize_mx(T.nqc[:, 0:128], T.nqs[:, 0:128], T.nt[:, 0:512]), r=["nthi", "ntlo", "ntz"], w=["nq"])
+        mm(6, 128, "kq", KB, "nq", 0)
+        mm(7, 128, "kq", KG + 112 - 16 * h, "nq", 0, h == 0, h == NG - 1)
+
+    def take_offsets():
+        ts(T.off[:], bank(6, 0, NM), 160.0, None, A.add, r=[ps(6)], w=["off"])
+
+    def score_columns(n, k):
+        tt(half("dg", n), bank(k), T.diag[:], A.mult, r=[ps(k), "diag"], w=["dg" + n])
+        scopy(half("row", n), bank(k), r=[ps(k)], w=["row" + n])
+        scan(half("sc", n), half("dg", n), r=["rst", "dg" + n], w=["sc" + n])
+
+    def blocks(u):
+        return range(max(1, 4 * u), 4 * u + 4)
+
+    def part(n, m):
+        o, e = 4 * TILE[m // 4][0], m % 4
+        return T["mt" + n][:, o + e:o + 64 * m:4]
+
+    def score(n, m):
+        return half("sc", n, 16 * m + 15, 16 * m + 16)
+
+    def compare(n, k):
+        for u in BY_VECTOR:
+            for m in blocks(u):
+                ts(part(n, m), bank(k, 0, 16 * m), score(n, m), None, A.is_lt, r=[ps(k), "sc" + n, "mz%s%d" % (n, u)], w=["mt%s%d" % (n, m)])
+
+    def scalar_compare(n):
+        late = None
+        for m in [m for u in BY_SCALAR for m in blocks(u)] + [None]:
+            if m is not None:
+                j, jk = junk(16 * m)
+                do("s", lambda: S.activation(j, half("row", n, 0, 16 * m), F.Sign, bias=score(n, m), scale=-1.0), r=["row" + n, "sc" + n], w=[jk])
+            if late:
+                q, i, ik = late
+                do("s", lambda: S.activation(part(n, q), i, F.Relu, accum_out=T["acc" + n][:, q:q + 1]),
+                   r=[ik, "mz%s%d" % (n, q // 4)], w=["mt%s%d" % (n, q)], p=["acc" + n])
+            late = (m, j, jk)
+
+    def add_up(n):
+        for u in BY_VECTOR:
+            for m in blocks(u):
+                ssum(part(n, m), 16 * m, T["acc" + n][:, m:m + 1], "acc" + n, ["mt%s%d" % (n, m)])
+
+    def tile_sums(n, us, to):
+        for u in us:
+            (o, w), key = TILE[u], "mq%s%d" % (n, u)
+            c = o + (1088 if n == "B" else 0)
+            do("v", lambda: V.quantize_mx(T.mqc[:, c:c + w], T.mqs[:, c:c + w], T["mt" + n][:, 4 * o:4 * (o + w)]),
+               r=["mz%s%d" % (n, u)] + ["mt%s%d" % (n, m) for m in blocks(u)], w=[key])
+            mm(to, w, "kq", KO, "mq", c, u == BY_VECTOR[0], u == BY_SCALAR[-1], key)
+
+    def spread_scores(n):
+        scopy(half("sg", n), half("sc", n).indirect(T.l15[:, 0:NM]), r=["sc" + n, "l15"], w=["sg" + n])
+
+    def equals_in_block(n, k):
+        tt(half("sx", n), half("sc", n).indirect(T.l15[:, 0:NM]), T.trib[:], A.add, r=["sc" + n, "l15", "trib"], w=["sx" + n])
+        tt(half("eq", n), bank(k), half("sx", n), A.is_equal, r=[ps(k), "sx" + n], w=["eq" + n])
+        scan(half("ee", n), half("eq", n), r=["rst", "eq" + n], w=["ee" + n])
+
+    def larger_in_block(n, k):
+        tt(half("gt", n), bank(k), half("sg", n), A.is_gt, r=[ps(k), "sg" + n], w=["gt" + n])
+        tt(T["ow" + n][:], T.ramp[:], lasts("ee", n), A.add, r=["ramp", "ee" + n], w=["ow" + n])
+        scan(half("gg", n), half("gt", n), r=["rst", "gt" + n], w=["gg" + n])
+
+    def place(n, to):
+        ow = T["ow" + n]
+        tt(T.rkd[:], bank(to), T.diag[:], A.mult, r=[ps(to), "diag"], w=["rkd"])
+        tt(ow[:], ow[:], lasts("gg", n), A.add, r=["gg" + n], w=["ow" + n])
+        scan(half("cs", n), T.rkd[:], r=["rst", "rkd"], w=["cs" + n])
+        tt(ow[:], ow[:], T["acc" + n][:], A.subtract, r=["acc" + n, "acc0" + n], w=["ow" + n])
+        tt(T["pl" + n][:], ow[:], lasts("cs", n), A.add, r=["ow" + n, "cs" + n], w=["pl" + n])
+
+    def table(h):
+        mm(h % 4, NC, "kq", KW + 128 * h, "cq", 0)
+
+    def copy_table(h):
+        k = h % 4
+        if h == 0:
+            tt(plane("cw", 0), bank(k), T.tab0[:], A.add, r=[ps(k), "tab0"], w=["cw0"])
+        else:
+            scopy(plane("cw", h), bank(k), r=[ps(k)], w=["cw%d" % h])
+
+    def look_up(h, prev):
+        new = "kr%d" % (h % 2)
+        tt(T[new][:], plane("cw", h).indirect(T.off[:, 0:NM]), T[prev][:], A.add, r=["cw%d" % h, "off", prev], w=[new])
+        return new
+
+    def count_teams(prev, c):
+        j, jk = junk(NC)
+        do("s", lambda: S.activation(j, T[prev][:], F.Sign, bias=T.pk[:, c:c + 1], scale=-1.0, accum_out=T.cnt[:, c:c + 1]),
+           r=[prev, "pk"], w=["cnt%d" % c, jk])
+
+    def draft_round(t):
+        X, PX, PY, YQ = "xq%d" % t, "px%d" % t, "py%d" % t, "yq%d" % t
+        last = t == 1
+        if t == 0:
+            early_constants()
+        own_places(X)
+        if t == 0:
+            middle_constants()
+        ts(T.d0[:, 0:3], T.a0[:, 0:3], -1.0, 159.0, A.mult, A.add, r=["a0"], w=["d0"])
+        for c in range(3):
+            a, b, ma, mb = block_of(c)
+            ts(T.xn[:, a:b], T.mask8[:, ma:mb], T.d0[:, c:c + 1], None, A.mult, r=["mask8", "d0"], p=["xn"])
+        digits_high()
+        ts(T.offo[:, 0:3], T.d0[:, 0:3], 160.0, None, A.add, r=["d0"], w=["offo"])
+        digits_low_and_spread(0)
+        if t == 0:
+            quant("kq", KE, KE + 512, "et", 0, ["et", "et0", "et1", "et2", "et3"])
+            fill(T.ct[:], 0.0, "ct")
+        mm(5, NC, "up", 128, PX, 0)
+        mm(4, NC, "up", 0, PX, 0)
+        take_offsets()
+        score_columns("B", 5)
+        score_columns("A", 4)
+        compare("B", 5)
+        scalar_compare("B")
+        tile_sums("B", BY_VECTOR, 3)
+        spread_scores("B")
+        add_up("B")
+        equals_in_block("B", 5)
+        compare("A", 4)
+        scalar_compare("A")
+        spread_scores("A")
+        add_up("A")
+        tile_sums("A", BY_VECTOR, 6)
+        tile_sums("B", BY_SCALAR, 3)
+        larger_in_block("B", 5)
+        equals_in_block("A", 4)
+        place("B", 3)
+        if t == 0:
+            quant("kq", KW, KW + 512, "wg", 0, ["wg0"])
+            quant("kq", KW + 512, KW + 1024, "wg", 2048, ["wg1"])
+        tile_sums("A", BY_SCALAR, 6)
+        for b in range(4):
+            k = (0, 1, 2, 0)[b]
+            mm(k, NC, "kq", KE + 128 * b, PX, 0)
+            scopy(plane("fp", b), bank(k), r=[ps(k)], w=["fp%d" % b])
+        larger_in_block("A", 4)
+        tt(T.bx[:], T.plB[:, 0:NM].indirect(T.lm[:, 0:NM]), T.diag[:], A.mult, r=["plB", "lm", "diag"], w=["bx"])
+        place("A", 6)
+        vcopy(T.aoff[:], T.plA[:], r=["plA"], w=["aoff"])
+        vcopy(T.cx[:, 0:NC].indirect(T.aoff[:, 0:NM]), T.bx[:], r=["aoff", "bx"], w=["cx"])
+        ts(T.ct[:, 0:4 * NC:4], T.cx[:], MG32, MG32, A.add, A.subtract, r=["cx", "ct"], w=["cthi"])
+        tt(T.ct[:, 1:4 * NC:4], T.cx[:], T.ct[:, 0:4 * NC:4], A.subtract, r=["cx", "cthi", "ct"], w=["ctlo"])
+        quant("cq", 0, NC, "ct", 0, ["cthi", "ctlo", "ct"])
+        for h in range(4):
+            table(h)
+        vcopy(T.pk[:, 0:3], T.tiec[:, 0:3], r=["tiec"], w=["pk"])
+        copy_table(0)
+        copy_table(1)
+        prev = "tier"
+        for h in range(NG):
+            own = h < NG - 1
+            if h:
+                ns = 3 if h < 3 else 2
+                for c in range(ns):
+                    count_teams(prev, c)
+                for c in range(ns):
+                    a, b, ma, mb = block_of(c)
+                    scopy(T.xn[:, a:b], T.mask8n[:, ma:mb], T.cnt[:, c:c + 1], r=["mask8n", "cnt%d" % c], p=["xn"])
+                if h == 1:
+                    vcopy(T.ir[:, 0:NC].indirect(T.aoff[:, 0:NM]), T.iot[:], r=["aoff", "iot"], w=["ir"])
+                elif h == 2:
+                    tt(T.di[:], T.ir[:], T.diag[:], A.mult, r=["ir", "diag"], w=["di"])
+                    scan(T.si[:], T.di[:], r=["rst", "di"], w=["si"])
+                    vcopy(T.inva[:], T.si[:, 15:NC:16], r=["si"], w=["inva"])
+                else:
+                    ts(T.cb[:, 0:NC], T[prev][:], T.pk[:, 2:3], 2.0, A.is_lt, A.mult, r=[prev, "pk"], w=["cb"])
+                    do("v", lambda: V.tensor_reduce(T.cnt[:, 2:3], T.cb[:], AxisListType.X, A.add), r=["cb", "cbz"], w=["cnt2"])
+                    a, b, ma, mb = block_of(2)
+                    ts(T.xn[:, a:b], T.mask8n[:, ma:mb], T.cnt[:, 2:3], None, A.mult, r=["mask8n", "cnt2"], p=["xn"])
+                digits_high()
+                if own:
+                    ts(T.offo[:, 0:3], T.cnt[:, 0:3], -0.5, 160.0, A.mult, A.add, r=["cnt0", "cnt1", "cnt2"], w=["offo"])
+                digits_low_and_spread(h)
+            if own:
+                tt(T.ogd[:], plane("cw", h).indirect(T.offo[:, 0:3]), T.diag[:, 0:48], A.mult, r=["cw%d" % h, "offo", "diag"], w=["ogd"])
+                scan(T.os1[:], T.ogd[:], 48, r=["rst", "ogd"], w=["os1"])
+                if h:
+                    take_offsets()
+                tt(T.pk[:, 0:3], T.pk[:, 0:3], T.os1[:, 15:48:16], A.add, r=["os1"], w=["pk"])
+                prev = look_up(h, prev)
+            if h < 4:
+                table(h + 4)
+            if 1 <= h < NG - 1:
+                copy_table(h + 1)
+            if 3 <= h <= 6:
+                scopy(plane("fs", h - 3), plane("fp", h - 3).indirect(T.inva[:, 0:NM]), r=["fp%d" % (h - 3), "inva"], w=["fs%d" % (h - 3)])
+        ts(T.noff[:], bank(7, 0, NM), 160.0, None, A.add, r=[ps(7)], w=["noff"])
+        if last:
+            take_offsets()
+        for k in range(2):
+            vcopy(T.zt[:, k:4 * NC:4], plane("fs", k).indirect(T.noff[:, 0:NM]), r=["fs%d" % k, "noff"], p=["zt"])
+            j = 2 + k
+            scopy(T.zt[:, j:4 * NC:4], plane("fs", j).indirect(T.noff[:, 0:NM]), r=["fs%d" % j, "noff"], p=["zt"])
+        quant("zq", 0, NC, "zt", 0, ["zt"])
+        for b in range(4):
+            mm(4 + b, NC, "ww", 128 * (b + 4), "zq", 0)
+            mm(b, NC, "ww", 128 * b, "zq", 0)
+            scopy(plane("cc", b), bank(4 + b), r=[ps(4 + b)], w=["cc%d" % b])
+
+        def larger(b):
+            tt(plane("yp", b), bank(b), plane("cc", b), A.max, r=[ps(b), "cc%d" % b], w=["yp%d" % b])
+
+        vcopy(T.sr[:, 0:NC].indirect(T.noff[:, 0:NM]), T.iot[:], r=["noff", "iot"], w=["sr"])
+        larger(0)
+        tt(T.rkd[:], T.sr[:, 0:NC].indirect(T.aoff[:, 0:NM]), T.diag[:], A.mult, r=["sr", "aoff", "diag"], w=["rkd"])
+        larger(1)
+        scan(T.rks[:], T.rkd[:], r=["rst", "rkd"], w=["rks"])
+        larger(2)
+        vcopy(T.koff[:], T.rks[:, 15:NC:16], r=["rks"], w=["koff"])
+        larger(3)
+        for k in range(2):
+            scopy(T.yt[:, k:4 * NC:4], plane("yp", k).indirect(T.koff[:, 0:NM]), 0.03125, r=["yp%d" % k, "koff"], p=["yt"])
+            j = 2 + k
+            ts(T.yt[:, j:4 * NC:4], plane("yp", j).indirect(T.koff[:, 0:NM]), 0.03125, None, A.mult, r=["yp%d" % j, "koff"], p=["yt"])
+        quant(YQ, 0, NC, "yt", 0, ["yt"])
+        send_tile(t, 4 * t + 2, PY, YQ)
+        if last:
+            prev = look_up(NG - 1, prev)
+            tt(T.tsb[0:1, :], T[prev][0:1, :], T.tier[0:1, :], A.subtract, r=[prev, "tier"], w=["tsb"])
+            dma("sy", T.tot[:, :], T.tsb[0:1, :], r=["tsb"])
+        else:
+            quant("vq", 0, 128, "vt", 0, ["vt"])
+        for b in range(4):
+            mm(b, NC, "kq", KE + 128 * b, X, 0, True, False)
+        for b in range(4):
+            mm(b, NC, "kq", KE + 128 * b, PY, 0, False, True)
+            cp = scopy if b % 2 else vcopy
+            cp(T.xt1[:, b:4 * NC:4], bank(b), r=[ps(b)], p=["xt1"])
+        quant("xq%d" % (t + 1), 0, NC, "xt1", 0, ["xt1"])
+
+    draft_round(0)
+    send_tile(1, 4, "px1", "xq1")
+    draft_round(1)
+
+    mm(4, NC, "vq", 0, "xq2", 0)
+    dma("sy", T.oc[:, :], codes("xq2", 0, NC), r=["xq2"])
+    for k in range(4):
+        dma("sy", T.osc[4 * k:4 * k + 4, :], T.xq2s[32 * k:32 * k + 4, 0:NC], r=["xq2"])
+    scopy(T.ysb[:], bank(4), r=[ps(4)], w=["ysb"])
+    dma("s", T.y[:, :], T.ysb[:], r=["ysb"])
+
+    for s in ("v", "s", "t", "gp"):
+        g.sync.wait_ge(T.sem[s], count[s])
+    for k in range(tally["dma"]):
+        g.sync.wait_ge(T.sem["d%d" % k], 16)
+    for k in range(8):
+        g.sync.wait_ge(T.sem["rx%d" % k], engines_between(partner(k // 4), core))
+    g.sync.wait_ge(T.sem["ls"], tally["ls"])

@@ -1,10 +1,12 @@
-from concourse.mybir import dt, AluOpType as A, AxisListType, ActivationFunctionType as F
+from concourse.mybir import dt, AluOpType as A, ActivationFunctionType as F
 
 NC = 320
 NG = 8
 NM = 20
-TILE = ((0, 128), (128, 128), (256, 192), (448, 320), (768, 320))
-BY_VECTOR, BY_SCALAR = (4, 1, 0), (2, 3)
+TILE = ((0, 320), (320, 320), (640, 192), (832, 128), (960, 128))
+MT = 1088
+BY_SCALAR = (16, 15, 14, 13)
+BY_VECTOR = tuple(m for m in range(NM - 1, 0, -1) if m not in BY_SCALAR)
 PIECE = (0, 128, 192)
 
 F32, BF, I32, U16, FP8, U8 = "float32", "bfloat16", "int32", "uint16", "float8_e4m3fn_x4", "uint8"
@@ -20,32 +22,33 @@ def _mx(name, cols):
     _sb(name + "s", cols, U8)
 
 
-for _n, _c in (("tab0", NC), ("tier", NC), ("iot", NC), ("hcol", 1), ("pif", 1), ("trib", NC), ("ramp", NM),
+for _n, _c in (("tab0", NC), ("tier", NC), ("iot", NC), ("hcol", 1), ("pif", 1), ("ramp", NM),
                ("mask8", 8), ("mask8n", 8), ("h8", 8), ("tiec", 4), ("triv", 128), ("lf", 48),
-               ("a0", 4), ("d0", 4), ("dg", 2 * NC), ("sc", 2 * NC), ("sx", 2 * NC), ("sg", 2 * NC), ("row", 2 * NC), ("cs", 2 * NC),
-               ("accA", NM), ("accB", NM), ("owA", NM), ("owB", NM), ("plA", NM), ("plB", NM),
-               ("bx", NC), ("cx", NC), ("ir", NC), ("di", NC), ("si", NC),
-               ("xn", 24), ("kr0", NC), ("kr1", NC), ("pk", 4), ("cnt", 4), ("ogd", 48), ("os1", 48),
+               ("a0", 4), ("d0", 4), ("r1", 384), ("dg", 2 * NC), ("sc", 2 * NC), ("cs", NC),
+               ("accA", NM), ("accB", NM), ("owA", NM), ("owB", NM), ("plA", NM),
+               ("bx", NC), ("bt", NC), ("cx", NC), ("ir", NC), ("di", NC), ("si", NC),
+               ("xn", 84), ("kr0", NC), ("kr1", NC), ("pk", 4), ("cnt", 4), ("ogd", 48), ("os1", 48),
                ("sr", NC), ("rkd", NC), ("rks", NC), ("cc", 4 * NC), ("ysb", NC), ("tsb", NC), ("cw", NG * NC)):
     _sb(_n, _c, F32)
-for _n, _c in (("ipr", NC), ("diag", NC), ("rst", NC), ("bdi", 512), ("gob", 512), ("go", 512), ("xt0", 4 * NC), ("xt1", 4 * NC),
-               ("ut", 512), ("vt", 512), ("ones", 512), ("ident", 128), ("et", 2048), ("wg", 4096), ("bd", 512), ("bg", 960), ("tri128", 128),
-               ("a0c", 3 * 448), ("eqb", 128), ("eq", 2 * NC), ("ee", 2 * NC), ("gt", 2 * NC), ("gg", 2 * NC), ("mtA", 4352), ("mtB", 4352),
-               ("junk", 4 * 448), ("cb", 328), ("ct", 4 * NC), ("nt", 512), ("zt", 4 * NC), ("yt", 4 * NC),
+for _n, _c in (("ipr", NC), ("diag", NC), ("rst", NC), ("dpos", NC), ("rstn", NC), ("go", 512), ("go0", 512), ("xt0", 4 * NC), ("xt1", 4 * NC),
+               ("ut", 512), ("vt", 512), ("ones", 512), ("ident", 128), ("eb", 516), ("wg", 4096), ("bd", 512), ("bg", 960), ("tri", 128),
+               ("tpos", 128), ("a0c", 3 * 448), ("dd", 2 * NC), ("mtA", 4 * MT), ("mtB", 4 * MT),
+               ("junk", 4 * 448), ("cb", NC), ("cbs", NC), ("ct", 4 * NC), ("nt", 512), ("zt", 4 * NC), ("yt", 4 * NC),
                ("fp", 4 * NC), ("fs", 4 * NC), ("yp", 4 * NC)):
     _sb(_n, _c, BF)
 _sb("pi_i", 4, I32)
-for _n, _c in (("l15", NM), ("lm", NM), ("lu", 24), ("aoff", NM), ("inva", NM), ("off", NM), ("offo", 4), ("noff", NM), ("koff", NM)):
+for _n, _c in (("lm", NM), ("lu", 24), ("aoff", NM), ("inva", NM), ("off", NM), ("offo", 4), ("noff", NM), ("koff", NM)):
     _sb(_n, _c, U16)
-KE, KW, KB, KG, KO = 0, 512, 1536, 1664, 1904
+KE, KW, KB, KG, KO, KF = 0, 512, 1536, 1664, 1904, 2032
 for _n, _c in (("xq0", NC), ("xq1", NC), ("xq2", NC), ("px0", NC), ("px1", NC), ("py0", NC), ("py1", NC), ("uq", 128), ("up", 384), ("vq", 128),
-               ("kq", 2032), ("mq", 2176), ("nq", 128), ("cq", NC), ("zq", NC), ("yq0", NC), ("yq1", NC), ("ww", 1024)):
+               ("kq", 2160), ("mq", 2 * MT), ("nq", 128), ("cq", NC), ("zq", NC), ("yq0", NC), ("yq1", NC), ("ww", 1024)):
     _mx(_n, _c)
 
 SEMAPHORES = ["v", "s", "t", "gp", "ls"] + ["d%d" % k for k in range(16)] + ["rx%d" % k for k in range(8)]
 
 MG16 = 1.5 * 2.0 ** 27
 MG32 = 1.5 * 2.0 ** 28
+FAR = 1e29
 
 
 def rank_program(g, core, T, topo):
@@ -152,21 +155,23 @@ def rank_program(g, core, T, topo):
         o = NC if n == "B" else 0
         return T[name][:, o + a:o + b:step]
 
-    def lasts(name, n):
-        return half(name, n, 15, NC, 16)
-
     def junk(n):
         k = tally["junk"] % 4
         tally["junk"] += 1
         return T.junk[:, 448 * k:448 * k + n], "junk%d" % k
 
-    def quant(name, a, b, tile, ta, r):
-        do("v", lambda: V.quantize_mx(T[name + "c"][:, a:b], T[name + "s"][:, a:b], T[tile][:, ta:ta + 4 * (b - a)]), r=r, p=[name])
+    def quant(name, a, b, tile, ta, r, key=None):
+        kw = {"w": [key]} if key else {"p": [name]}
+        do("v", lambda: V.quantize_mx(T[name + "c"][:, a:b], T[name + "s"][:, a:b], T[tile][:, ta:ta + 4 * (b - a)]), r=r, **kw)
 
-    def mm(k, n, left, la, right, ra, start=True, stop=True, key=None):
+    def constants(a, n, tile, ta, r):
+        quant("kq", a, a + n, tile, ta, r, "kq%d" % a)
+
+    def mm(k, n, left, la, right, ra, start=True, stop=True, key=None, lkey=None):
         kw = {"w": [ps(k)]} if start else {"p": [ps(k)]}
+        lkey = lkey or ("kq%d" % la if left == "kq" else left)
         do("t", lambda: PE.matmul_mx(bank(k, 0, n), T[left + "c"][:, la:la + 128], T[left + "s"][:, la:la + 128],
-                                     T[right + "c"][:, ra:ra + n], T[right + "s"][:, ra:ra + n], start, stop), r=[left, key or right], **kw)
+                                     T[right + "c"][:, ra:ra + n], T[right + "s"][:, ra:ra + n], start, stop), r=[lkey, key or right], **kw)
 
     def ts(out, in0, s1, s2, op0, op1=None, **k):
         if op1 is None:
@@ -183,6 +188,9 @@ def rank_program(g, core, T, topo):
     def scopy(out, in_, scale=1.0, **k):
         do("s", lambda: S.activation(out, in_, F.Copy, scale=scale), **k)
 
+    def sline(out, in_, scale, bias, **k):
+        do("s", lambda: S.activation(out, in_, F.Identity, bias=bias, scale=scale), **k)
+
     def ssum(in_, n, col, key, r):
         j, jk = junk(n)
         do("s", lambda: S.activation(j, in_, F.Copy, accum_out=col), r=r, w=[jk], p=[key])
@@ -193,176 +201,186 @@ def rank_program(g, core, T, topo):
     def fill(ap, c, key):
         do("v", lambda: V.memset(ap, c), w=[key])
 
-    def iota(name, a, b, pattern, base, cm):
+    def iota(name, a, b, pattern, base, cm, key=None):
         ap = T[name][:, a:b]
         if name == "pi_i":
-            do("gp", lambda: g.iota(ap, pattern, base, cm), p=[name])
+            do("gp", lambda: g.iota(ap, pattern, base, cm), w=[name])
         else:
-            do("gp", lambda: g.iota(ap, pattern, base, cm, allow_small_or_imprecise_dtypes=True), p=[name])
+            do("gp", lambda: g.iota(ap, pattern, base, cm, allow_small_or_imprecise_dtypes=True), w=[key or name])
 
-    dma("sy", T.xt0[:, :], T.x[:, :], p=["xt0"])
-    dma("s", T.ut[:, :], T.u[:, :], w=["ut"])
-    dma("sy", codes("ww", 0, 1024), T.wc[:, :], p=["ww"])
-    dma("sy", T.wws[:, :], T.ws[:, :], p=["ww"])
-    dma("sy", T.vt[:, :], T.v[:, :], w=["vt"])
-
-    iota("lf", 0, 8, [[16, 8]], 0, 0)
-    iota("lf", 8, 16, [[16, 8]], 1, 0)
-    iota("lf", 16, 24, [[0, 8]], 0, 0)
-    iota("triv", 0, 128, [[1, 128]], 0, -1)
-    iota("pi_i", 0, 1, [[0, 1]], 0, 1)
-    iota("h8", 0, 8, [[1, 8]], 0, 0)
-    iota("tiec", 0, 2, [[-128, 2]], 511, -1)
-    iota("tiec", 2, 3, [[0, 1]], 511 - PIECE[2], -1)
-    fill(T.ones[:], 1.0, "ones")
-    fill(T.et[:], 0.0, "et")
-    fill(T.nt[:], 0.0, "ntz")
-    vcopy(T.lu[:], T.lf[:, 0:24], r=["lf"], w=["lu"])
-    ts(T.tri128[:], T.triv[:], 0.0, None, A.is_lt, r=["triv"], w=["tri128"])
-    ts(T.ident[:], T.triv[:], 0.0, None, A.is_equal, r=["triv"], w=["ident"])
-    fill(T.cb[:, NC:328], -40.0, "cbz")
-    fill(T.bg[:], 0.0, "bg")
-    for n in "BA":
-        fill(T["acc" + n][:, 0:1], 0.0, "acc0" + n)
+    def unfilled(n):
         for u, (o, w) in enumerate(TILE):
-            a, b = 4 * o + 256 * u, 4 * (o + w)
+            a, b = 4 * o + 64 * (17 - 4 * u), 4 * (o + w)
             scopy(T["mt" + n][:, a:b], T.ones[:, 0:b - a], 0.0, r=["ones"], w=["mz%s%d" % (n, u)])
 
-    quant("xq0", 0, NC, "xt0", 0, ["xt0"])
-    quant("uq", 0, 128, "ut", 0, ["ut"])
-    do("v", lambda: V.tensor_copy(T.upc[:, 0:384].bitcast(dt.uint32), T.uqc[:, 0:128].bitcast(dt.uint32).indirect(T.lu[:, 0:24])), r=["uq", "lu"], p=["up"])
-    do("s", lambda: S.activation(T.ups[:, 0:384], T.uqs[:, 0:128].indirect(T.lu[:, 0:24]), F.Copy), r=["uq", "lu"], p=["up"])
-    send_tile(0, 0, "px0", "xq0")
+    def row_to_all(h):
+        scopy(T.wg[:, 512 * h:512 * h + 512], T.ones[:], T.mask8[:, h:h + 1], r=["ones", "mask8"], w=["wg%d" % h])
 
-    def early_constants():
+    def quantise_row_to_all(h):
+        constants(KW + 128 * h, 128, "wg", 512 * h, ["wg%d" % h])
+
+    def quantise_unpacking(b):
+        constants(KE + 128 * b, 128, "eb", 3 - b, ["eb", "ebz"])
+
+    def while_x_comes():
+        iota("lf", 0, 16, [[1, 2], [16, 8]], 0, 0, "lf0")
+        iota("pi_i", 0, 1, [[0, 1]], 0, 1)
+        iota("h8", 0, 8, [[1, 8]], 0, 0)
+        iota("triv", 0, 128, [[1, 128]], 0, -1)
         iota("ipr", 0, NC, [[0, NM], [1, 16]], 0, 0)
-        iota("bdi", 0, 512, [[0, 8], [1, 16], [0, 4]], 0, 0)
-        iota("lf", 24, 44, [[16, NM]], 15, 0)
-        iota("gob", 0, 512, [[1, 8], [0, 64]], 0, 0)
-        iota("tier", 0, NC, [[-1, NC]], 511, 0)
-        iota("tab0", 0, NC, [[-1, NC]], 319, 0)
+        iota("lf", 24, 44, [[16, NM]], 15, 0, "lf1")
+        iota("tiec", 0, 2, [[-128, 2]], 511, -1, "tiec0")
+        iota("tiec", 2, 3, [[0, 1]], 511 - PIECE[2], -1, "tiec1")
         iota("iot", 0, NC, [[1, NC]], 0, 0)
+        fill(T.ones[:], 1.0, "ones")
+        fill(T.bd[:], 0.0, "bdz")
         ts(T.pi_i[:, 1:2], T.pi_i[:, 0:1], 15, None, A.bitwise_and, r=["pi_i"], w=["pi1"])
         ts(T.pi_i[:, 2:3], T.pi_i[:, 0:1], 4, None, A.arith_shift_right, r=["pi_i"], w=["pi2"])
-        ts(T.tiec[:, 0:3], T.tiec[:, 0:3], 1.0 / 512, 1.0 / 1024, A.mult, A.add, w=["tiec"])
+        fill(T.nt[:], 0.0, "ntz")
         vcopy(T.hcol[:], T.pi_i[:, 2:3], r=["pi2"], w=["hcol"])
         vcopy(T.pif[:], T.pi_i[:, 1:2], r=["pi1"], w=["pif"])
+        vcopy(T.lu[:, 0:16], T.lf[:, 0:16], r=["lf0"], p=["lu"])
+        do("v", lambda: V.memset(T.lu[:, 16:24], 0), p=["lu"])
         ts(T.mask8[:], T.h8[:], T.hcol[:, 0:1], None, A.is_equal, r=["h8", "hcol"], w=["mask8"])
         ts(T.mask8n[:], T.h8[:], T.hcol[:, 0:1], -0.5, A.is_equal, A.mult, r=["h8", "hcol"], w=["mask8n"])
-        for b in range(4):
-            scopy(T.et[:, 512 * b + b:512 * (b + 1):4], T.ident[:], r=["ident", "et"], w=["et%d" % b])
-
-    def middle_constants():
-        for h in range(NG):
-            scopy(T.wg[:, 512 * h:512 * h + 512], T.ones[:], T.mask8[:, h:h + 1], r=["ones", "mask8"], p=["wg%d" % (h // 4)])
-        scopy(T.tier[:], T.tier[:], 1.0 / 512, w=["tier"])
+        ts(T.tri[:], T.triv[:], 0.0, None, A.is_lt, r=["triv"], w=["tri"])
+        ts(T.ident[:], T.triv[:], 0.0, None, A.is_equal, r=["triv"], w=["ident"])
+        fill(T.bg[:], 0.0, "bgz")
+        fill(T.go0[:], 0.0, "go0z")
         ts(T.diag[:], T.ipr[:], T.pif[:, 0:1], None, A.is_equal, r=["ipr", "pif"], w=["diag"])
         ts(T.rst[:], T.ipr[:], 0.0, None, A.is_gt, r=["ipr"], w=["rst"])
-        ts(T.bd[:], T.bdi[:], T.pif[:, 0:1], None, A.is_equal, r=["bdi", "pif"], w=["bd"])
-        vcopy(T.l15[:], T.lf[:, 24:44], r=["lf"], w=["l15"])
-        quant("kq", KB, KB + 128, "bd", 0, ["bd"])
-        vcopy(T.bg[:, 448:512], T.bd[:, 0:64], r=["bd"], w=["bg"])
-        ts(T.go[:], T.gob[:], T.hcol[:, 0:1], None, A.is_equal, r=["gob", "hcol"], w=["go"])
-        quant("kq", KG, KG + 240, "bg", 0, ["bg"])
-        ts(T.lm[:], T.lf[:, 24:44], -15.0, 0.0625, A.add, A.mult, r=["lf"], w=["lm"])
-        ts(T.ramp[:], T.lf[:, 24:44], -15.0, None, A.add, r=["lf"], w=["ramp"])
-        quant("kq", KO, KO + 128, "go", 0, ["go"])
-        ts(T.trib[:], T.ipr[:], T.pif[:, 0:1], 1e29, A.is_ge, A.mult, r=["ipr", "pif"], w=["trib"])
+        ts(T.bd[:, 1:512:4], T.ipr[:, 0:128], T.pif[:, 0:1], None, A.is_equal, r=["ipr", "pif", "bdz"], p=["bd"])
+        ts(T.bd[:, 2:512:4], T.ipr[:, 0:128], T.pif[:, 0:1], -1.0, A.is_equal, A.mult, r=["ipr", "pif", "bdz"], p=["bd"])
+        fill(T.xn[:, 0:84:2], 0.0, "xnz")
+        fill(T.xn[:, 1:84:2], MG16, "xnm")
+        for n in "AB":
+            fill(T["acc" + n][:, 0:1], 0.0, "acc0" + n)
+        vcopy(T.bg[:, 448:512], T.bd[:, 0:64], r=["bd", "bgz"], w=["bg"])
+        constants(KB, 128, "bd", 0, ["bd"])
+        for e in range(4):
+            vcopy(T.go0[:, e:512:64], T.mask8[:], r=["mask8", "go0z"], p=["go0"])
+        constants(KG, 240, "bg", 0, ["bg"])
+        unfilled("A")
+        for h in range(NG):
+            scopy(T.go[:, 64 * h:64 * h + 64], T.ones[:, 0:64], T.mask8[:, h:h + 1], r=["ones", "mask8"], p=["go"])
+        sline(T.tpos[:], T.tri[:], 2 * FAR, -FAR, r=["tri"], w=["tpos"])
+        sline(T.dpos[:], T.diag[:], 2 * FAR, -FAR, r=["diag"], w=["dpos"])
+        sline(T.rstn[:], T.rst[:], 2 * FAR, -FAR, r=["rst"], w=["rstn"])
 
-    def own_places(X):
+    def while_own_scores_come():
+        ts(T.tiec[:, 0:3], T.tiec[:, 0:3], 1.0 / 512, 1.0 / 1024, A.mult, A.add, r=["tiec0", "tiec1"], w=["tiec"])
+        ts(T.lm[:], T.lf[:, 24:44], -15.0, 0.0625, A.add, A.mult, r=["lf1"], w=["lm"])
+        ts(T.ramp[:], T.lf[:, 24:44], T.pif[:, 0:1], None, A.subtract, r=["lf1", "pif"], w=["ramp"])
+        constants(KO, 128, "go", 0, ["go"])
+        constants(KF, 128, "go0", 0, ["go0"])
+        row_to_all(0)
+
+    def while_codes_come():
+        fill(T.ct[:, 2:4 * NC:4], 0.0, "ct2")
+        fill(T.ct[:, 3:4 * NC:4], 0.0, "ct3")
+        fill(T.eb[:], 0.0, "ebz")
+        quantise_row_to_all(0)
+        vcopy(T.eb[:, 3:515:4], T.ident[:], r=["ident", "ebz"], w=["eb"])
+        row_to_all(1)
+        unfilled("B")
+        sline(T.tab0[:], T.iot[:], -1.0, 319.0, r=["iot"], w=["tab0"])
+        sline(T.tier[:], T.iot[:], -1.0 / 512, 511.0 / 512, r=["iot"], w=["tier"])
+        row_to_all(2)
+        quantise_row_to_all(1)
+
+    def own_scores(X):
         mm(0, NC, "up", 256, X, 0)
         for c in range(3):
             mm(1 + c, 128, X, PIECE[c], "uq", 0)
+
+    def own_places():
         for c in range(3):
             o, sc, k, rr = PIECE[c], bank(1 + c, 0, 1), 448 * c, [ps(0), ps(1 + c)]
-            key = "a0c%d" % c
-            ts(T.eqb[:], bank(0, o, o + 128), sc, None, A.is_equal, r=rr, w=["eqb"])
+            key, r1 = "a0c%d" % c, T.r1[:, 128 * c:128 * c + 128]
+            tt(r1, bank(0, o, o + 128), T.tpos[:], A.min, r=[ps(0), "tpos"], w=["r1%d" % c])
             if o:
                 ts(T.a0c[:, k:k + o], bank(0, 0, o), sc, None, A.is_ge, r=rr, p=[key])
             ts(T.a0c[:, k + o:k + NC], bank(0, o, NC), sc, None, A.is_gt, r=rr, p=[key])
-            tt(T.a0c[:, k + NC:k + NC + 128], T.eqb[:], T.tri128[:], A.mult, r=["eqb", "tri128"], p=[key])
+            ts(T.a0c[:, k + NC:k + NC + 128], r1, sc, None, A.is_equal, r=["r1%d" % c, ps(1 + c)], p=[key])
             ssum(T.a0c[:, k:k + 448], 448, T.a0[:, c:c + 1], "a0", [key])
 
     def block_of(c):
         return (8 * c, 8 * c + 8, 0, 8) if c < 2 else (16, 20, 4, 8)
 
-    def digits_high():
-        ts(T.nt[:, 0:4 * NM:4], T.xn[:, 0:NM], MG16, MG16, A.add, A.subtract, r=["xn", "ntz"], w=["nthi"])
+    def slots(a, b):
+        return T.xn[:, 2 + 4 * a:2 + 4 * b:4]
 
-    def digits_low_and_spread(h):
-        tt(T.nt[:, 1:4 * NM:4], T.xn[:, 0:NM], T.nt[:, 0:4 * NM:4], A.subtract, r=["xn", "nthi", "ntz"], w=["ntlo"])
-        do("v", lambda: V.quantize_mx(T.nqc[:, 0:128], T.nqs[:, 0:128], T.nt[:, 0:512]), r=["nthi", "ntlo", "ntz"], w=["nq"])
-        mm(6, 128, "kq", KB, "nq", 0)
-        mm(7, 128, "kq", KG + 112 - 16 * h, "nq", 0, h == 0, h == NG - 1)
+    def digits():
+        do("v", lambda: V.tensor_tensor_scan(T.nt[:, 0:4 * NM], T.xn[:, 2:2 + 4 * NM], T.xn[:, 0:4 * NM], 0.0, A.add, A.subtract),
+           r=["xn", "xnz", "xnm", "ntz"], w=["nt"])
+
+    def spread(h, every=True):
+        quant("nq", 0, 128, "nt", 0, ["nt", "ntz"], "nq")
+        if every:
+            mm(6, 128, "kq", KB, "nq", 0)
+        mm(7, 128, "kq", KG + 112 - 16 * h, "nq", 0, h == 0, h == NG - 1, lkey="kq%d" % KG)
 
     def take_offsets():
         ts(T.off[:], bank(6, 0, NM), 160.0, None, A.add, r=[ps(6)], w=["off"])
 
-    def score_columns(n, k):
-        tt(half("dg", n), bank(k), T.diag[:], A.mult, r=[ps(k), "diag"], w=["dg" + n])
-        scopy(half("row", n), bank(k), r=[ps(k)], w=["row" + n])
-        scan(half("sc", n), half("dg", n), r=["rst", "dg" + n], w=["sc" + n])
+    VB, SB, CB = {"A": 4, "B": 5}, {"A": 0, "B": 1}, {"A": 2, "B": 3}
 
-    def blocks(u):
-        return range(max(1, 4 * u), 4 * u + 4)
+    def own_column(n):
+        tt(half("dg", n), bank(VB[n]), T.dpos[:], A.min, r=[ps(VB[n]), "dpos"], w=["dg" + n])
+
+    def carry(n):
+        do("v", lambda: V.tensor_tensor_scan(half("sc", n), T.rstn[:], half("dg", n), 0.0, A.min, A.max), r=["rstn", "dg" + n], w=["sc" + n])
 
     def part(n, m):
-        o, e = 4 * TILE[m // 4][0], m % 4
+        o, e = 4 * TILE[(NM - m) // 4][0], (NM - m) % 4
         return T["mt" + n][:, o + e:o + 64 * m:4]
+
+    def zeros(n, m):
+        return "mz%s%d" % (n, (NM - m) // 4)
 
     def score(n, m):
         return half("sc", n, 16 * m + 15, 16 * m + 16)
 
-    def compare(n, k):
-        for u in BY_VECTOR:
-            for m in blocks(u):
-                ts(part(n, m), bank(k, 0, 16 * m), score(n, m), None, A.is_lt, r=[ps(k), "sc" + n, "mz%s%d" % (n, u)], w=["mt%s%d" % (n, m)])
+    def inside(n):
+        tt(part(n, NM), bank(VB[n]), half("sc", n), A.is_le, r=[ps(VB[n]), "sc" + n, zeros(n, NM)], w=["mt%s%d" % (n, NM)])
+
+    def inside_sums(n):
+        scan(half("dd", n), part(n, NM), r=["rst", "mt%s%d" % (n, NM)], w=["dd" + n])
+
+    def compare(n, ms):
+        for m in ms:
+            ts(part(n, m), bank(VB[n], 0, 16 * m), score(n, m), None, A.is_lt, r=[ps(VB[n]), "sc" + n, zeros(n, m)], w=["mt%s%d" % (n, m)])
 
     def scalar_compare(n):
         late = None
-        for m in [m for u in BY_SCALAR for m in blocks(u)] + [None]:
+        for m in BY_SCALAR + (None,):
             if m is not None:
                 j, jk = junk(16 * m)
-                do("s", lambda: S.activation(j, half("row", n, 0, 16 * m), F.Sign, bias=score(n, m), scale=-1.0), r=["row" + n, "sc" + n], w=[jk])
+                do("s", lambda: S.activation(j, bank(SB[n], 0, 16 * m), F.Sign, bias=score(n, m), scale=-1.0), r=[ps(SB[n]), "sc" + n], w=[jk])
             if late:
                 q, i, ik = late
                 do("s", lambda: S.activation(part(n, q), i, F.Relu, accum_out=T["acc" + n][:, q:q + 1]),
-                   r=[ik, "mz%s%d" % (n, q // 4)], w=["mt%s%d" % (n, q)], p=["acc" + n])
+                   r=[ik, zeros(n, q)], w=["mt%s%d" % (n, q)], p=["acc" + n])
             late = (m, j, jk)
 
     def add_up(n):
-        for u in BY_VECTOR:
-            for m in blocks(u):
-                ssum(part(n, m), 16 * m, T["acc" + n][:, m:m + 1], "acc" + n, ["mt%s%d" % (n, m)])
+        for m in BY_VECTOR:
+            ssum(part(n, m), 16 * m, T["acc" + n][:, m:m + 1], "acc" + n, ["mt%s%d" % (n, m)])
 
-    def tile_sums(n, us, to):
+    def column_sums(n, us):
+        o, c, key = TILE[us[0]][0], TILE[us[0]][0] + (MT if n == "B" else 0), "mq%s%d" % (n, us[0])
+        w = sum(TILE[u][1] for u in us)
+        r = ["mz%s%d" % (n, u) for u in us] + ["mt%s%d" % (n, NM - 4 * u - e) for u in us for e in range(4)]
+        quant("mq", c, c + w, "mt" + n, 4 * o, r, key)
         for u in us:
-            (o, w), key = TILE[u], "mq%s%d" % (n, u)
-            c = o + (1088 if n == "B" else 0)
-            do("v", lambda: V.quantize_mx(T.mqc[:, c:c + w], T.mqs[:, c:c + w], T["mt" + n][:, 4 * o:4 * (o + w)]),
-               r=["mz%s%d" % (n, u)] + ["mt%s%d" % (n, m) for m in blocks(u)], w=[key])
-            mm(to, w, "kq", KO, "mq", c, u == BY_VECTOR[0], u == BY_SCALAR[-1], key)
+            mm(CB[n], TILE[u][1], "kq", KO if n == "A" else KF, "mq", c + TILE[u][0] - o, u == 0, u == 1, key)
 
-    def spread_scores(n):
-        scopy(half("sg", n), half("sc", n).indirect(T.l15[:, 0:NM]), r=["sc" + n, "l15"], w=["sg" + n])
-
-    def equals_in_block(n, k):
-        tt(half("sx", n), half("sc", n).indirect(T.l15[:, 0:NM]), T.trib[:], A.add, r=["sc" + n, "l15", "trib"], w=["sx" + n])
-        tt(half("eq", n), bank(k), half("sx", n), A.is_equal, r=[ps(k), "sx" + n], w=["eq" + n])
-        scan(half("ee", n), half("eq", n), r=["rst", "eq" + n], w=["ee" + n])
-
-    def larger_in_block(n, k):
-        tt(half("gt", n), bank(k), half("sg", n), A.is_gt, r=[ps(k), "sg" + n], w=["gt" + n])
-        tt(T["ow" + n][:], T.ramp[:], lasts("ee", n), A.add, r=["ramp", "ee" + n], w=["ow" + n])
-        scan(half("gg", n), half("gt", n), r=["rst", "gt" + n], w=["gg" + n])
-
-    def place(n, to):
+    def row_part(n, k):
         ow = T["ow" + n]
-        tt(T.rkd[:], bank(to), T.diag[:], A.mult, r=[ps(to), "diag"], w=["rkd"])
-        tt(ow[:], ow[:], lasts("gg", n), A.add, r=["gg" + n], w=["ow" + n])
-        scan(half("cs", n), T.rkd[:], r=["rst", "rkd"], w=["cs" + n])
-        tt(ow[:], ow[:], T["acc" + n][:], A.subtract, r=["acc" + n, "acc0" + n], w=["ow" + n])
-        tt(T["pl" + n][:], ow[:], lasts("cs", n), A.add, r=["ow" + n, "cs" + n], w=["pl" + n])
+        if k == 0:
+            tt(ow[:], T.ramp[:], half("dd", n, 15, NC, 16), A.subtract, r=["ramp", "dd" + n], w=["ow" + n])
+        else:
+            tt(ow[:], ow[:], T["acc" + n][:], A.subtract, r=["acc" + n, "acc0" + n], w=["ow" + n])
 
     def table(h):
         mm(h % 4, NC, "kq", KW + 128 * h, "cq", 0)
@@ -384,110 +402,144 @@ def rank_program(g, core, T, topo):
         do("s", lambda: S.activation(j, T[prev][:], F.Sign, bias=T.pk[:, c:c + 1], scale=-1.0, accum_out=T.cnt[:, c:c + 1]),
            r=[prev, "pk"], w=["cnt%d" % c, jk])
 
-    def draft_round(t):
-        X, PX, PY, YQ = "xq%d" % t, "px%d" % t, "py%d" % t, "yq%d" % t
-        last = t == 1
-        if t == 0:
-            early_constants()
-        own_places(X)
-        if t == 0:
-            middle_constants()
+    def own_totals(h):
+        tt(T.ogd[:], plane("cw", h).indirect(T.offo[:, 0:3]), T.diag[:, 0:48], A.mult, r=["cw%d" % h, "offo", "offo2", "diag"], w=["ogd"])
+
+    def own_totals_picked():
+        scan(T.os1[:], T.ogd[:], 48, r=["rst", "ogd"], w=["os1"])
+
+    def own_totals_added(old):
+        tt(T.pk[:, 0:3], T[old][:, 0:3], T.os1[:, 15:48:16], A.add, r=["os1", old], w=["pk"])
+
+    def unpack(b, PX):
+        mm(4 + b % 2, NC, "kq", KE + 128 * b, PX, 0)
+
+    def places(t, PX):
+        for n, a in (("A", 0), ("B", 128)):
+            mm(VB[n], NC, "up", a, PX, 0)
+        for n, a in (("A", 0), ("B", 128)):
+            mm(SB[n], NC, "up", a, PX, 0)
+        own_column("A")
         ts(T.d0[:, 0:3], T.a0[:, 0:3], -1.0, 159.0, A.mult, A.add, r=["a0"], w=["d0"])
+        own_column("B")
+        carry("A")
         for c in range(3):
             a, b, ma, mb = block_of(c)
-            ts(T.xn[:, a:b], T.mask8[:, ma:mb], T.d0[:, c:c + 1], None, A.mult, r=["mask8", "d0"], p=["xn"])
-        digits_high()
+            ts(slots(a, b), T.mask8[:, ma:mb], T.d0[:, c:c + 1], None, A.mult, r=["mask8", "d0", "xnz"], p=["xn"])
+        carry("B")
+        digits()
+        inside("A")
+        spread(0)
         ts(T.offo[:, 0:3], T.d0[:, 0:3], 160.0, None, A.add, r=["d0"], w=["offo"])
-        digits_low_and_spread(0)
-        if t == 0:
-            quant("kq", KE, KE + 512, "et", 0, ["et", "et0", "et1", "et2", "et3"])
-            fill(T.ct[:], 0.0, "ct")
-        mm(5, NC, "up", 128, PX, 0)
-        mm(4, NC, "up", 0, PX, 0)
-        take_offsets()
-        score_columns("B", 5)
-        score_columns("A", 4)
-        compare("B", 5)
-        scalar_compare("B")
-        tile_sums("B", BY_VECTOR, 3)
-        spread_scores("B")
-        add_up("B")
-        equals_in_block("B", 5)
-        compare("A", 4)
         scalar_compare("A")
-        spread_scores("A")
+        compare("A", BY_VECTOR)
         add_up("A")
-        tile_sums("A", BY_VECTOR, 6)
-        tile_sums("B", BY_SCALAR, 3)
-        larger_in_block("B", 5)
-        equals_in_block("A", 4)
-        place("B", 3)
-        if t == 0:
-            quant("kq", KW, KW + 512, "wg", 0, ["wg0"])
-            quant("kq", KW + 512, KW + 1024, "wg", 2048, ["wg1"])
-        tile_sums("A", BY_SCALAR, 6)
-        for b in range(4):
-            k = (0, 1, 2, 0)[b]
-            mm(k, NC, "kq", KE + 128 * b, PX, 0)
-            scopy(plane("fp", b), bank(k), r=[ps(k)], w=["fp%d" % b])
-        larger_in_block("A", 4)
-        tt(T.bx[:], T.plB[:, 0:NM].indirect(T.lm[:, 0:NM]), T.diag[:], A.mult, r=["plB", "lm", "diag"], w=["bx"])
-        place("A", 6)
+        take_offsets()
+        inside("B")
+        scalar_compare("B")
+        compare("B", BY_VECTOR)
+        add_up("B")
+        column_sums("A", (0,))
+        column_sums("A", (2, 3, 4))
+        column_sums("A", (1,))
+        inside_sums("A")
+        inside_sums("B")
+        row_part("A", 0)
+        tt(T.rkd[:], bank(CB["A"]), T.diag[:], A.mult, r=[ps(CB["A"]), "diag"], w=["rkd"])
+        column_sums("B", (0,))
+        scan(T.cs[:], T.rkd[:], r=["rst", "rkd"], w=["cs"])
+        row_part("A", 1)
+        row_part("B", 0)
+        column_sums("B", (2, 3, 4))
+        tt(T.plA[:], T.owA[:], T.cs[:, 15:NC:16], A.add, r=["owA", "cs"], w=["plA"])
+        column_sums("B", (1,))
         vcopy(T.aoff[:], T.plA[:], r=["plA"], w=["aoff"])
-        vcopy(T.cx[:, 0:NC].indirect(T.aoff[:, 0:NM]), T.bx[:], r=["aoff", "bx"], w=["cx"])
-        ts(T.ct[:, 0:4 * NC:4], T.cx[:], MG32, MG32, A.add, A.subtract, r=["cx", "ct"], w=["cthi"])
-        tt(T.ct[:, 1:4 * NC:4], T.cx[:], T.ct[:, 0:4 * NC:4], A.subtract, r=["cx", "cthi", "ct"], w=["ctlo"])
-        quant("cq", 0, NC, "ct", 0, ["cthi", "ctlo", "ct"])
-        for h in range(4):
+        steps = [
+            lambda: row_part("B", 1),
+            lambda: tt(T.bx[:], T.owB[:, 0:NM].indirect(T.lm[:, 0:NM]), T.diag[:], A.mult, r=["owB", "lm", "diag"], w=["bx"]),
+            lambda: tt(T.bt[:], bank(CB["B"]), T.bx[:], A.add, r=[ps(CB["B"]), "bx"], w=["bt"]),
+            lambda: vcopy(T.cx[:, 0:NC].indirect(T.aoff[:, 0:NM]), T.bt[:], r=["aoff", "bt"], w=["cx"])]
+        for b in range(4):
+            steps[b]()
+            if t == 0:
+                quantise_unpacking(b)
+        H = NC // 2
+        for a in (0, H):
+            ts(T.ct[:, 4 * a:4 * (a + H):4], T.cx[:, a:a + H], MG32, MG32, A.add, A.subtract, r=["cx"], w=["cthi%d" % a])
+        for a in (0, H):
+            tt(T.ct[:, 4 * a + 1:4 * (a + H):4], T.cx[:, a:a + H], T.ct[:, 4 * a:4 * (a + H):4], A.subtract, r=["cx", "cthi%d" % a], w=["ctlo%d" % a])
+        for a in (0, H):
+            quant("cq", a, a + H, "ct", 4 * a, ["cthi%d" % a, "ctlo%d" % a, "ct2", "ct3"])
+
+    def draft(t, PX):
+        last = t == 1
+        for h in range(2):
             table(h)
-        vcopy(T.pk[:, 0:3], T.tiec[:, 0:3], r=["tiec"], w=["pk"])
-        copy_table(0)
-        copy_table(1)
-        prev = "tier"
-        for h in range(NG):
+            copy_table(h)
+        own_totals(0)
+        prev = look_up(0, "tier")
+        own_totals_picked()
+        if t == 0:
+            quantise_row_to_all(2)
+        own_totals_added("tiec")
+        for h in range(1, NG):
             own = h < NG - 1
-            if h:
-                ns = 3 if h < 3 else 2
-                for c in range(ns):
-                    count_teams(prev, c)
-                for c in range(ns):
-                    a, b, ma, mb = block_of(c)
-                    scopy(T.xn[:, a:b], T.mask8n[:, ma:mb], T.cnt[:, c:c + 1], r=["mask8n", "cnt%d" % c], p=["xn"])
-                if h == 1:
-                    vcopy(T.ir[:, 0:NC].indirect(T.aoff[:, 0:NM]), T.iot[:], r=["aoff", "iot"], w=["ir"])
-                elif h == 2:
-                    tt(T.di[:], T.ir[:], T.diag[:], A.mult, r=["ir", "diag"], w=["di"])
-                    scan(T.si[:], T.di[:], r=["rst", "di"], w=["si"])
-                    vcopy(T.inva[:], T.si[:, 15:NC:16], r=["si"], w=["inva"])
-                else:
-                    ts(T.cb[:, 0:NC], T[prev][:], T.pk[:, 2:3], 2.0, A.is_lt, A.mult, r=[prev, "pk"], w=["cb"])
-                    do("v", lambda: V.tensor_reduce(T.cnt[:, 2:3], T.cb[:], AxisListType.X, A.add), r=["cb", "cbz"], w=["cnt2"])
-                    a, b, ma, mb = block_of(2)
-                    ts(T.xn[:, a:b], T.mask8n[:, ma:mb], T.cnt[:, 2:3], None, A.mult, r=["mask8n", "cnt2"], p=["xn"])
-                digits_high()
-                if own:
-                    ts(T.offo[:, 0:3], T.cnt[:, 0:3], -0.5, 160.0, A.mult, A.add, r=["cnt0", "cnt1", "cnt2"], w=["offo"])
-                digits_low_and_spread(h)
             if own:
-                tt(T.ogd[:], plane("cw", h).indirect(T.offo[:, 0:3]), T.diag[:, 0:48], A.mult, r=["cw%d" % h, "offo", "diag"], w=["ogd"])
-                scan(T.os1[:], T.ogd[:], 48, r=["rst", "ogd"], w=["os1"])
-                if h:
-                    take_offsets()
-                tt(T.pk[:, 0:3], T.pk[:, 0:3], T.os1[:, 15:48:16], A.add, r=["os1"], w=["pk"])
+                table(h + 1)
+            if h < 3:
+                unpack(2 * h - 2, PX)
+                unpack(2 * h - 1, PX)
+            ns = 3 if h < 3 else 2
+            for c in range(ns):
+                count_teams(prev, c)
+            for c in range(ns):
+                a, b, ma, mb = block_of(c)
+                scopy(slots(a, b), T.mask8n[:, ma:mb], T.cnt[:, c:c + 1], r=["mask8n", "cnt%d" % c], p=["xn"])
+            if h == 1:
+                vcopy(T.ir[:, 0:NC].indirect(T.aoff[:, 0:NM]), T.iot[:], r=["aoff", "iot"], w=["ir"])
+            elif h == 2:
+                tt(T.di[:], T.ir[:], T.diag[:], A.mult, r=["ir", "diag"], w=["di"])
+                scan(T.si[:], T.di[:], r=["rst", "di"], w=["si"])
+                vcopy(T.inva[:], T.si[:, 15:NC:16], r=["si"], w=["inva"])
+            else:
+                ts(T.cb[:], T[prev][:], T.pk[:, 2:3], None, A.is_gt, r=[prev, "pk"], w=["cb"])
+                do("v", lambda: V.tensor_tensor_scan(T.cbs[:], T.ones[:, 0:NC], T.cb[:], -160.0, A.mult, A.add), r=["cb", "ones"], w=["cbs"])
+                a, b, ma, mb = block_of(2)
+                ts(slots(a, b), T.mask8[:, ma:mb], T.cbs[:, NC - 1:NC], None, A.mult, r=["mask8", "cbs"], p=["xn"])
+            digits()
+            if own:
+                ts(T.offo[:, 0:ns], T.cnt[:, 0:ns], -0.5, 160.0, A.mult, A.add, r=["cnt%d" % c for c in range(ns)], w=["offo"])
+                if ns == 2:
+                    ts(T.offo[:, 2:3], T.cbs[:, NC - 1:NC], 160.0, None, A.add, r=["cbs"], w=["offo2"])
+            spread(h, own or last)
+            if own:
+                own_totals(h)
+                own_totals_picked()
+                take_offsets()
+                own_totals_added("pk")
                 prev = look_up(h, prev)
-            if h < 4:
-                table(h + 4)
-            if 1 <= h < NG - 1:
+            if t == 0 and h + 2 < NG:
+                row_to_all(h + 2)
+                quantise_row_to_all(h + 2)
+            if own:
                 copy_table(h + 1)
-            if 3 <= h <= 6:
+            if h < 3:
+                for b in (2 * h - 2, 2 * h - 1):
+                    scopy(plane("fp", b), bank(4 + b % 2), r=[ps(4 + b % 2)], w=["fp%d" % b])
+            elif own:
                 scopy(plane("fs", h - 3), plane("fp", h - 3).indirect(T.inva[:, 0:NM]), r=["fp%d" % (h - 3), "inva"], w=["fs%d" % (h - 3)])
+        return prev
+
+    def layer(t, prev):
+        X, PY, YQ = "xq%d" % t, "py%d" % t, "yq%d" % t
+        last = t == 1
         ts(T.noff[:], bank(7, 0, NM), 160.0, None, A.add, r=[ps(7)], w=["noff"])
         if last:
             take_offsets()
-        for k in range(2):
-            vcopy(T.zt[:, k:4 * NC:4], plane("fs", k).indirect(T.noff[:, 0:NM]), r=["fs%d" % k, "noff"], p=["zt"])
-            j = 2 + k
-            scopy(T.zt[:, j:4 * NC:4], plane("fs", j).indirect(T.noff[:, 0:NM]), r=["fs%d" % j, "noff"], p=["zt"])
+        for k in range(4):
+            cp = scopy if k else vcopy
+            cp(T.zt[:, k:4 * NC:4], plane("fs", k).indirect(T.noff[:, 0:NM]), r=["fs%d" % k, "noff"], p=["zt"])
+        vcopy(T.sr[:, 0:NC].indirect(T.noff[:, 0:NM]), T.iot[:], r=["noff", "iot"], w=["sr"])
         quant("zq", 0, NC, "zt", 0, ["zt"])
         for b in range(4):
             mm(4 + b, NC, "ww", 128 * (b + 4), "zq", 0)
@@ -497,14 +549,12 @@ def rank_program(g, core, T, topo):
         def larger(b):
             tt(plane("yp", b), bank(b), plane("cc", b), A.max, r=[ps(b), "cc%d" % b], w=["yp%d" % b])
 
-        vcopy(T.sr[:, 0:NC].indirect(T.noff[:, 0:NM]), T.iot[:], r=["noff", "iot"], w=["sr"])
-        larger(0)
         tt(T.rkd[:], T.sr[:, 0:NC].indirect(T.aoff[:, 0:NM]), T.diag[:], A.mult, r=["sr", "aoff", "diag"], w=["rkd"])
-        larger(1)
         scan(T.rks[:], T.rkd[:], r=["rst", "rkd"], w=["rks"])
-        larger(2)
+        larger(0)
         vcopy(T.koff[:], T.rks[:, 15:NC:16], r=["rks"], w=["koff"])
-        larger(3)
+        for b in range(1, 4):
+            larger(b)
         for k in range(2):
             scopy(T.yt[:, k:4 * NC:4], plane("yp", k).indirect(T.koff[:, 0:NM]), 0.03125, r=["yp%d" % k, "koff"], p=["yt"])
             j = 2 + k
@@ -525,9 +575,29 @@ def rank_program(g, core, T, topo):
             cp(T.xt1[:, b:4 * NC:4], bank(b), r=[ps(b)], p=["xt1"])
         quant("xq%d" % (t + 1), 0, NC, "xt1", 0, ["xt1"])
 
-    draft_round(0)
-    send_tile(1, 4, "px1", "xq1")
-    draft_round(1)
+    dma("sy", T.xt0[:, :], T.x[:, :], p=["xt0"])
+    dma("sy", T.ut[:, :], T.u[:, :], w=["ut"])
+    while_x_comes()
+    quant("xq0", 0, NC, "xt0", 0, ["xt0"])
+    send_tile(0, 0, "px0", "xq0")
+    quant("uq", 0, 128, "ut", 0, ["ut"])
+    do("v", lambda: V.tensor_copy(T.upc[:, 0:384].bitcast(dt.uint32), T.uqc[:, 0:128].bitcast(dt.uint32).indirect(T.lu[:, 0:24])), r=["uq", "lu"], p=["up"])
+    do("s", lambda: S.activation(T.ups[:, 0:384], T.uqs[:, 0:128].indirect(T.lu[:, 0:24]), F.Copy), r=["uq", "lu"], p=["up"])
+    dma("sy", codes("ww", 0, 1024), T.wc[:, :], r=["px0"], p=["ww"])
+    dma("sy", T.wws[:, :], T.ws[:, :], p=["ww"])
+    dma("sy", T.vt[:, :], T.v[:, :], w=["vt"])
+    for t in range(2):
+        PX = "px%d" % t
+        own_scores("xq%d" % t)
+        if t == 0:
+            while_own_scores_come()
+        own_places()
+        if t == 0:
+            while_codes_come()
+        places(t, PX)
+        layer(t, draft(t, PX))
+        if t == 0:
+            send_tile(1, 4, "px1", "xq1")
 
     mm(4, NC, "vq", 0, "xq2", 0)
     dma("sy", T.oc[:, :], codes("xq2", 0, NC), r=["xq2"])

@@ -5,7 +5,7 @@ NG = 8
 NM = 20
 TILE = ((0, 320), (320, 320), (640, 192), (832, 128), (960, 128))
 MT = 1088
-BY_SCALAR = (16, 15, 14, 13)
+BY_SCALAR = (19, 18, 17)
 BY_VECTOR = tuple(m for m in range(NM - 1, 0, -1) if m not in BY_SCALAR)
 PIECE = (0, 128, 192)
 
@@ -23,7 +23,7 @@ def _mx(name, cols):
 
 
 for _n, _c in (("tab0", NC), ("tier", NC), ("iot", NC), ("hcol", 1), ("pif", 1), ("ramp", NM),
-               ("mask8", 8), ("mask8n", 8), ("h8", 8), ("tiec", 4), ("triv", 128), ("lf", 48),
+               ("mask8", 8), ("mask8n", 8), ("maskw", 8), ("h8", 8), ("tiec", 4), ("triv", 128), ("lf", 48),
                ("a0", 4), ("d0", 4), ("r1", 384), ("dg", 2 * NC), ("sc", 2 * NC), ("cs", NC),
                ("accA", NM), ("accB", NM), ("owA", NM), ("owB", NM), ("plA", NM),
                ("bx", NC), ("bt", NC), ("cx", NC), ("ir", NC), ("di", NC), ("si", NC),
@@ -31,7 +31,7 @@ for _n, _c in (("tab0", NC), ("tier", NC), ("iot", NC), ("hcol", 1), ("pif", 1),
                ("sr", NC), ("rkd", NC), ("rks", NC), ("cc", 4 * NC), ("ysb", NC), ("tsb", NC), ("cw", NG * NC)):
     _sb(_n, _c, F32)
 for _n, _c in (("ipr", NC), ("diag", NC), ("rst", NC), ("dpos", NC), ("rstn", NC), ("go", 512), ("go0", 512), ("xt0", 4 * NC), ("xt1", 4 * NC),
-               ("ut", 512), ("vt", 512), ("ones", 512), ("ident", 128), ("eb", 516), ("wg", 4096), ("bd", 512), ("bg", 960), ("tri", 128),
+               ("ut", 512), ("vt", 512), ("ones", 512), ("eb", 516), ("wg", 4096), ("bd", 512), ("bg", 960), ("tri", 128),
                ("tpos", 128), ("a0c", 3 * 448), ("dd", 2 * NC), ("mtA", 4 * MT), ("mtB", 4 * MT),
                ("junk", 4 * 448), ("cb", NC), ("cbs", NC), ("ct", 4 * NC), ("nt", 512), ("zt", 4 * NC), ("yt", 4 * NC),
                ("fp", 4 * NC), ("fs", 4 * NC), ("yp", 4 * NC)):
@@ -44,7 +44,10 @@ for _n, _c in (("xq0", NC), ("xq1", NC), ("xq2", NC), ("px0", NC), ("px1", NC), 
                ("kq", 2160), ("mq", 2 * MT), ("nq", 128), ("cq", NC), ("zq", NC), ("yq0", NC), ("yq1", NC), ("ww", 1024)):
     _mx(_n, _c)
 
-SEMAPHORES = ["v", "s", "t", "gp", "ls"] + ["d%d" % k for k in range(16)] + ["rx%d" % k for k in range(8)]
+SEMAPHORES = ["v", "s", "t", "gp", "ls"] + ["d%d" % k for k in range(16)] + ["rx%d" % k for k in range(16)]
+H = NC // 2
+HALVES = (0, H)
+SPLIT_0, SPLIT_X, SPLIT_Y = True, True, True
 
 MG16 = 1.5 * 2.0 ** 27
 MG32 = 1.5 * 2.0 ** 28
@@ -61,6 +64,7 @@ def rank_program(g, core, T, topo):
     count = {"v": 0, "s": 0, "t": 0, "gp": 0}
     state = {}
     tally = {"dma": 0, "ls": 0, "junk": 0}
+    arrivals = []
 
     def st(k):
         if k not in state:
@@ -123,18 +127,26 @@ def rank_program(g, core, T, topo):
     def engines_between(a, b):
         return len(topo.engines(a, b))
 
-    def send(dst, rx, out, in_, r):
+    def send(dst, out, in_, r):
         waits("gp", r, (), ())
         rid, pid, _ = topo.addr(dst)
-        g.remote_dma(out, in_, T.sem["rx%d" % rx], T.sem["ls"], pid, rid, topo.mask(core, dst))
+        rx = "rx%d" % len(arrivals)
+        g.remote_dma(out, in_, T.sem[rx], T.sem["ls"], pid, rid, topo.mask(core, dst))
         tally["ls"] += engines_between(core, dst)
+        arrivals.append((rx, engines_between(dst, core)))
+        return arrivals[-1] + ({},)
 
-    def send_tile(t, rx, land, name):
-        q = partner(t)
-        send(q, rx, codes(land, 0, NC), codes(name, 0, NC), [name])
-        send(q, rx + 1, T[land + "s"][:, 0:NC], T[name + "s"][:, 0:NC], [name])
-        n = engines_between(q, core)
-        st(land)["w"] = [("rx%d" % rx, n, {}), ("rx%d" % (rx + 1), n, {})]
+    def hk(name, a):
+        return "%s@%d" % (name, a)
+
+    def both(name):
+        return [hk(name, a) for a in HALVES]
+
+    def send_tile(t, land, name, halves):
+        a, b, r = halves[0], halves[-1] + H, [hk(name, a) for a in halves]
+        came = [send(partner(t), codes(land, a, b), codes(name, a, b), r), send(partner(t), T[land + "s"][:, a:b], T[name + "s"][:, a:b], r)]
+        for a in halves:
+            st(hk(land, a))["w"] = came
 
     def partner(t):
         return T.cores[rank ^ (1 << t)]
@@ -170,8 +182,9 @@ def rank_program(g, core, T, topo):
     def mm(k, n, left, la, right, ra, start=True, stop=True, key=None, lkey=None):
         kw = {"w": [ps(k)]} if start else {"p": [ps(k)]}
         lkey = lkey or ("kq%d" % la if left == "kq" else left)
+        r = [x for side in (lkey, key or right) for x in (both(side) if side[:2] in ("xq", "px", "cq") and "@" not in side else [side])]
         do("t", lambda: PE.matmul_mx(bank(k, 0, n), T[left + "c"][:, la:la + 128], T[left + "s"][:, la:la + 128],
-                                     T[right + "c"][:, ra:ra + n], T[right + "s"][:, ra:ra + n], start, stop), r=[lkey, key or right], **kw)
+                                     T[right + "c"][:, ra:ra + n], T[right + "s"][:, ra:ra + n], start, stop), r=r, **kw)
 
     def ts(out, in0, s1, s2, op0, op1=None, **k):
         if op1 is None:
@@ -208,13 +221,19 @@ def rank_program(g, core, T, topo):
         else:
             do("gp", lambda: g.iota(ap, pattern, base, cm, allow_small_or_imprecise_dtypes=True), w=[key or name])
 
+    def clear(name, a, b, key, step=1):
+        do("gp", lambda: g.iota(T[name][:, a:b:step], [[0, (b - a + step - 1) // step]], 0, 0, allow_small_or_imprecise_dtypes=True), w=[key])
+
     def unfilled(n):
         for u, (o, w) in enumerate(TILE):
             a, b = 4 * o + 64 * (17 - 4 * u), 4 * (o + w)
-            scopy(T["mt" + n][:, a:b], T.ones[:, 0:b - a], 0.0, r=["ones"], w=["mz%s%d" % (n, u)])
+            if n == "A":
+                scopy(T.mtA[:, a:b], T.ones[:, 0:b - a], 0.0, r=["ones"], w=["mzA%d" % u])
+            else:
+                clear("mtB", a, b, "mzB%d" % u)
 
     def row_to_all(h):
-        scopy(T.wg[:, 512 * h:512 * h + 512], T.ones[:], T.mask8[:, h:h + 1], r=["ones", "mask8"], w=["wg%d" % h])
+        scopy(T.wg[:, 512 * h:512 * h + 512], T.ones[:], T.maskw[:, h:h + 1], r=["ones", "maskw"], w=["wg%d" % h])
 
     def quantise_row_to_all(h):
         constants(KW + 128 * h, 128, "wg", 512 * h, ["wg%d" % h])
@@ -231,62 +250,63 @@ def rank_program(g, core, T, topo):
         iota("lf", 24, 44, [[16, NM]], 15, 0, "lf1")
         iota("tiec", 0, 2, [[-128, 2]], 511, -1, "tiec0")
         iota("tiec", 2, 3, [[0, 1]], 511 - PIECE[2], -1, "tiec1")
-        iota("iot", 0, NC, [[1, NC]], 0, 0)
         fill(T.ones[:], 1.0, "ones")
         fill(T.bd[:], 0.0, "bdz")
         ts(T.pi_i[:, 1:2], T.pi_i[:, 0:1], 15, None, A.bitwise_and, r=["pi_i"], w=["pi1"])
         ts(T.pi_i[:, 2:3], T.pi_i[:, 0:1], 4, None, A.arith_shift_right, r=["pi_i"], w=["pi2"])
-        fill(T.nt[:], 0.0, "ntz")
+        fill(T.go0[:], 0.0, "go0z")
         vcopy(T.hcol[:], T.pi_i[:, 2:3], r=["pi2"], w=["hcol"])
         vcopy(T.pif[:], T.pi_i[:, 1:2], r=["pi1"], w=["pif"])
         vcopy(T.lu[:, 0:16], T.lf[:, 0:16], r=["lf0"], p=["lu"])
         do("v", lambda: V.memset(T.lu[:, 16:24], 0), p=["lu"])
         ts(T.mask8[:], T.h8[:], T.hcol[:, 0:1], None, A.is_equal, r=["h8", "hcol"], w=["mask8"])
-        ts(T.mask8n[:], T.h8[:], T.hcol[:, 0:1], -0.5, A.is_equal, A.mult, r=["h8", "hcol"], w=["mask8n"])
+        ts(T.maskw[:], T.h8[:], T.hcol[:, 0:1], 512.0, A.is_equal, A.mult, r=["h8", "hcol"], w=["maskw"])
         ts(T.tri[:], T.triv[:], 0.0, None, A.is_lt, r=["triv"], w=["tri"])
-        ts(T.ident[:], T.triv[:], 0.0, None, A.is_equal, r=["triv"], w=["ident"])
-        fill(T.bg[:], 0.0, "bgz")
-        fill(T.go0[:], 0.0, "go0z")
+        fill(T.nt[:], 0.0, "ntz")
         ts(T.diag[:], T.ipr[:], T.pif[:, 0:1], None, A.is_equal, r=["ipr", "pif"], w=["diag"])
         ts(T.rst[:], T.ipr[:], 0.0, None, A.is_gt, r=["ipr"], w=["rst"])
-        ts(T.bd[:, 1:512:4], T.ipr[:, 0:128], T.pif[:, 0:1], None, A.is_equal, r=["ipr", "pif", "bdz"], p=["bd"])
-        ts(T.bd[:, 2:512:4], T.ipr[:, 0:128], T.pif[:, 0:1], -1.0, A.is_equal, A.mult, r=["ipr", "pif", "bdz"], p=["bd"])
-        fill(T.xn[:, 0:84:2], 0.0, "xnz")
-        fill(T.xn[:, 1:84:2], MG16, "xnm")
-        for n in "AB":
-            fill(T["acc" + n][:, 0:1], 0.0, "acc0" + n)
-        vcopy(T.bg[:, 448:512], T.bd[:, 0:64], r=["bd", "bgz"], w=["bg"])
-        constants(KB, 128, "bd", 0, ["bd"])
         for e in range(4):
             vcopy(T.go0[:, e:512:64], T.mask8[:], r=["mask8", "go0z"], p=["go0"])
-        constants(KG, 240, "bg", 0, ["bg"])
         unfilled("A")
         for h in range(NG):
             scopy(T.go[:, 64 * h:64 * h + 64], T.ones[:, 0:64], T.mask8[:, h:h + 1], r=["ones", "mask8"], p=["go"])
         sline(T.tpos[:], T.tri[:], 2 * FAR, -FAR, r=["tri"], w=["tpos"])
         sline(T.dpos[:], T.diag[:], 2 * FAR, -FAR, r=["diag"], w=["dpos"])
         sline(T.rstn[:], T.rst[:], 2 * FAR, -FAR, r=["rst"], w=["rstn"])
+        row_to_all(0)
+
+    def between_halves_of_x():
+        ts(T.bd[:, 1:512:4], T.ipr[:, 0:128], T.pif[:, 0:1], None, A.is_equal, r=["ipr", "pif", "bdz"], p=["bd"])
+        ts(T.bd[:, 2:512:4], T.ipr[:, 0:128], T.pif[:, 0:1], -1.0, A.is_equal, A.mult, r=["ipr", "pif", "bdz"], p=["bd"])
+        fill(T.xn[:, 0:84:2], 0.0, "xnz")
+        fill(T.xn[:, 1:84:2], MG16, "xnm")
+        for n in "AB":
+            fill(T["acc" + n][:, 0:1], 0.0, "acc0" + n)
+        ts(T.mask8n[:], T.h8[:], T.hcol[:, 0:1], -0.5, A.is_equal, A.mult, r=["h8", "hcol"], w=["mask8n"])
+
+    def behind_the_first_writes():
+        unfilled("B")
+        clear("bg", 0, 960, "bgz")
+        clear("ct", 2, 4 * NC, "ct2", 4)
+        clear("ct", 3, 4 * NC, "ct3", 4)
+        clear("eb", 0, 516, "ebz")
+        iota("tab0", 0, NC, [[-512, NC]], 512 * (NC - 1), 0)
+        iota("tier", 0, NC, [[-1, NC]], 511, 0)
+        iota("iot", 0, NC, [[1, NC]], 0, 0)
 
     def while_own_scores_come():
-        ts(T.tiec[:, 0:3], T.tiec[:, 0:3], 1.0 / 512, 1.0 / 1024, A.mult, A.add, r=["tiec0", "tiec1"], w=["tiec"])
+        ts(T.tiec[:, 0:3], T.tiec[:, 0:3], 0.5, None, A.add, r=["tiec0", "tiec1"], w=["tiec"])
         ts(T.lm[:], T.lf[:, 24:44], -15.0, 0.0625, A.add, A.mult, r=["lf1"], w=["lm"])
         ts(T.ramp[:], T.lf[:, 24:44], T.pif[:, 0:1], None, A.subtract, r=["lf1", "pif"], w=["ramp"])
         constants(KO, 128, "go", 0, ["go"])
         constants(KF, 128, "go0", 0, ["go0"])
-        row_to_all(0)
+        row_to_all(1)
 
     def while_codes_come():
-        fill(T.ct[:, 2:4 * NC:4], 0.0, "ct2")
-        fill(T.ct[:, 3:4 * NC:4], 0.0, "ct3")
-        fill(T.eb[:], 0.0, "ebz")
+        constants(KB, 128, "bd", 0, ["bd"])
         quantise_row_to_all(0)
-        vcopy(T.eb[:, 3:515:4], T.ident[:], r=["ident", "ebz"], w=["eb"])
-        row_to_all(1)
-        unfilled("B")
-        sline(T.tab0[:], T.iot[:], -1.0, 319.0, r=["iot"], w=["tab0"])
-        sline(T.tier[:], T.iot[:], -1.0 / 512, 511.0 / 512, r=["iot"], w=["tier"])
-        row_to_all(2)
         quantise_row_to_all(1)
+        row_to_all(2)
 
     def own_scores(X):
         mm(0, NC, "up", 256, X, 0)
@@ -367,9 +387,9 @@ def rank_program(g, core, T, topo):
         for m in BY_VECTOR:
             ssum(part(n, m), 16 * m, T["acc" + n][:, m:m + 1], "acc" + n, ["mt%s%d" % (n, m)])
 
-    def column_sums(n, us):
+    def column_sums(t, n, us):
         o, c, key = TILE[us[0]][0], TILE[us[0]][0] + (MT if n == "B" else 0), "mq%s%d" % (n, us[0])
-        w = sum(TILE[u][1] for u in us)
+        w = sum(TILE[u][1] for u in us) - (64 if t and us[0] else 0)
         r = ["mz%s%d" % (n, u) for u in us] + ["mt%s%d" % (n, NM - 4 * u - e) for u in us for e in range(4)]
         quant("mq", c, c + w, "mt" + n, 4 * o, r, key)
         for u in us:
@@ -386,15 +406,11 @@ def rank_program(g, core, T, topo):
         mm(h % 4, NC, "kq", KW + 128 * h, "cq", 0)
 
     def copy_table(h):
-        k = h % 4
-        if h == 0:
-            tt(plane("cw", 0), bank(k), T.tab0[:], A.add, r=[ps(k), "tab0"], w=["cw0"])
-        else:
-            scopy(plane("cw", h), bank(k), r=[ps(k)], w=["cw%d" % h])
+        scopy(plane("cw", h), bank(h % 4), r=[ps(h % 4)], w=["cw%d" % h])
 
-    def look_up(h, prev):
+    def look_up(h, prev, a=0, b=NC):
         new = "kr%d" % (h % 2)
-        tt(T[new][:], plane("cw", h).indirect(T.off[:, 0:NM]), T[prev][:], A.add, r=["cw%d" % h, "off", prev], w=[new])
+        tt(T[new][:, a:b], plane("cw", h).indirect(T.off[:, a // 16:b // 16]), T[prev][:, a:b], A.add, r=["cw%d" % h, "off", prev], p=[new])
         return new
 
     def count_teams(prev, c):
@@ -420,67 +436,73 @@ def rank_program(g, core, T, topo):
         for n, a in (("A", 0), ("B", 128)):
             mm(SB[n], NC, "up", a, PX, 0)
         own_column("A")
-        ts(T.d0[:, 0:3], T.a0[:, 0:3], -1.0, 159.0, A.mult, A.add, r=["a0"], w=["d0"])
         own_column("B")
         carry("A")
-        for c in range(3):
-            a, b, ma, mb = block_of(c)
-            ts(slots(a, b), T.mask8[:, ma:mb], T.d0[:, c:c + 1], None, A.mult, r=["mask8", "d0", "xnz"], p=["xn"])
         carry("B")
-        digits()
-        inside("A")
-        spread(0)
-        ts(T.offo[:, 0:3], T.d0[:, 0:3], 160.0, None, A.add, r=["d0"], w=["offo"])
         scalar_compare("A")
         compare("A", BY_VECTOR)
         add_up("A")
-        take_offsets()
+        inside("A")
         inside("B")
         scalar_compare("B")
         compare("B", BY_VECTOR)
         add_up("B")
-        column_sums("A", (0,))
-        column_sums("A", (2, 3, 4))
-        column_sums("A", (1,))
+        column_sums(t, "A", (0,))
+        column_sums(t, "A", (2, 3, 4))
+        column_sums(t, "A", (1,))
         inside_sums("A")
         inside_sums("B")
         row_part("A", 0)
+        if t == 0:
+            vcopy(T.bg[:, 448:512], T.bd[:, 0:64], r=["bd", "bgz"], w=["bg"])
+            ts(T.eb[:, 3:515:4], T.triv[:], 0.0, None, A.is_equal, r=["triv", "ebz"], w=["eb"])
+        column_sums(t, "B", (0,))
         tt(T.rkd[:], bank(CB["A"]), T.diag[:], A.mult, r=[ps(CB["A"]), "diag"], w=["rkd"])
-        column_sums("B", (0,))
+        column_sums(t, "B", (2, 3, 4))
         scan(T.cs[:], T.rkd[:], r=["rst", "rkd"], w=["cs"])
         row_part("A", 1)
         row_part("B", 0)
-        column_sums("B", (2, 3, 4))
+        column_sums(t, "B", (1,))
         tt(T.plA[:], T.owA[:], T.cs[:, 15:NC:16], A.add, r=["owA", "cs"], w=["plA"])
-        column_sums("B", (1,))
         vcopy(T.aoff[:], T.plA[:], r=["plA"], w=["aoff"])
-        steps = [
-            lambda: row_part("B", 1),
-            lambda: tt(T.bx[:], T.owB[:, 0:NM].indirect(T.lm[:, 0:NM]), T.diag[:], A.mult, r=["owB", "lm", "diag"], w=["bx"]),
-            lambda: tt(T.bt[:], bank(CB["B"]), T.bx[:], A.add, r=[ps(CB["B"]), "bx"], w=["bt"]),
-            lambda: vcopy(T.cx[:, 0:NC].indirect(T.aoff[:, 0:NM]), T.bt[:], r=["aoff", "bt"], w=["cx"])]
-        for b in range(4):
-            steps[b]()
-            if t == 0:
-                quantise_unpacking(b)
-        H = NC // 2
-        for a in (0, H):
+        row_part("B", 1)
+        ts(T.d0[:, 0:3], T.a0[:, 0:3], -1.0, 159.0, A.mult, A.add, r=["a0"], w=["d0"])
+        tt(T.bx[:], T.owB[:, 0:NM].indirect(T.lm[:, 0:NM]), T.diag[:], A.mult, r=["owB", "lm", "diag"], w=["bx"])
+        for c in range(3):
+            a, b, ma, mb = block_of(c)
+            ts(slots(a, b), T.mask8[:, ma:mb], T.d0[:, c:c + 1], None, A.mult, r=["mask8", "d0", "xnz"], p=["xn"])
+        tt(T.bt[:], bank(CB["B"]), T.bx[:], A.add, r=[ps(CB["B"]), "bx"], w=["bt"])
+        if t == 0:
+            constants(KG, 240, "bg", 0, ["bg"])
+        digits()
+        ts(T.offo[:, 0:3], T.d0[:, 0:3], 160.0, None, A.add, r=["d0"], w=["offo"])
+        vcopy(T.cx[:, 0:NC].indirect(T.aoff[:, 0:NM]), T.bt[:], r=["aoff", "bt"], w=["cx"])
+        spread(0)
+        for a in HALVES:
             ts(T.ct[:, 4 * a:4 * (a + H):4], T.cx[:, a:a + H], MG32, MG32, A.add, A.subtract, r=["cx"], w=["cthi%d" % a])
-        for a in (0, H):
+        for a in HALVES:
             tt(T.ct[:, 4 * a + 1:4 * (a + H):4], T.cx[:, a:a + H], T.ct[:, 4 * a:4 * (a + H):4], A.subtract, r=["cx", "cthi%d" % a], w=["ctlo%d" % a])
-        for a in (0, H):
-            quant("cq", a, a + H, "ct", 4 * a, ["cthi%d" % a, "ctlo%d" % a, "ct2", "ct3"])
+        for a in HALVES:
+            quant("cq", a, a + H, "ct", 4 * a, ["cthi%d" % a, "ctlo%d" % a, "ct2", "ct3"], hk("cq", a))
+        take_offsets()
+        if t == 0:
+            for b in range(4):
+                quantise_unpacking(b)
 
     def draft(t, PX):
         last = t == 1
-        for h in range(2):
-            table(h)
-            copy_table(h)
-        own_totals(0)
-        prev = look_up(0, "tier")
-        own_totals_picked()
+        for n, a in enumerate(HALVES):
+            mm(2 * n, H, "kq", KW, "cq", a, key=hk("cq", a))
+        table(1)
+        for n, a in enumerate(HALVES):
+            tt(plane("cw", 0, a, a + H), bank(2 * n, 0, H), T.tab0[:, a:a + H], A.add, r=[ps(2 * n), "tab0"], p=["cw0"])
+        copy_table(1)
         if t == 0:
             quantise_row_to_all(2)
+        own_totals(0)
+        look_up(0, "tier", 0, H)
+        own_totals_picked()
+        prev = look_up(0, "tier", H, NC)
         own_totals_added("tiec")
         for h in range(1, NG):
             own = h < NG - 1
@@ -541,49 +563,82 @@ def rank_program(g, core, T, topo):
             cp(T.zt[:, k:4 * NC:4], plane("fs", k).indirect(T.noff[:, 0:NM]), r=["fs%d" % k, "noff"], p=["zt"])
         vcopy(T.sr[:, 0:NC].indirect(T.noff[:, 0:NM]), T.iot[:], r=["noff", "iot"], w=["sr"])
         quant("zq", 0, NC, "zt", 0, ["zt"])
-        for b in range(4):
-            mm(4 + b, NC, "ww", 128 * (b + 4), "zq", 0)
+        for b in (4, 5, 0, 6, 1, 7, 2, 3):
             mm(b, NC, "ww", 128 * b, "zq", 0)
-            scopy(plane("cc", b), bank(4 + b), r=[ps(4 + b)], w=["cc%d" % b])
-
-        def larger(b):
-            tt(plane("yp", b), bank(b), plane("cc", b), A.max, r=[ps(b), "cc%d" % b], w=["yp%d" % b])
-
+            if b >= 4:
+                scopy(plane("cc", b - 4), bank(b), r=[ps(b)], w=["cc%d" % (b - 4)])
         tt(T.rkd[:], T.sr[:, 0:NC].indirect(T.aoff[:, 0:NM]), T.diag[:], A.mult, r=["sr", "aoff", "diag"], w=["rkd"])
         scan(T.rks[:], T.rkd[:], r=["rst", "rkd"], w=["rks"])
-        larger(0)
-        vcopy(T.koff[:], T.rks[:, 15:NC:16], r=["rks"], w=["koff"])
-        for b in range(1, 4):
-            larger(b)
-        for k in range(2):
-            scopy(T.yt[:, k:4 * NC:4], plane("yp", k).indirect(T.koff[:, 0:NM]), 0.03125, r=["yp%d" % k, "koff"], p=["yt"])
-            j = 2 + k
-            ts(T.yt[:, j:4 * NC:4], plane("yp", j).indirect(T.koff[:, 0:NM]), 0.03125, None, A.mult, r=["yp%d" % j, "koff"], p=["yt"])
-        quant(YQ, 0, NC, "yt", 0, ["yt"])
-        send_tile(t, 4 * t + 2, PY, YQ)
+        for b in range(4):
+            tt(plane("yp", b), bank(b), plane("cc", b), A.max, r=[ps(b), "cc%d" % b], w=["yp%d" % b])
+            if b == 0:
+                vcopy(T.koff[:], T.rks[:, 15:NC:16], r=["rks"], w=["koff"])
+        for a in HALVES:
+            for k in range(4):
+                out, src = T.yt[:, 4 * a + k:4 * (a + H):4], plane("yp", k).indirect(T.koff[:, a // 16:(a + H) // 16])
+                if k < (3 if a else 2):
+                    scopy(out, src, 0.03125, r=["yp%d" % k, "koff"], p=["yt%d" % a])
+                else:
+                    ts(out, src, 0.03125, None, A.mult, r=["yp%d" % k, "koff"], p=["yt%d" % a])
+            quant(YQ, a, a + H, "yt", 4 * a, ["yt%d" % a], hk(YQ, a))
+            if SPLIT_Y:
+                send_tile(t, PY, YQ, (a,))
+        if not SPLIT_Y:
+            send_tile(t, PY, YQ, HALVES)
         if last:
             prev = look_up(NG - 1, prev)
             tt(T.tsb[0:1, :], T[prev][0:1, :], T.tier[0:1, :], A.subtract, r=[prev, "tier"], w=["tsb"])
+            ts(T.tsb[0:1, :], T.tsb[0:1, :], 1.0 / 512, None, A.mult, w=["tsb"])
             dma("sy", T.tot[:, :], T.tsb[0:1, :], r=["tsb"])
         else:
             quant("vq", 0, 128, "vt", 0, ["vt"])
-        for b in range(4):
-            mm(b, NC, "kq", KE + 128 * b, X, 0, True, False)
-        for b in range(4):
-            mm(b, NC, "kq", KE + 128 * b, PY, 0, False, True)
-            cp = scopy if b % 2 else vcopy
-            cp(T.xt1[:, b:4 * NC:4], bank(b), r=[ps(b)], p=["xt1"])
-        quant("xq%d" % (t + 1), 0, NC, "xt1", 0, ["xt1"])
+        NX = "xq%d" % (t + 1)
+        for n, a in enumerate(HALVES):
+            for b in range(4):
+                mm(4 * n + b, H, "kq", KE + 128 * b, X, a, True, False, hk(X, a))
+        for n, a in enumerate(HALVES):
+            for b in range(4):
+                mm(4 * n + b, H, "kq", KE + 128 * b, PY, a, False, True, hk(PY, a))
+        for n, a in enumerate(HALVES):
+            for b in range(4):
+                cp = scopy if b % 2 else vcopy
+                cp(T.xt1[:, 4 * a + b:4 * (a + H):4], bank(4 * n + b, 0, H), r=[ps(4 * n + b)], p=["xt1%d" % a])
+            if last and n:
+                store_y(0, 0)
+            quant(NX, a, a + H, "xt1", 4 * a, ["xt1%d" % a], hk(NX, a))
+            if last:
+                store(n, a)
+            elif SPLIT_X:
+                send_tile(1, "px1", NX, (a,))
+        if not last and not SPLIT_X:
+            send_tile(1, "px1", NX, HALVES)
 
-    dma("sy", T.xt0[:, :], T.x[:, :], p=["xt0"])
+    def store(n, a):
+        key = hk("xq2", a)
+        mm(4 * n, H, "vq", 0, "xq2", a, key=key)
+        dma("sy", T.oc[:, 4 * a:4 * (a + H)], codes("xq2", a, a + H), r=[key])
+
+    def store_y(n, a):
+        vcopy(T.ysb[:, a:a + H], bank(4 * n, 0, H), r=[ps(4 * n)], w=["ysb%d" % a])
+        dma("s" if n else "sy", T.y[:, a:a + H], T.ysb[:, a:a + H], r=["ysb%d" % a])
+
+    for a in HALVES:
+        dma("sy", T.xt0[:, 4 * a:4 * (a + H)], T.x[:, 4 * a:4 * (a + H)], w=["xt0%d" % a])
     dma("sy", T.ut[:, :], T.u[:, :], w=["ut"])
     while_x_comes()
-    quant("xq0", 0, NC, "xt0", 0, ["xt0"])
-    send_tile(0, 0, "px0", "xq0")
+    for a in HALVES:
+        quant("xq0", a, a + H, "xt0", 4 * a, ["xt0%d" % a], hk("xq0", a))
+        if SPLIT_0:
+            send_tile(0, "px0", "xq0", (a,))
+        if a == 0:
+            between_halves_of_x()
+    if not SPLIT_0:
+        send_tile(0, "px0", "xq0", HALVES)
+    behind_the_first_writes()
     quant("uq", 0, 128, "ut", 0, ["ut"])
     do("v", lambda: V.tensor_copy(T.upc[:, 0:384].bitcast(dt.uint32), T.uqc[:, 0:128].bitcast(dt.uint32).indirect(T.lu[:, 0:24])), r=["uq", "lu"], p=["up"])
     do("s", lambda: S.activation(T.ups[:, 0:384], T.uqs[:, 0:128].indirect(T.lu[:, 0:24]), F.Copy), r=["uq", "lu"], p=["up"])
-    dma("sy", codes("ww", 0, 1024), T.wc[:, :], r=["px0"], p=["ww"])
+    dma("sy", codes("ww", 0, 1024), T.wc[:, :], r=both("px0"), p=["ww"])
     dma("sy", T.wws[:, :], T.ws[:, :], p=["ww"])
     dma("sy", T.vt[:, :], T.v[:, :], w=["vt"])
     for t in range(2):
@@ -596,20 +651,14 @@ def rank_program(g, core, T, topo):
             while_codes_come()
         places(t, PX)
         layer(t, draft(t, PX))
-        if t == 0:
-            send_tile(1, 4, "px1", "xq1")
-
-    mm(4, NC, "vq", 0, "xq2", 0)
-    dma("sy", T.oc[:, :], codes("xq2", 0, NC), r=["xq2"])
     for k in range(4):
-        dma("sy", T.osc[4 * k:4 * k + 4, :], T.xq2s[32 * k:32 * k + 4, 0:NC], r=["xq2"])
-    scopy(T.ysb[:], bank(4), r=[ps(4)], w=["ysb"])
-    dma("s", T.y[:, :], T.ysb[:], r=["ysb"])
+        dma("sy", T.osc[4 * k:4 * k + 4, :], T.xq2s[32 * k:32 * k + 4, 0:NC], r=both("xq2"))
+    store_y(1, H)
 
     for s in ("v", "s", "t", "gp"):
         g.sync.wait_ge(T.sem[s], count[s])
     for k in range(tally["dma"]):
         g.sync.wait_ge(T.sem["d%d" % k], 16)
-    for k in range(8):
-        g.sync.wait_ge(T.sem["rx%d" % k], engines_between(partner(k // 4), core))
+    for s, n in arrivals:
+        g.sync.wait_ge(T.sem[s], n)
     g.sync.wait_ge(T.sem["ls"], tally["ls"])

@@ -1,11 +1,13 @@
-from concourse.mybir import dt, AluOpType as A, ActivationFunctionType as F
+from concourse.mybir import dt, AluOpType as A, AxisListType, ActivationFunctionType as F
 
 NC = 320
 NG = 8
 NM = 20
 TILE = ((0, 320), (320, 320), (640, 192), (832, 128), (960, 128))
 MT = 1088
-BY_SCALAR = (19, 18, 17)
+SHORT = 192
+ORDER = "AB"
+BY_SCALAR = (19, 18, 17, 16, 15, 9)
 BY_VECTOR = tuple(m for m in range(NM - 1, 0, -1) if m not in BY_SCALAR)
 PIECE = (0, 128, 192)
 
@@ -24,30 +26,31 @@ def _mx(name, cols):
 
 for _n, _c in (("tab0", NC), ("tier", NC), ("iot", NC), ("hcol", 1), ("pif", 1), ("ramp", NM),
                ("mask8", 8), ("mask8n", 8), ("maskw", 8), ("h8", 8), ("tiec", 4), ("triv", 128), ("lf", 48),
-               ("a0", 4), ("d0", 4), ("r1", 384), ("dg", 2 * NC), ("sc", 2 * NC), ("cs", NC),
+               ("a0", 12), ("d0", 4), ("r1", NC), ("dg", 2 * NC), ("sc", 2 * NC), ("cs", NC + 16),
                ("accA", NM), ("accB", NM), ("owA", NM), ("owB", NM), ("plA", NM),
-               ("bx", NC), ("bt", NC), ("cx", NC), ("ir", NC), ("di", NC), ("si", NC),
+               ("bx", NC), ("bt", NC), ("cx", NC), ("df", NM),
                ("xn", 84), ("kr0", NC), ("kr1", NC), ("pk", 4), ("cnt", 4), ("ogd", 48), ("os1", 48),
-               ("sr", NC), ("rkd", NC), ("rks", NC), ("cc", 4 * NC), ("ysb", NC), ("tsb", NC), ("cw", NG * NC)):
+               ("sr", NC), ("rkd", NC), ("rks", NC), ("cc", 4 * NC), ("ysb", NC), ("tsb", 8), ("cw", NG * NC)):
     _sb(_n, _c, F32)
 for _n, _c in (("ipr", NC), ("diag", NC), ("rst", NC), ("dpos", NC), ("rstn", NC), ("go", 512), ("go0", 512), ("xt0", 4 * NC), ("xt1", 4 * NC),
-               ("ut", 512), ("vt", 512), ("ones", 512), ("eb", 516), ("wg", 4096), ("bd", 512), ("bg", 960), ("tri", 128),
-               ("tpos", 128), ("a0c", 3 * 448), ("dd", 2 * NC), ("mtA", 4 * MT), ("mtB", 4 * MT),
-               ("junk", 4 * 448), ("cb", NC), ("cbs", NC), ("ct", 4 * NC), ("nt", 512), ("zt", 4 * NC), ("yt", 4 * NC),
-               ("fp", 4 * NC), ("fs", 4 * NC), ("yp", 4 * NC)):
+               ("ut", 512), ("vt", 512), ("ones", 512), ("eb", 516), ("wg", 4096), ("bd", 512), ("bg", 960), ("tri", NC),
+               ("tpos", NC), ("a0c", 3 * 448), ("dd", NC), ("rs2", SHORT), ("ds", 8 * SHORT), ("mtA", 4 * MT), ("mtB", 4 * MT),
+               ("junk", 16 * 448), ("cb", NC), ("cbs", NC), ("ct", 4 * NC), ("nt", 512), ("zt", 4 * NC), ("yt", 4 * NC),
+               ("fp", 4 * NC), ("fs", 4 * NC), ("yp", 4 * NC), ("iom", NC), ("ir", NC + 32), ("it", 2 * NC + 32)):
     _sb(_n, _c, BF)
 _sb("pi_i", 4, I32)
-for _n, _c in (("lm", NM), ("lu", 24), ("aoff", NM), ("inva", NM), ("off", NM), ("offo", 4), ("noff", NM), ("koff", NM)):
+for _n, _c in (("lm", NM), ("lu", 24), ("aoff", NM), ("inva", 32), ("lt", 2), ("off", NM), ("offo", 4), ("noff", NM), ("koff", NM)):
     _sb(_n, _c, U16)
 KE, KW, KB, KG, KO, KF = 0, 512, 1536, 1664, 1904, 2032
 for _n, _c in (("xq0", NC), ("xq1", NC), ("xq2", NC), ("px0", NC), ("px1", NC), ("py0", NC), ("py1", NC), ("uq", 128), ("up", 384), ("vq", 128),
-               ("kq", 2160), ("mq", 2 * MT), ("nq", 128), ("cq", NC), ("zq", NC), ("yq0", NC), ("yq1", NC), ("ww", 1024)):
+               ("kq", 2160), ("mq", 2 * MT), ("nq", 256), ("cq", NC), ("zq", NC), ("yq0", NC), ("yq1", NC), ("ww", 1024)):
     _mx(_n, _c)
 
-SEMAPHORES = ["v", "s", "t", "gp", "ls"] + ["d%d" % k for k in range(16)] + ["rx%d" % k for k in range(16)]
+SEMAPHORES = ["v", "s", "t", "gp", "ls"] + ["d%d" % k for k in range(20)] + ["rx%d" % k for k in range(16)]
 H = NC // 2
 HALVES = (0, H)
 SPLIT_0, SPLIT_X, SPLIT_Y = True, True, True
+SPLIT_P, REDUCE_V, FILL_V = True, False, ()
 
 MG16 = 1.5 * 2.0 ** 27
 MG32 = 1.5 * 2.0 ** 28
@@ -168,7 +171,7 @@ def rank_program(g, core, T, topo):
         return T[name][:, o + a:o + b:step]
 
     def junk(n):
-        k = tally["junk"] % 4
+        k = tally["junk"] % 16
         tally["junk"] += 1
         return T.junk[:, 448 * k:448 * k + n], "junk%d" % k
 
@@ -224,13 +227,15 @@ def rank_program(g, core, T, topo):
     def clear(name, a, b, key, step=1):
         do("gp", lambda: g.iota(T[name][:, a:b:step], [[0, (b - a + step - 1) // step]], 0, 0, allow_small_or_imprecise_dtypes=True), w=[key])
 
-    def unfilled(n):
-        for u, (o, w) in enumerate(TILE):
-            a, b = 4 * o + 64 * (17 - 4 * u), 4 * (o + w)
-            if n == "A":
-                scopy(T.mtA[:, a:b], T.ones[:, 0:b - a], 0.0, r=["ones"], w=["mzA%d" % u])
+    def unfilled(n, us, eng):
+        for u in us:
+            a, b, key = 4 * TILE[u][0] + 64 * (17 - 4 * u), 4 * sum(TILE[u]), "mz%s%d" % (n, u)
+            if eng == "s":
+                scopy(T["mt" + n][:, a:b], T.ones[:, 0:b - a], 0.0, r=["ones"], w=[key])
+            elif eng == "v":
+                fill(T["mt" + n][:, a:b], 0.0, key)
             else:
-                clear("mtB", a, b, "mzB%d" % u)
+                clear("mt" + n, a, b, key)
 
     def row_to_all(h):
         scopy(T.wg[:, 512 * h:512 * h + 512], T.ones[:], T.maskw[:, h:h + 1], r=["ones", "maskw"], w=["wg%d" % h])
@@ -261,15 +266,12 @@ def rank_program(g, core, T, topo):
         do("v", lambda: V.memset(T.lu[:, 16:24], 0), p=["lu"])
         ts(T.mask8[:], T.h8[:], T.hcol[:, 0:1], None, A.is_equal, r=["h8", "hcol"], w=["mask8"])
         ts(T.maskw[:], T.h8[:], T.hcol[:, 0:1], 512.0, A.is_equal, A.mult, r=["h8", "hcol"], w=["maskw"])
-        ts(T.tri[:], T.triv[:], 0.0, None, A.is_lt, r=["triv"], w=["tri"])
-        fill(T.nt[:], 0.0, "ntz")
+        for c in range(3):
+            o = 128 * c - PIECE[c]
+            ts(T.tri[:, 128 * c:128 * c + 128 - o], T.triv[:, o:128], 0.0, None, A.is_lt, r=["triv"], p=["tri"])
         ts(T.diag[:], T.ipr[:], T.pif[:, 0:1], None, A.is_equal, r=["ipr", "pif"], w=["diag"])
         ts(T.rst[:], T.ipr[:], 0.0, None, A.is_gt, r=["ipr"], w=["rst"])
-        for e in range(4):
-            vcopy(T.go0[:, e:512:64], T.mask8[:], r=["mask8", "go0z"], p=["go0"])
-        unfilled("A")
-        for h in range(NG):
-            scopy(T.go[:, 64 * h:64 * h + 64], T.ones[:, 0:64], T.mask8[:, h:h + 1], r=["ones", "mask8"], p=["go"])
+        unfilled("B", range(5), "s")
         sline(T.tpos[:], T.tri[:], 2 * FAR, -FAR, r=["tri"], w=["tpos"])
         sline(T.dpos[:], T.diag[:], 2 * FAR, -FAR, r=["diag"], w=["dpos"])
         sline(T.rstn[:], T.rst[:], 2 * FAR, -FAR, r=["rst"], w=["rstn"])
@@ -278,51 +280,98 @@ def rank_program(g, core, T, topo):
     def between_halves_of_x():
         ts(T.bd[:, 1:512:4], T.ipr[:, 0:128], T.pif[:, 0:1], None, A.is_equal, r=["ipr", "pif", "bdz"], p=["bd"])
         ts(T.bd[:, 2:512:4], T.ipr[:, 0:128], T.pif[:, 0:1], -1.0, A.is_equal, A.mult, r=["ipr", "pif", "bdz"], p=["bd"])
-        fill(T.xn[:, 0:84:2], 0.0, "xnz")
-        fill(T.xn[:, 1:84:2], MG16, "xnm")
-        for n in "AB":
-            fill(T["acc" + n][:, 0:1], 0.0, "acc0" + n)
-        ts(T.mask8n[:], T.h8[:], T.hcol[:, 0:1], -0.5, A.is_equal, A.mult, r=["h8", "hcol"], w=["mask8n"])
+        for e in range(4):
+            vcopy(T.go0[:, e:512:64], T.mask8[:], r=["mask8", "go0z"], p=["go0"])
+        fill(T.rs2[:], 1.0, "rs2")
 
     def behind_the_first_writes():
-        unfilled("B")
+        unfilled("A", [u for u in (0, 2, 1, 3, 4) if u not in FILL_V], "gp")
+        iota("go", 0, 512, [[1, 8], [0, 64]], 0, 0)
         clear("bg", 0, 960, "bgz")
+        clear("eb", 0, 516, "ebz")
+        clear("nt", 4 * NM, 512, "ntz")
         clear("ct", 2, 4 * NC, "ct2", 4)
         clear("ct", 3, 4 * NC, "ct3", 4)
-        clear("eb", 0, 516, "ebz")
         iota("tab0", 0, NC, [[-512, NC]], 512 * (NC - 1), 0)
         iota("tier", 0, NC, [[-1, NC]], 511, 0)
+        iota("iom", 0, NC, [[1, NC]], -160, 0)
+        clear("ir", 0, 16, "irz0")
+        clear("ir", NC + 16, NC + 32, "irz")
         iota("iot", 0, NC, [[1, NC]], 0, 0)
 
-    def while_own_scores_come():
+    def while_u_comes():
         ts(T.tiec[:, 0:3], T.tiec[:, 0:3], 0.5, None, A.add, r=["tiec0", "tiec1"], w=["tiec"])
         ts(T.lm[:], T.lf[:, 24:44], -15.0, 0.0625, A.add, A.mult, r=["lf1"], w=["lm"])
         ts(T.ramp[:], T.lf[:, 24:44], T.pif[:, 0:1], None, A.subtract, r=["lf1", "pif"], w=["ramp"])
-        constants(KO, 128, "go", 0, ["go"])
-        constants(KF, 128, "go0", 0, ["go0"])
-        row_to_all(1)
+        fill(T.xn[:, 0:84:2], 0.0, "xnz")
+        fill(T.xn[:, 1:84:2], MG16, "xnm")
+        fill(T.rs2[:, 128:129], 0.0, "rs2")
+        fill(T.tiec[0:64, 2:3], 2.0 ** 22, "tiec")
+        fill(T.a0c[:, 3 * 448 - 64:3 * 448], 1.0, "a0z")
 
-    def while_codes_come():
+    def while_own_scores_come():
+        constants(KF, 128, "go0", 0, ["go0"])
         constants(KB, 128, "bd", 0, ["bd"])
         quantise_row_to_all(0)
-        quantise_row_to_all(1)
-        row_to_all(2)
+        ts(T.mask8n[:], T.h8[:], T.hcol[:, 0:1], -0.5, A.is_equal, A.mult, r=["h8", "hcol"], w=["mask8n"])
+        vcopy(T.owA[:], T.ramp[:], r=["ramp"], w=["ow0A", "ow1A", "ow5A", "ow9A"])
+        fill(T.cs[:, 15:16], 0.0, "csz")
+
+    def adding_up_by_group():
+        ts(T.go[:], T.go[:], T.hcol[:, 0:1], None, A.is_equal, r=["hcol"], w=["go"])
+
+    def list_of_turned_rows(k):
+        if k == 0:
+            tt(T.pi_i[:, 3:4], T.pi_i[:, 0:1], T.pi_i[:, 2:3], A.add, r=["pi_i", "pi2"], w=["pi3"])
+        elif k == 1:
+            ts(T.pi_i[:, 3:4], T.pi_i[:, 3:4], 1, None, A.bitwise_and, w=["pi3"])
+        elif k == 2:
+            ts(T.lf[:, 16:17], T.pi_i[:, 3:4], NC + 16.0, None, A.mult, r=["pi3"], w=["lf2"])
+        elif k == 3:
+            ts(T.lt[:, 0:1], T.pif[:, 0:1], 16.0, T.lf[:, 16:17], A.mult, A.add, r=["pif", "lf2"], w=["lt0"])
+        else:
+            ts(T.lt[:, 1:2], T.lt[:, 0:1], 256.0, 2.0 * NC, A.add, A.min, r=["lt0"], w=["lt"])
+
+    OB = (1, 3, 2)
 
     def own_scores(X):
         mm(0, NC, "up", 256, X, 0)
-        for c in range(3):
-            mm(1 + c, 128, X, PIECE[c], "uq", 0)
+        for c in (0, 2, 1):
+            mm(OB[c], 128, X, PIECE[c], "uq", 0)
+        mm(4, NC, "up", 256, X, 0)
 
     def own_places():
-        for c in range(3):
-            o, sc, k, rr = PIECE[c], bank(1 + c, 0, 1), 448 * c, [ps(0), ps(1 + c)]
-            key, r1 = "a0c%d" % c, T.r1[:, 128 * c:128 * c + 128]
-            tt(r1, bank(0, o, o + 128), T.tpos[:], A.min, r=[ps(0), "tpos"], w=["r1%d" % c])
-            if o:
-                ts(T.a0c[:, k:k + o], bank(0, 0, o), sc, None, A.is_ge, r=rr, p=[key])
-            ts(T.a0c[:, k + o:k + NC], bank(0, o, NC), sc, None, A.is_gt, r=rr, p=[key])
-            ts(T.a0c[:, k + NC:k + NC + 128], r1, sc, None, A.is_equal, r=["r1%d" % c, ps(1 + c)], p=[key])
-            ssum(T.a0c[:, k:k + 448], 448, T.a0[:, c:c + 1], "a0", [key])
+        long = ((0, NC), (2, 256))
+        scopy(T.a0[:, 4:6], T.ps[:, 512:1025:512], r=[ps(1), ps(2)], w=["own"])
+        for c, n in long:
+            do("s", lambda: S.activation(T.a0c[:, 448 * c:448 * c + n], bank(4, 0, n), F.Sign, bias=T.a0[:, 4 + c // 2:5 + c // 2], scale=-1.0),
+               r=[ps(4), "own"], p=["a0c%d" % c])
+        tt(T.r1[:], bank(0), T.tpos[:], A.min, r=[ps(0), "tpos"], w=["r1"])
+        for c in (1, 0, 2):
+            o, sc, k, rr, key = 128 * c, bank(OB[c], 0, 1), 448 * c, [ps(0), ps(OB[c])], "a0c%d" % c
+            if c == 1:
+                ts(T.a0c[:, k:k + o], bank(0, 0, o), sc, -1.0, A.is_ge, A.mult, r=rr, p=[key])
+                ts(T.a0c[:, k + o:k + NC], bank(0, o, NC), sc, -1.0, A.is_gt, A.mult, r=rr, p=[key])
+            if c < 2:
+                ts(T.a0c[:, k + NC:k + 448], T.r1[:, o:o + 128], sc, -1.0, A.is_equal, A.mult, r=["r1", ps(OB[c])], p=[key])
+            else:
+                ts(T.a0c[:, k + o:k + NC], bank(0, o, NC), sc, None, A.is_le, r=rr, p=[key])
+                ts(T.a0c[:, k + NC:k + 384], T.r1[:, o:NC], sc, None, A.not_equal, r=["r1", ps(OB[c])], p=[key])
+
+    def own_sums():
+        if REDUCE_V:
+            do("v", lambda: V.tensor_reduce(T.a0[:, 1:2], T.a0c[:, 448:896], AxisListType.X, A.add), r=["a0c1"], p=["a0"])
+        for c in (0, 2) if REDUCE_V else (1, 0, 2):
+            j, jk = junk(448)
+            do("s", lambda: S.activation(j, T.a0c[:, 448 * c:448 * c + 448], F.Sign, bias=0.5 if c == 2 else -0.5, scale=-1.0, accum_out=T.a0[:, c:c + 1]),
+               r=["a0c%d" % c, "a0z"], w=[jk], p=["a0"])
+
+    def first_turns():
+        if REDUCE_V:
+            ts(T.d0[:, 0:3:2], T.a0[:, 0:3:2], -0.5, -65.0, A.mult, A.add, r=["a0"], p=["d0"])
+            ts(T.d0[:, 1:2], T.a0[:, 1:2], 159.0, None, A.add, r=["a0"], p=["d0"])
+        else:
+            ts(T.d0[:, 0:3], T.a0[:, 0:3], -0.5, -65.0, A.mult, A.add, r=["a0"], w=["d0"])
 
     def block_of(c):
         return (8 * c, 8 * c + 8, 0, 8) if c < 2 else (16, 20, 4, 8)
@@ -335,21 +384,35 @@ def rank_program(g, core, T, topo):
            r=["xn", "xnz", "xnm", "ntz"], w=["nt"])
 
     def spread(h, every=True):
-        quant("nq", 0, 128, "nt", 0, ["nt", "ntz"], "nq")
+        a = 0 if h else 128
+        quant("nq", a, a + 128, "nt", 0, ["nt", "ntz"], hk("nq", a))
         if every:
-            mm(6, 128, "kq", KB, "nq", 0)
-        mm(7, 128, "kq", KG + 112 - 16 * h, "nq", 0, h == 0, h == NG - 1, lkey="kq%d" % KG)
+            mm(6, 128, "kq", KB, "nq", a, key=hk("nq", a))
+        for k in ((), (0, 1))[h] if h < 2 else (h,):
+            a = 0 if k else 128
+            mm(7, 128, "kq", KG + 112 - 16 * k, "nq", a, k == 0, k == NG - 1, hk("nq", a), "kq%d" % KG)
 
     def take_offsets():
         ts(T.off[:], bank(6, 0, NM), 160.0, None, A.add, r=[ps(6)], w=["off"])
 
-    VB, SB, CB = {"A": 4, "B": 5}, {"A": 0, "B": 1}, {"A": 2, "B": 3}
+    EB, VB, SB, CB = {"A": 6, "B": 7}, {"A": 4, "B": 5}, {"A": 0, "B": 1}, {"A": 2, "B": 3}
+    EARLY = tuple(m for m in BY_VECTOR if 16 * m < H)
+    LATE = tuple(m for m in BY_VECTOR if 16 * m >= H)
 
-    def own_column(n):
-        tt(half("dg", n), bank(VB[n]), T.dpos[:], A.min, r=[ps(VB[n]), "dpos"], w=["dg" + n])
+    def scores(n, a):
+        return (VB if a else EB)[n]
 
-    def carry(n):
-        do("v", lambda: V.tensor_tensor_scan(half("sc", n), T.rstn[:], half("dg", n), 0.0, A.min, A.max), r=["rstn", "dg" + n], w=["sc" + n])
+    def span(a):
+        return (a, a + H) if SPLIT_P else (0, NC)
+
+    def own_column(n, a):
+        k, (x, y) = scores(n, a), span(a)
+        tt(half("dg", n, x, y), bank(k, x, y), T.dpos[:, 0:y - x], A.min, r=[ps(k), "dpos"], w=[hk("dg" + n, a)])
+
+    def carry(n, a):
+        x, y = span(a)
+        do("v", lambda: V.tensor_tensor_scan(half("sc", n, x, y), T.rstn[:, 0:y - x], half("dg", n, x, y), 0.0, A.min, A.max),
+           r=["rstn", hk("dg" + n, a)], w=[hk("sc" + n, a)])
 
     def part(n, m):
         o, e = 4 * TILE[(NM - m) // 4][0], (NM - m) % 4
@@ -361,30 +424,34 @@ def rank_program(g, core, T, topo):
     def score(n, m):
         return half("sc", n, 16 * m + 15, 16 * m + 16)
 
-    def inside(n):
-        tt(part(n, NM), bank(VB[n]), half("sc", n), A.is_le, r=[ps(VB[n]), "sc" + n, zeros(n, NM)], w=["mt%s%d" % (n, NM)])
+    def inside(n, a):
+        k, (x, y) = scores(n, a), span(a)
+        tt(T["mt" + n][:, 4 * x:4 * y:4], bank(k, x, y), half("sc", n, x, y), A.is_le,
+           r=[ps(k), hk("sc" + n, a)] + ([zeros(n, NM)] if a else []), p=["mt%s%d" % (n, NM)])
 
-    def inside_sums(n):
-        scan(half("dd", n), part(n, NM), r=["rst", "mt%s%d" % (n, NM)], w=["dd" + n])
+    def inside_sums():
+        scan(T.dd[:], part("B", NM), r=["rst", "mtB%d" % NM], w=["dd"])
 
-    def compare(n, ms):
+    def compare(n, ms, a):
+        k = scores(n, a)
         for m in ms:
-            ts(part(n, m), bank(VB[n], 0, 16 * m), score(n, m), None, A.is_lt, r=[ps(VB[n]), "sc" + n, zeros(n, m)], w=["mt%s%d" % (n, m)])
+            ts(part(n, m), bank(k, 0, 16 * m), score(n, m), None, A.is_lt, r=[ps(k), hk("sc" + n, a), zeros(n, m)], w=["mt%s%d" % (n, m)])
 
-    def scalar_compare(n):
+    def scalar_compare(rows, a):
         late = None
-        for m in BY_SCALAR + (None,):
-            if m is not None:
+        for n, m in [(n, m) for n in rows for m in BY_SCALAR if (16 * m >= H) == (a > 0) or not SPLIT_P] + [(None, None)]:
+            if m:
+                k = (SB if a else CB)[n]
                 j, jk = junk(16 * m)
-                do("s", lambda: S.activation(j, bank(SB[n], 0, 16 * m), F.Sign, bias=score(n, m), scale=-1.0), r=[ps(SB[n]), "sc" + n], w=[jk])
+                do("s", lambda: S.activation(j, bank(k, 0, 16 * m), F.Sign, bias=score(n, m), scale=-1.0), r=[ps(k), hk("sc" + n, a)], w=[jk])
             if late:
-                q, i, ik = late
-                do("s", lambda: S.activation(part(n, q), i, F.Relu, accum_out=T["acc" + n][:, q:q + 1]),
-                   r=[ik, zeros(n, q)], w=["mt%s%d" % (n, q)], p=["acc" + n])
-            late = (m, j, jk)
+                o, q, i, ik = late
+                do("s", lambda: S.activation(part(o, q), i, F.Relu, accum_out=T["acc" + o][:, q:q + 1]),
+                   r=[ik, zeros(o, q)], w=["mt%s%d" % (o, q)], p=["acc9" + o if q == 9 else "acc" + o])
+            late = m and (n, m, j, jk)
 
-    def add_up(n):
-        for m in BY_VECTOR:
+    def add_up(n, ms):
+        for m in [m for m in ms if m > 8]:
             ssum(part(n, m), 16 * m, T["acc" + n][:, m:m + 1], "acc" + n, ["mt%s%d" % (n, m)])
 
     def column_sums(t, n, us):
@@ -395,12 +462,25 @@ def rank_program(g, core, T, topo):
         for u in us:
             mm(CB[n], TILE[u][1], "kq", KO if n == "A" else KF, "mq", c + TILE[u][0] - o, u == 0, u == 1, key)
 
+    def short_sums(n):
+        o, d = 4 * TILE[3][0], 4 * SHORT if n == "B" else 0
+        for e in range(4):
+            a = d + SHORT * (3 - e)
+            do("v", lambda: V.tensor_tensor_scan(T.ds[:, a:a + SHORT], T.rs2[:], T["mt" + n][:, o + e:o + 4 * SHORT:4], 0.0, A.mult, A.add),
+               r=["rs2"] + ["mt%s%d" % (n, m - e) for m in (8, 4)] + ["mz%s%d" % (n, u) for u in (3, 4)], p=["ds" + n])
+
     def row_part(n, k):
-        ow = T["ow" + n]
+        ow, d = T["ow" + n], 4 * SHORT if n == "B" else 0
+        old, key = (ow, "owB") if n == "B" else (T.ramp, "ramp")
         if k == 0:
-            tt(ow[:], T.ramp[:], half("dd", n, 15, NC, 16), A.subtract, r=["ramp", "dd" + n], w=["ow" + n])
+            tt(ow[:], T.ramp[:], T.dd[:, 15:NC:16], A.subtract, r=["ramp", "dd"], w=["owB", "ow1B", "ow5B", "ow9B", "ow10B"])
+        elif k == 1:
+            for m, end in ((5, 127), (1, 191)):
+                tt(ow[:, m:m + 4], old[:, m:m + 4], T.ds[:, d + end:d + 4 * SHORT:SHORT], A.subtract, r=["ds" + n, key], w=["ow%d%s" % (m, n)])
+        elif k == 2:
+            tt(ow[:, 9:10], old[:, 9:10], T["acc" + n][:, 9:10], A.subtract, r=["acc9" + n, key], w=["ow9" + n])
         else:
-            tt(ow[:], ow[:], T["acc" + n][:], A.subtract, r=["acc" + n, "acc0" + n], w=["ow" + n])
+            tt(ow[:, 10:NM], old[:, 10:NM], T["acc" + n][:, 10:NM], A.subtract, r=["acc" + n, key], w=["ow10" + n])
 
     def table(h):
         mm(h % 4, NC, "kq", KW + 128 * h, "cq", 0)
@@ -431,53 +511,76 @@ def rank_program(g, core, T, topo):
         mm(4 + b % 2, NC, "kq", KE + 128 * b, PX, 0)
 
     def places(t, PX):
-        for n, a in (("A", 0), ("B", 128)):
-            mm(VB[n], NC, "up", a, PX, 0)
-        for n, a in (("A", 0), ("B", 128)):
-            mm(SB[n], NC, "up", a, PX, 0)
-        own_column("A")
-        own_column("B")
-        carry("A")
-        carry("B")
-        scalar_compare("A")
-        compare("A", BY_VECTOR)
-        add_up("A")
-        inside("A")
-        inside("B")
-        scalar_compare("B")
-        compare("B", BY_VECTOR)
-        add_up("B")
-        column_sums(t, "A", (0,))
-        column_sums(t, "A", (2, 3, 4))
-        column_sums(t, "A", (1,))
-        inside_sums("A")
-        inside_sums("B")
-        row_part("A", 0)
+        UP = {"A": 0, "B": 128}
+        for banks in (EB, CB) if SPLIT_P else ():
+            for n in "BA":
+                mm(banks[n], H, "up", UP[n], PX, 0, key=hk(PX, 0))
+        for banks in (VB, SB):
+            for n in ORDER:
+                mm(banks[n], NC, "up", UP[n], PX, 0)
+        for a in HALVES if SPLIT_P else (H,):
+            for step in (own_column, carry):
+                for n in ORDER if a else "BA":
+                    step(n, a)
+            if a == 0:
+                scalar_compare("BA", 0)
+                for n in "BA":
+                    inside(n, 0)
+        scalar_compare(ORDER, H)
+        for n in "BA":
+            compare(n, EARLY, 0 if SPLIT_P else H)
+        for n in "BA":
+            inside(n, H)
+            compare(n, LATE, H)
+            add_up(n, LATE + EARLY)
         if t == 0:
-            vcopy(T.bg[:, 448:512], T.bd[:, 0:64], r=["bd", "bgz"], w=["bg"])
-            ts(T.eb[:, 3:515:4], T.triv[:], 0.0, None, A.is_equal, r=["triv", "ebz"], w=["eb"])
-        column_sums(t, "B", (0,))
-        tt(T.rkd[:], bank(CB["A"]), T.diag[:], A.mult, r=[ps(CB["A"]), "diag"], w=["rkd"])
-        column_sums(t, "B", (2, 3, 4))
-        scan(T.cs[:], T.rkd[:], r=["rst", "rkd"], w=["cs"])
-        row_part("A", 1)
+            adding_up_by_group()
+        inside_sums()
+        short_sums("B")
         row_part("B", 0)
-        column_sums(t, "B", (1,))
-        tt(T.plA[:], T.owA[:], T.cs[:, 15:NC:16], A.add, r=["owA", "cs"], w=["plA"])
-        vcopy(T.aoff[:], T.plA[:], r=["plA"], w=["aoff"])
-        row_part("B", 1)
-        ts(T.d0[:, 0:3], T.a0[:, 0:3], -1.0, 159.0, A.mult, A.add, r=["a0"], w=["d0"])
-        tt(T.bx[:], T.owB[:, 0:NM].indirect(T.lm[:, 0:NM]), T.diag[:], A.mult, r=["owB", "lm", "diag"], w=["bx"])
+        short_sums("A")
+        if t == 0:
+            constants(KO, 128, "go", 0, ["go"])
+        first_turns()
+        for n in "AB":
+            row_part(n, 1)
+            row_part(n, 2)
+            column_sums(t, n, (0,))
+            column_sums(t, n, (2, 3, 4))
+            if n == "B":
+                tt(T.rkd[:], bank(CB["A"]), T.diag[:], A.mult, r=[ps(CB["A"]), "diag"], w=["rkd"])
+            column_sums(t, n, (1,))
+        do("v", lambda: V.tensor_tensor_scan(T.cs[:, 16:16 + NC], T.rkd[:], part("A", NM), 0.0, A.add, A.subtract), r=["rkd", "mtA%d" % NM], w=["cs"])
+
+        def row_of_b(a):
+            tt(T.bx[:, a:a + H], T.owB[:, 0:10 + a // 16].indirect(T.lm[:, a // 16:a // 16 + 10]), T.diag[:, 0:H], A.mult,
+               r=["owB", "ow1B", "ow5B", "ow9B", "lm", "diag"] + (["ow10B"] if a else []), w=[hk("bx", a)])
+
+        def whole_b(a):
+            tt(T.bt[:, a:a + H], bank(CB["B"], a, a + H), T.bx[:, a:a + H], A.add, r=[ps(CB["B"]), hk("bx", a)], w=[hk("bt", a)])
+
+        row_of_b(0)
+        tt(T.df[:], T.cs[:, 31:NC + 16:16], T.cs[:, 15:NC:16], A.subtract, r=["cs", "csz"], w=["df"])
+        whole_b(0)
+        tt(T.plA[:], T.owA[:], T.df[:], A.add, r=["ow0A", "ow1A", "ow5A", "ow9A", "df"], w=["plA", "pl10"])
+        row_part("B", 3)
+        vcopy(T.aoff[:, 0:10], T.plA[:, 0:10], r=["plA"], w=["aoff0"])
+        row_of_b(H)
         for c in range(3):
             a, b, ma, mb = block_of(c)
-            ts(slots(a, b), T.mask8[:, ma:mb], T.d0[:, c:c + 1], None, A.mult, r=["mask8", "d0", "xnz"], p=["xn"])
-        tt(T.bt[:], bank(CB["B"]), T.bx[:], A.add, r=[ps(CB["B"]), "bx"], w=["bt"])
+            scopy(slots(a, b), T.mask8[:, ma:mb], T.d0[:, c:c + 1], r=["mask8", "d0", "xnz"], p=["xn"])
         if t == 0:
-            constants(KG, 240, "bg", 0, ["bg"])
-        digits()
+            for h in range(1, NG):
+                row_to_all(h)
+        vcopy(T.cx[:, 0:NC].indirect(T.aoff[:, 0:10]), T.bt[:, 0:H], r=["aoff0", hk("bt", 0)], w=["cx"])
+        tt(T.plA[:, 10:NM], T.plA[:, 10:NM], T.accA[:, 10:NM], A.subtract, r=["accA"], w=["pl10"])
+        whole_b(H)
+        vcopy(T.aoff[:, 10:NM], T.plA[:, 10:NM], r=["pl10"], w=["aoff"])
         ts(T.offo[:, 0:3], T.d0[:, 0:3], 160.0, None, A.add, r=["d0"], w=["offo"])
-        vcopy(T.cx[:, 0:NC].indirect(T.aoff[:, 0:NM]), T.bt[:], r=["aoff", "bt"], w=["cx"])
+        digits()
+        vcopy(T.cx[:, 0:NC].indirect(T.aoff[:, 10:NM]), T.bt[:, H:NC], r=["aoff", hk("bt", H)], w=["cx"])
         spread(0)
+
         for a in HALVES:
             ts(T.ct[:, 4 * a:4 * (a + H):4], T.cx[:, a:a + H], MG32, MG32, A.add, A.subtract, r=["cx"], w=["cthi%d" % a])
         for a in HALVES:
@@ -486,8 +589,8 @@ def rank_program(g, core, T, topo):
             quant("cq", a, a + H, "ct", 4 * a, ["cthi%d" % a, "ctlo%d" % a, "ct2", "ct3"], hk("cq", a))
         take_offsets()
         if t == 0:
-            for b in range(4):
-                quantise_unpacking(b)
+            quantise_row_to_all(1)
+            vcopy(T.bg[:, 448:512], T.bd[:, 0:64], r=["bd", "bgz"], w=["bg"])
 
     def draft(t, PX):
         last = t == 1
@@ -504,60 +607,80 @@ def rank_program(g, core, T, topo):
         own_totals_picked()
         prev = look_up(0, "tier", H, NC)
         own_totals_added("tiec")
+        small = [lambda k=k: list_of_turned_rows(k) for k in range(5)] if t == 0 else []
         for h in range(1, NG):
             own = h < NG - 1
             if own:
                 table(h + 1)
-            if h < 3:
-                unpack(2 * h - 2, PX)
-                unpack(2 * h - 1, PX)
-            ns = 3 if h < 3 else 2
+            if h in (3, 4):
+                unpack(2 * h - 6, PX)
+                unpack(2 * h - 5, PX)
+            ns = 3 if h == 1 else 2
             for c in range(ns):
                 count_teams(prev, c)
-            for c in range(ns):
-                a, b, ma, mb = block_of(c)
-                scopy(slots(a, b), T.mask8n[:, ma:mb], T.cnt[:, c:c + 1], r=["mask8n", "cnt%d" % c], p=["xn"])
             if h == 1:
-                vcopy(T.ir[:, 0:NC].indirect(T.aoff[:, 0:NM]), T.iot[:], r=["aoff", "iot"], w=["ir"])
-            elif h == 2:
-                tt(T.di[:], T.ir[:], T.diag[:], A.mult, r=["ir", "diag"], w=["di"])
-                scan(T.si[:], T.di[:], r=["rst", "di"], w=["si"])
-                vcopy(T.inva[:], T.si[:, 15:NC:16], r=["si"], w=["inva"])
+                vcopy(T.ir[:, 16:16 + NC].indirect(T.aoff[:, 0:NM]), T.iom[:], r=["aoff0", "aoff", "iom"], w=["ir"])
             else:
                 ts(T.cb[:], T[prev][:], T.pk[:, 2:3], None, A.is_gt, r=[prev, "pk"], w=["cb"])
+                if h == 2:
+                    do("v", lambda: V.transpose(T.it[:, NC:2 * NC + 32], T.ir[:, 0:NC + 32]), r=["ir", "irz0", "irz"], p=["it"])
+                elif h == 3 and t == 0:
+                    quantise_unpacking(2)
                 do("v", lambda: V.tensor_tensor_scan(T.cbs[:], T.ones[:, 0:NC], T.cb[:], -160.0, A.mult, A.add), r=["cb", "ones"], w=["cbs"])
+                if h < 4 and t == 0:
+                    quantise_unpacking(3 * h - 6)
                 a, b, ma, mb = block_of(2)
                 ts(slots(a, b), T.mask8[:, ma:mb], T.cbs[:, NC - 1:NC], None, A.mult, r=["mask8", "cbs"], p=["xn"])
+                if h == 2 and t == 0:
+                    quantise_unpacking(1)
+            for c in range(ns):
+                a, b, ma, mb = block_of(c)
+                if c < 2 < ns:
+                    ts(slots(a, b), T.mask8n[:, ma:mb], T.cnt[:, c:c + 1], None, A.mult, r=["mask8n", "cnt%d" % c], p=["xn"])
+                else:
+                    scopy(slots(a, b), T.mask8n[:, ma:mb], T.cnt[:, c:c + 1], r=["mask8n", "cnt%d" % c], p=["xn"])
+            if t == 0 and h == 1:
+                small.pop(0)()
+                constants(KG, 240, "bg", 0, ["bg"])
+                small.pop(0)()
+                ts(T.eb[:, 3:515:4], T.triv[:], 0.0, None, A.is_equal, r=["triv", "ebz"], w=["eb"])
             digits()
-            if own:
+            if own or last:
                 ts(T.offo[:, 0:ns], T.cnt[:, 0:ns], -0.5, 160.0, A.mult, A.add, r=["cnt%d" % c for c in range(ns)], w=["offo"])
                 if ns == 2:
                     ts(T.offo[:, 2:3], T.cbs[:, NC - 1:NC], 160.0, None, A.add, r=["cbs"], w=["offo2"])
-            spread(h, own or last)
+                elif small:
+                    small.pop(0)()
+            spread(h, own)
             if own:
                 own_totals(h)
+                if h == 1:
+                    do("v", lambda: V.transpose(T.it[:, 0:NC], T.ir[:, 16:16 + NC]), r=["ir"], p=["it"])
+                elif h == 2:
+                    ts(T.inva[:], T.it[:, 0:2 * NC + 32].indirect(T.lt[:, 0:2]), 160.0, None, A.add, r=["it", "lt"], w=["inva"])
                 own_totals_picked()
                 take_offsets()
                 own_totals_added("pk")
+                if small:
+                    small.pop(0)()
                 prev = look_up(h, prev)
+                if small:
+                    small.pop(0)()
             if t == 0 and h + 2 < NG:
-                row_to_all(h + 2)
                 quantise_row_to_all(h + 2)
             if own:
                 copy_table(h + 1)
-            if h < 3:
-                for b in (2 * h - 2, 2 * h - 1):
+            if h in (3, 4):
+                for b in (2 * h - 6, 2 * h - 5):
                     scopy(plane("fp", b), bank(4 + b % 2), r=[ps(4 + b % 2)], w=["fp%d" % b])
-            elif own:
-                scopy(plane("fs", h - 3), plane("fp", h - 3).indirect(T.inva[:, 0:NM]), r=["fp%d" % (h - 3), "inva"], w=["fs%d" % (h - 3)])
+            if h >= 4:
+                scopy(plane("fs", h - 4), plane("fp", h - 4).indirect(T.inva[:, 0:NM]), r=["fp%d" % (h - 4), "inva"], w=["fs%d" % (h - 4)])
         return prev
 
     def layer(t, prev):
         X, PY, YQ = "xq%d" % t, "py%d" % t, "yq%d" % t
         last = t == 1
         ts(T.noff[:], bank(7, 0, NM), 160.0, None, A.add, r=[ps(7)], w=["noff"])
-        if last:
-            take_offsets()
         for k in range(4):
             cp = scopy if k else vcopy
             cp(T.zt[:, k:4 * NC:4], plane("fs", k).indirect(T.noff[:, 0:NM]), r=["fs%d" % k, "noff"], p=["zt"])
@@ -567,7 +690,7 @@ def rank_program(g, core, T, topo):
             mm(b, NC, "ww", 128 * b, "zq", 0)
             if b >= 4:
                 scopy(plane("cc", b - 4), bank(b), r=[ps(b)], w=["cc%d" % (b - 4)])
-        tt(T.rkd[:], T.sr[:, 0:NC].indirect(T.aoff[:, 0:NM]), T.diag[:], A.mult, r=["sr", "aoff", "diag"], w=["rkd"])
+        tt(T.rkd[:], T.sr[:, 0:NC].indirect(T.aoff[:, 0:NM]), T.diag[:], A.mult, r=["sr", "aoff0", "aoff", "diag"], w=["rkd"])
         scan(T.rks[:], T.rkd[:], r=["rst", "rkd"], w=["rks"])
         for b in range(4):
             tt(plane("yp", b), bank(b), plane("cc", b), A.max, r=[ps(b), "cc%d" % b], w=["yp%d" % b])
@@ -586,10 +709,14 @@ def rank_program(g, core, T, topo):
         if not SPLIT_Y:
             send_tile(t, PY, YQ, HALVES)
         if last:
-            prev = look_up(NG - 1, prev)
-            tt(T.tsb[0:1, :], T[prev][0:1, :], T.tier[0:1, :], A.subtract, r=[prev, "tier"], w=["tsb"])
-            ts(T.tsb[0:1, :], T.tsb[0:1, :], 1.0 / 512, None, A.mult, w=["tsb"])
-            dma("sy", T.tot[:, :], T.tsb[0:1, :], r=["tsb"])
+            own_totals(NG - 1)
+            own_totals_picked()
+            own_totals_added("pk")
+            tt(T.tsb[:, 0:3], T.pk[:, 0:3], T.tiec[:, 0:3], A.subtract, r=["pk", "tiec"], w=["tsb"])
+            scopy(T.tsb[:, 4:7], T.tsb[:, 0:3], 1.0 / 512, r=["tsb"], w=["tot"])
+            for c in range(3):
+                a = 128 * c - PIECE[c]
+                dma("sy", T.tot[:, 128 * c:128 * c + 128 - a], T.tsb[a:128, 4 + c:5 + c], r=["tot"] + both(PY))
         else:
             quant("vq", 0, 128, "vt", 0, ["vt"])
         NX = "xq%d" % (t + 1)
@@ -634,10 +761,11 @@ def rank_program(g, core, T, topo):
             between_halves_of_x()
     if not SPLIT_0:
         send_tile(0, "px0", "xq0", HALVES)
-    behind_the_first_writes()
+    while_u_comes()
     quant("uq", 0, 128, "ut", 0, ["ut"])
     do("v", lambda: V.tensor_copy(T.upc[:, 0:384].bitcast(dt.uint32), T.uqc[:, 0:128].bitcast(dt.uint32).indirect(T.lu[:, 0:24])), r=["uq", "lu"], p=["up"])
     do("s", lambda: S.activation(T.ups[:, 0:384], T.uqs[:, 0:128].indirect(T.lu[:, 0:24]), F.Copy), r=["uq", "lu"], p=["up"])
+    behind_the_first_writes()
     dma("sy", codes("ww", 0, 1024), T.wc[:, :], r=both("px0"), p=["ww"])
     dma("sy", T.wws[:, :], T.ws[:, :], p=["ww"])
     dma("sy", T.vt[:, :], T.v[:, :], w=["vt"])
@@ -647,8 +775,9 @@ def rank_program(g, core, T, topo):
         if t == 0:
             while_own_scores_come()
         own_places()
+        own_sums()
         if t == 0:
-            while_codes_come()
+            unfilled("A", FILL_V, "v")
         places(t, PX)
         layer(t, draft(t, PX))
     for k in range(4):

@@ -1,4 +1,4 @@
-from concourse.mybir import dt, AluOpType as A, AxisListType, ActivationFunctionType as F
+from concourse.mybir import dt, AluOpType as A, ActivationFunctionType as F
 
 NC = 320
 NG = 8
@@ -10,6 +10,16 @@ ORDER = "AB"
 BY_SCALAR = (19, 18, 17, 16, 15, 9)
 BY_VECTOR = tuple(m for m in range(NM - 1, 0, -1) if m not in BY_SCALAR)
 PIECE = (0, 128, 192)
+M = NC + 1
+NBUF = 6
+BESIDE = ({(1, 2): "r8 r9", (2, 0): "e", (2, 2): "r10 r11 p0", (3, 0): "u0", (3, 1): "u1", (3, 2): "r12 r13 p1", (4, 0): "u2", (4, 1): "u3",
+           (4, 2): "r14 r15 t0 t1", (5, 0): "l", (5, 2): "r16"},
+          {(1, 2): "p0", (2, 2): "p1", (3, 2): "t0 t1", (4, 0): "l"})
+UNPACK = (4, 5)
+SORT = ({6: (0, 1), 7: (2, 3)}, {4: (0,), 5: (1,), 6: (2,), 7: (3,)})
+ZS = (20, 0, 0, 10)
+YS = (2, 3)
+EARLY_ROWS = 0
 
 F32, BF, I32, U16, FP8, U8 = "float32", "bfloat16", "int32", "uint16", "float8_e4m3fn_x4", "uint8"
 SCRATCH = {"ps": ("psum", [128, 4096], F32)}
@@ -24,36 +34,35 @@ def _mx(name, cols):
     _sb(name + "s", cols, U8)
 
 
-for _n, _c in (("tab0", NC), ("tier", NC), ("iot", NC), ("hcol", 1), ("pif", 1), ("ramp", NM),
-               ("mask8", 8), ("mask8n", 8), ("maskw", 8), ("h8", 8), ("tiec", 4), ("triv", 128), ("lf", 48),
-               ("a0", 12), ("d0", 4), ("r1", NC), ("dg", 2 * NC), ("sc", 2 * NC), ("cs", NC + 16),
-               ("accA", NM), ("accB", NM), ("owA", NM), ("owB", NM), ("plA", NM),
-               ("bx", NC), ("bt", NC), ("cx", NC), ("df", NM),
-               ("xn", 84), ("kr0", NC), ("kr1", NC), ("pk", 4), ("cnt", 4), ("ogd", 48), ("os1", 48),
-               ("sr", NC), ("rkd", NC), ("rks", NC), ("cc", 4 * NC), ("ysb", NC), ("tsb", 8), ("cw", NG * NC)):
+for _n, _c in (("tab0", NC), ("tier", NC), ("col", 12), ("ramp", NM), ("mask", 32), ("tiec", 8), ("triv", 128), ("lf", 56),
+               ("a0", 12), ("r1", NC), ("dg", 2 * NC), ("sc", 2 * NC), ("cs", NC + 16),
+               ("accA", NM), ("accB", NM), ("owA", NM), ("owB", NM), ("plA", 2 * NM),
+               ("bx", NC), ("bt", NC), ("cx", NC),
+               ("xn", 84), ("kr0", NC), ("pk", 8), ("cnt", 4), ("ogd", 48), ("os1", 48),
+               ("sr", NC), ("rkd", NC), ("kd", 2 * NC), ("cc", 4 * NC), ("ysb", NC), ("tsb", 12), ("cw", NG * NC)):
     _sb(_n, _c, F32)
 for _n, _c in (("ipr", NC), ("diag", NC), ("rst", NC), ("dpos", NC), ("rstn", NC), ("go", 512), ("go0", 512), ("xt0", 4 * NC), ("xt1", 4 * NC),
-               ("ut", 512), ("vt", 512), ("ones", 512), ("eb", 516), ("wg", 4096), ("bd", 512), ("bg", 960), ("tri", NC),
+               ("ut", 512), ("vt", 512), ("ones", 512), ("eb", 516), ("wg", NBUF * 512), ("rr", 512), ("bd", 512), ("bg", 960), ("tri", NC),
                ("tpos", NC), ("a0c", 3 * 448), ("dd", NC), ("rs2", SHORT), ("ds", 8 * SHORT), ("mtA", 4 * MT), ("mtB", 4 * MT),
-               ("junk", 16 * 448), ("cb", NC), ("cbs", NC), ("ct", 4 * NC), ("nt", 512), ("zt", 4 * NC), ("yt", 4 * NC),
-               ("fp", 4 * NC), ("fs", 4 * NC), ("yp", 4 * NC), ("iom", NC), ("ir", NC + 32), ("it", 2 * NC + 32)):
+               ("junk", 16 * 448), ("cb", 2 * NC), ("rk", 2 * NC), ("ct", 4 * NC), ("nt", 512), ("cd", 4 * NC), ("gt", 4 * NC), ("gu", 4 * NC), ("zt", 4 * NC),
+               ("yt", 4 * NC), ("fp", 4 * NC), ("fs", 4 * NC), ("yp", 4 * NC), ("iom", NC), ("ir", NC + 32), ("it", 2 * NC + 32)):
     _sb(_n, _c, BF)
-_sb("pi_i", 4, I32)
-for _n, _c in (("lm", NM), ("lu", 24), ("aoff", NM), ("inva", 32), ("lt", 2), ("off", NM), ("offo", 4), ("noff", NM), ("koff", NM)):
+_sb("pi_i", 8, I32)
+for _n, _c in (("lm", NM), ("lu", 24), ("aoff", NM), ("inva", 32), ("lt", 2), ("off", NM), ("offo", 4), ("offm", NM), ("noff", NM), ("koff", NM)):
     _sb(_n, _c, U16)
-KE, KW, KB, KG, KO, KF = 0, 512, 1536, 1664, 1904, 2032
+KE, KW, KB, KG, KO, KF, K0, KM, KD = 0, 512, 1536, 1664, 1904, 2032, 2160, 2288, 2416
 for _n, _c in (("xq0", NC), ("xq1", NC), ("xq2", NC), ("px0", NC), ("px1", NC), ("py0", NC), ("py1", NC), ("uq", 128), ("up", 384), ("vq", 128),
-               ("kq", 2160), ("mq", 2 * MT), ("nq", 256), ("cq", NC), ("zq", NC), ("yq0", NC), ("yq1", NC), ("ww", 1024)):
+               ("kq", KD + 7 * 128), ("mq", 2 * MT), ("nq", 256), ("cq", NC), ("gq", NC), ("g0", NC), ("zq", NC), ("yq0", NC), ("yq1", NC), ("ww", 1024)):
     _mx(_n, _c)
 
 SEMAPHORES = ["v", "s", "t", "gp", "ls"] + ["d%d" % k for k in range(20)] + ["rx%d" % k for k in range(16)]
 H = NC // 2
 HALVES = (0, H)
-SPLIT_0, SPLIT_X, SPLIT_Y = True, True, True
-SPLIT_P, REDUCE_V, FILL_V = True, False, ()
 
-MG16 = 1.5 * 2.0 ** 27
-MG32 = 1.5 * 2.0 ** 28
+MG1 = 1.5 * 2.0 ** 23
+MG16 = 16 * MG1
+MG32 = 32 * MG1
+LIFT = 2.0 ** 21
 FAR = 1e29
 
 
@@ -145,11 +154,10 @@ def rank_program(g, core, T, topo):
     def both(name):
         return [hk(name, a) for a in HALVES]
 
-    def send_tile(t, land, name, halves):
-        a, b, r = halves[0], halves[-1] + H, [hk(name, a) for a in halves]
-        came = [send(partner(t), codes(land, a, b), codes(name, a, b), r), send(partner(t), T[land + "s"][:, a:b], T[name + "s"][:, a:b], r)]
-        for a in halves:
-            st(hk(land, a))["w"] = came
+    def send_half(t, land, name, a):
+        r = [hk(name, a)]
+        st(hk(land, a))["w"] = [send(partner(t), codes(land, a, a + H), codes(name, a, a + H), r),
+                                send(partner(t), T[land + "s"][:, a:a + H], T[name + "s"][:, a:a + H], r)]
 
     def partner(t):
         return T.cores[rank ^ (1 << t)]
@@ -170,13 +178,16 @@ def rank_program(g, core, T, topo):
         o = NC if n == "B" else 0
         return T[name][:, o + a:o + b:step]
 
+    def col(k):
+        return T.col[:, k:k + 1]
+
     def junk(n):
         k = tally["junk"] % 16
         tally["junk"] += 1
         return T.junk[:, 448 * k:448 * k + n], "junk%d" % k
 
     def quant(name, a, b, tile, ta, r, key=None):
-        kw = {"w": [key]} if key else {"p": [name]}
+        kw = {"w": key if isinstance(key, list) else [key]} if key else {"p": [name]}
         do("v", lambda: V.quantize_mx(T[name + "c"][:, a:b], T[name + "s"][:, a:b], T[tile][:, ta:ta + 4 * (b - a)]), r=r, **kw)
 
     def constants(a, n, tile, ta, r):
@@ -185,7 +196,7 @@ def rank_program(g, core, T, topo):
     def mm(k, n, left, la, right, ra, start=True, stop=True, key=None, lkey=None):
         kw = {"w": [ps(k)]} if start else {"p": [ps(k)]}
         lkey = lkey or ("kq%d" % la if left == "kq" else left)
-        r = [x for side in (lkey, key or right) for x in (both(side) if side[:2] in ("xq", "px", "cq") and "@" not in side else [side])]
+        r = [x for side in (lkey, key or right) for x in (both(side) if side[:2] in ("xq", "px", "cq", "gq", "zq") and "@" not in side else [side])]
         do("t", lambda: PE.matmul_mx(bank(k, 0, n), T[left + "c"][:, la:la + 128], T[left + "s"][:, la:la + 128],
                                      T[right + "c"][:, ra:ra + n], T[right + "s"][:, ra:ra + n], start, stop), r=r, **kw)
 
@@ -207,15 +218,18 @@ def rank_program(g, core, T, topo):
     def sline(out, in_, scale, bias, **k):
         do("s", lambda: S.activation(out, in_, F.Identity, bias=bias, scale=scale), **k)
 
-    def ssum(in_, n, col, key, r):
+    def ssum(in_, n, acc, key, r):
         j, jk = junk(n)
-        do("s", lambda: S.activation(j, in_, F.Copy, accum_out=col), r=r, w=[jk], p=[key])
+        do("s", lambda: S.activation(j, in_, F.Copy, accum_out=acc), r=r, w=[jk], p=[key])
+
+    def run(out, d0, d1, first, op0, op1, **k):
+        do("v", lambda: V.tensor_tensor_scan(out, d0, d1, first, op0, op1), **k)
 
     def scan(out, d1, n=NC, **k):
-        do("v", lambda: V.tensor_tensor_scan(out, T.rst[:, 0:n], d1, 0.0, A.mult, A.add), **k)
+        run(out, T.rst[:, 0:n], d1, 0.0, A.mult, A.add, **k)
 
-    def fill(ap, c, key):
-        do("v", lambda: V.memset(ap, c), w=[key])
+    def fill(ap, c, key, r=()):
+        do("v", lambda: V.memset(ap, c), r=r, w=[key])
 
     def iota(name, a, b, pattern, base, cm, key=None):
         ap = T[name][:, a:b]
@@ -232,93 +246,127 @@ def rank_program(g, core, T, topo):
             a, b, key = 4 * TILE[u][0] + 64 * (17 - 4 * u), 4 * sum(TILE[u]), "mz%s%d" % (n, u)
             if eng == "s":
                 scopy(T["mt" + n][:, a:b], T.ones[:, 0:b - a], 0.0, r=["ones"], w=[key])
-            elif eng == "v":
-                fill(T["mt" + n][:, a:b], 0.0, key)
             else:
                 clear("mt" + n, a, b, key)
 
-    def row_to_all(h):
-        scopy(T.wg[:, 512 * h:512 * h + 512], T.ones[:], T.maskw[:, h:h + 1], r=["ones", "maskw"], w=["wg%d" % h])
+    PG, PI, FIRST, REST, RA, RB, W0 = range(7)
+    PLAIN, W320, WK0, WKM, HALF, OWN = 0, 8, 9, 10, 16, 24
+    ROWS = [(KW, "ones", 0), (KD, "ones", W320), (KW + 128, "ones", 1), (KD + 128, "rr", 1), (KW + 256, "ones", 2), (KD + 256, "rr", 2),
+            (K0, "ones", WK0), (KM, "ones", WKM)]
+    for h in range(3, NG):
+        ROWS += [(KW + 128 * h, "ones", h)] + ([(KD + 128 * h, "rr", h)] if h < NG - 1 else [])
 
-    def quantise_row_to_all(h):
-        constants(KW + 128 * h, 128, "wg", 512 * h, ["wg%d" % h])
+    def row(*ks):
+        for k in ks:
+            if k < len(ROWS):
+                o, (_, name, c), step = 512 * (k % NBUF), ROWS[k], 1 if k < NBUF or ROWS[k][0] == KM else 2
+                scopy(T.wg[:, o:o + 512:step], T[name][:, 0:512:step], T.mask[:, c:c + 1],
+                      r=[name, "mask8", "maskw"] + (["maskk"] if k > 1 else []), w=["wg%d" % (k % NBUF)])
 
-    def quantise_unpacking(b):
-        constants(KE + 128 * b, 128, "eb", 3 - b, ["eb", "ebz"])
+    def quantise_row(*ks):
+        for k in ks:
+            if k < len(ROWS):
+                constants(ROWS[k][0], 128, "wg", 512 * (k % NBUF), ["wg%d" % (k % NBUF)])
+
+    def quantise_unpacking(*bs):
+        for b in bs:
+            constants(KE + 128 * b, 128, "eb", 3 - b, ["eb", "ebz"])
 
     def while_x_comes():
-        iota("lf", 0, 16, [[1, 2], [16, 8]], 0, 0, "lf0")
         iota("pi_i", 0, 1, [[0, 1]], 0, 1)
-        iota("h8", 0, 8, [[1, 8]], 0, 0)
+        iota("lf", 48, 56, [[1, 8]], 0, 0, "h8")
         iota("triv", 0, 128, [[1, 128]], 0, -1)
         iota("ipr", 0, NC, [[0, NM], [1, 16]], 0, 0)
+        iota("lf", 0, 16, [[1, 2], [16, 8]], 0, 0, "lf0")
         iota("lf", 24, 44, [[16, NM]], 15, 0, "lf1")
-        iota("tiec", 0, 2, [[-128, 2]], 511, -1, "tiec0")
-        iota("tiec", 2, 3, [[0, 1]], 511 - PIECE[2], -1, "tiec1")
+        iota("tiec", 0, 2, [[128, 2]], 1 - M, 1, "tiec0")
+        iota("tiec", 2, 3, [[0, 1]], 1 - M + PIECE[2], 1, "tiec1")
         fill(T.ones[:], 1.0, "ones")
-        fill(T.bd[:], 0.0, "bdz")
         ts(T.pi_i[:, 1:2], T.pi_i[:, 0:1], 15, None, A.bitwise_and, r=["pi_i"], w=["pi1"])
         ts(T.pi_i[:, 2:3], T.pi_i[:, 0:1], 4, None, A.arith_shift_right, r=["pi_i"], w=["pi2"])
         fill(T.go0[:], 0.0, "go0z")
-        vcopy(T.hcol[:], T.pi_i[:, 2:3], r=["pi2"], w=["hcol"])
-        vcopy(T.pif[:], T.pi_i[:, 1:2], r=["pi1"], w=["pif"])
-        vcopy(T.lu[:, 0:16], T.lf[:, 0:16], r=["lf0"], p=["lu"])
+        vcopy(col(PG), T.pi_i[:, 2:3], r=["pi2"], w=["hcol"])
+        vcopy(col(PI), T.pi_i[:, 1:2], r=["pi1"], w=["pif"])
         do("v", lambda: V.memset(T.lu[:, 16:24], 0), p=["lu"])
-        ts(T.mask8[:], T.h8[:], T.hcol[:, 0:1], None, A.is_equal, r=["h8", "hcol"], w=["mask8"])
-        ts(T.maskw[:], T.h8[:], T.hcol[:, 0:1], 512.0, A.is_equal, A.mult, r=["h8", "hcol"], w=["maskw"])
+        ts(T.mask[:, 0:8], T.lf[:, 48:56], col(PG), None, A.is_equal, r=["h8", "hcol"], w=["mask8"])
+        ts(T.mask[:, W320:W320 + 1], col(PG), 0.0, float(NC), A.is_equal, A.mult, r=["hcol"], w=["maskw"])
         for c in range(3):
             o = 128 * c - PIECE[c]
             ts(T.tri[:, 128 * c:128 * c + 128 - o], T.triv[:, o:128], 0.0, None, A.is_lt, r=["triv"], p=["tri"])
-        ts(T.diag[:], T.ipr[:], T.pif[:, 0:1], None, A.is_equal, r=["ipr", "pif"], w=["diag"])
-        ts(T.rst[:], T.ipr[:], 0.0, None, A.is_gt, r=["ipr"], w=["rst"])
+        ts(T.pi_i[:, 4:5], T.pi_i[:, 0:1], 31, None, A.bitwise_and, r=["pi_i"], w=["pi4"])
+        ts(T.pi_i[:, 5:6], T.pi_i[:, 0:1], 12, None, A.bitwise_and, r=["pi_i"], w=["pi5"])
+        ts(T.mask[:, OWN:OWN + 8], T.mask[:, 0:8], -2000.0, NC - 1.0, A.mult, A.add, r=["mask8"], w=["zm"])
+        ts(col(FIRST), col(PI), 0.0, None, A.is_equal, r=["pif"], p=["wk2"])
+        ts(col(REST), col(PI), 0.0, None, A.is_gt, r=["pif"], p=["wk2"])
+        for q in range(4):
+            do("v", lambda: V.memset(T.col[32 * q:32 * q + 32, RA:RA + 1], MG1 * 32 ** q), p=["mg0"])
+        ts(T.diag[:], T.ipr[:], col(PI), None, A.is_equal, r=["ipr", "pif"], w=["diag"])
         unfilled("B", range(5), "s")
         sline(T.tpos[:], T.tri[:], 2 * FAR, -FAR, r=["tri"], w=["tpos"])
-        sline(T.dpos[:], T.diag[:], 2 * FAR, -FAR, r=["diag"], w=["dpos"])
-        sline(T.rstn[:], T.rst[:], 2 * FAR, -FAR, r=["rst"], w=["rstn"])
-        row_to_all(0)
+        sline(T.rstn[:], T.ipr[:], 2 * FAR, -FAR, r=["ipr"], w=["rstn"])
 
-    def between_halves_of_x():
-        ts(T.bd[:, 1:512:4], T.ipr[:, 0:128], T.pif[:, 0:1], None, A.is_equal, r=["ipr", "pif", "bdz"], p=["bd"])
-        ts(T.bd[:, 2:512:4], T.ipr[:, 0:128], T.pif[:, 0:1], -1.0, A.is_equal, A.mult, r=["ipr", "pif", "bdz"], p=["bd"])
+    def while_u_comes():
+        vcopy(T.lu[:, 0:16], T.lf[:, 0:16], r=["lf0"], p=["lu"])
+        ts(T.mask[:, WK0:WK0 + 1], T.pi_i[:, 4:5], 0.0, None, A.is_equal, r=["pi4"], p=["maskk"])
+        ts(col(W0), T.pi_i[:, 5:6], 0.0, M - 1.0, A.is_equal, A.mult, r=["pi5"], w=["wk0"])
+        ts(col(RB), col(RA), 32.0, None, A.mult, r=["mg0"], w=["mg"])
+        ts(T.rst[:], T.ipr[:], 0.0, None, A.is_gt, r=["ipr"], w=["rst"])
+        sline(T.dpos[:], T.diag[:], 2 * FAR, -FAR, r=["diag"], w=["dpos"])
+
+    def before_u_is_picked():
         for e in range(4):
-            vcopy(T.go0[:, e:512:64], T.mask8[:], r=["mask8", "go0z"], p=["go0"])
+            vcopy(T.go0[:, e:512:64], T.mask[:, 0:8], r=["mask8", "go0z"], p=["go0"])
         fill(T.rs2[:], 1.0, "rs2")
 
     def behind_the_first_writes():
-        unfilled("A", [u for u in (0, 2, 1, 3, 4) if u not in FILL_V], "gp")
+        unfilled("A", (0, 2, 1, 3, 4), "gp")
         iota("go", 0, 512, [[1, 8], [0, 64]], 0, 0)
+        clear("bd", 0, 512, "bdz")
+        clear("rr", 0, 512, "rrz")
+        clear("nt", 4 * NM, 512, "ntz")
+        clear("ct", 1, 4 * NC, "ct1", 4)
+        clear("ct", 3, 4 * NC, "ct3", 4)
+        iota("tab0", 0, NC, [[-M, NC]], M * (NC - 1), 0)
+        iota("tier", 0, NC, [[-1, NC]], M - 1 + int(LIFT), 0)
+        clear("cd", 1, 4 * NC, "cdz", 2)
+        clear("gt", 0, 4 * NC, "gtz")
         clear("bg", 0, 960, "bgz")
         clear("eb", 0, 516, "ebz")
-        clear("nt", 4 * NM, 512, "ntz")
-        clear("ct", 2, 4 * NC, "ct2", 4)
-        clear("ct", 3, 4 * NC, "ct3", 4)
-        iota("tab0", 0, NC, [[-512, NC]], 512 * (NC - 1), 0)
-        iota("tier", 0, NC, [[-1, NC]], 511, 0)
         iota("iom", 0, NC, [[1, NC]], -160, 0)
         clear("ir", 0, 16, "irz0")
         clear("ir", NC + 16, NC + 32, "irz")
-        iota("iot", 0, NC, [[1, NC]], 0, 0)
+        clear("gu", 0, 4 * NC, "guz")
 
-    def while_u_comes():
-        ts(T.tiec[:, 0:3], T.tiec[:, 0:3], 0.5, None, A.add, r=["tiec0", "tiec1"], w=["tiec"])
+    def before_the_second_draft():
+        for name, es in (("gt", (1, 2, 3)), ("gu", (1,))):
+            for e in es:
+                do("gp", lambda: g.iota(T[name][:, e:4 * NC:4], [[0, NC]], 0, 0, allow_small_or_imprecise_dtypes=True), w=both(name))
+
+    def while_own_scores_come():
+        ts(T.tiec[:, 0:3], T.tiec[:, 0:3], -0.5, None, A.add, r=["tiec0", "tiec1"], w=["tiec"])
         ts(T.lm[:], T.lf[:, 24:44], -15.0, 0.0625, A.add, A.mult, r=["lf1"], w=["lm"])
-        ts(T.ramp[:], T.lf[:, 24:44], T.pif[:, 0:1], None, A.subtract, r=["lf1", "pif"], w=["ramp"])
+        ts(T.ramp[:], T.lf[:, 24:44], col(PI), None, A.subtract, r=["lf1", "pif"], w=["ramp"])
         fill(T.xn[:, 0:84:2], 0.0, "xnz")
         fill(T.xn[:, 1:84:2], MG16, "xnm")
         fill(T.rs2[:, 128:129], 0.0, "rs2")
-        fill(T.tiec[0:64, 2:3], 2.0 ** 22, "tiec")
+        fill(T.tiec[0:64, 2:3], -2.0 ** 22, "tiec")
         fill(T.a0c[:, 3 * 448 - 64:3 * 448], 1.0, "a0z")
-
-    def while_own_scores_come():
         constants(KF, 128, "go0", 0, ["go0"])
-        constants(KB, 128, "bd", 0, ["bd"])
-        quantise_row_to_all(0)
-        ts(T.mask8n[:], T.h8[:], T.hcol[:, 0:1], -0.5, A.is_equal, A.mult, r=["h8", "hcol"], w=["mask8n"])
+        ts(T.mask[:, WKM:WKM + 1], T.pi_i[:, 5:6], 4.0, col(W0), A.is_equal, A.add, r=["pi5", "wk0"], p=["maskk"])
+        row(*range(EARLY_ROWS))
+        ts(T.mask[:, HALF:HALF + 8], T.lf[:, 48:56], col(PG), 0.5, A.is_equal, A.mult, r=["h8", "hcol"], w=["mask8n"])
         vcopy(T.owA[:], T.ramp[:], r=["ramp"], w=["ow0A", "ow1A", "ow5A", "ow9A"])
         fill(T.cs[:, 15:16], 0.0, "csz")
+        ts(T.tiec[:, 4:7], T.tiec[:, 0:3], -LIFT, None, A.add, r=["tiec"], w=["tiecc"])
 
     def adding_up_by_group():
-        ts(T.go[:], T.go[:], T.hcol[:, 0:1], None, A.is_equal, r=["hcol"], w=["go"])
+        ts(T.go[:], T.go[:], col(PG), None, A.is_equal, r=["hcol"], w=["go"])
+
+    def late_patterns():
+        scopy(T.bd[:, 1:512:4], T.diag[:, 0:128], r=["diag", "bdz"], p=["bd"])
+        scopy(T.bd[:, 2:512:4], T.diag[:, 0:128], -1.0, r=["diag", "bdz"], p=["bd"])
+        for e, c in ((0, 1.0), (6, col(FIRST)), (10, col(REST))):
+            scopy(T.rr[:, e:512:16], T.ones[:, 0:32], c, r=["ones", "wk2", "rrz"], p=["rr"])
 
     def list_of_turned_rows(k):
         if k == 0:
@@ -328,7 +376,7 @@ def rank_program(g, core, T, topo):
         elif k == 2:
             ts(T.lf[:, 16:17], T.pi_i[:, 3:4], NC + 16.0, None, A.mult, r=["pi3"], w=["lf2"])
         elif k == 3:
-            ts(T.lt[:, 0:1], T.pif[:, 0:1], 16.0, T.lf[:, 16:17], A.mult, A.add, r=["pif", "lf2"], w=["lt0"])
+            ts(T.lt[:, 0:1], col(PI), 16.0, T.lf[:, 16:17], A.mult, A.add, r=["pif", "lf2"], w=["lt0"])
         else:
             ts(T.lt[:, 1:2], T.lt[:, 0:1], 256.0, 2.0 * NC, A.add, A.min, r=["lt0"], w=["lt"])
 
@@ -359,19 +407,13 @@ def rank_program(g, core, T, topo):
                 ts(T.a0c[:, k + NC:k + 384], T.r1[:, o:NC], sc, None, A.not_equal, r=["r1", ps(OB[c])], p=[key])
 
     def own_sums():
-        if REDUCE_V:
-            do("v", lambda: V.tensor_reduce(T.a0[:, 1:2], T.a0c[:, 448:896], AxisListType.X, A.add), r=["a0c1"], p=["a0"])
-        for c in (0, 2) if REDUCE_V else (1, 0, 2):
+        for c in (1, 0, 2):
             j, jk = junk(448)
             do("s", lambda: S.activation(j, T.a0c[:, 448 * c:448 * c + 448], F.Sign, bias=0.5 if c == 2 else -0.5, scale=-1.0, accum_out=T.a0[:, c:c + 1]),
                r=["a0c%d" % c, "a0z"], w=[jk], p=["a0"])
 
     def first_turns():
-        if REDUCE_V:
-            ts(T.d0[:, 0:3:2], T.a0[:, 0:3:2], -0.5, -65.0, A.mult, A.add, r=["a0"], p=["d0"])
-            ts(T.d0[:, 1:2], T.a0[:, 1:2], 159.0, None, A.add, r=["a0"], p=["d0"])
-        else:
-            ts(T.d0[:, 0:3], T.a0[:, 0:3], -0.5, -65.0, A.mult, A.add, r=["a0"], w=["d0"])
+        ts(T.a0[:, 8:11], T.a0[:, 0:3], -0.5, -65.0, A.mult, A.add, r=["a0"], w=["d0"])
 
     def block_of(c):
         return (8 * c, 8 * c + 8, 0, 8) if c < 2 else (16, 20, 4, 8)
@@ -380,20 +422,16 @@ def rank_program(g, core, T, topo):
         return T.xn[:, 2 + 4 * a:2 + 4 * b:4]
 
     def digits():
-        do("v", lambda: V.tensor_tensor_scan(T.nt[:, 0:4 * NM], T.xn[:, 2:2 + 4 * NM], T.xn[:, 0:4 * NM], 0.0, A.add, A.subtract),
-           r=["xn", "xnz", "xnm", "ntz"], w=["nt"])
+        run(T.nt[:, 0:4 * NM], T.xn[:, 2:2 + 4 * NM], T.xn[:, 0:4 * NM], 0.0, A.add, A.subtract, r=["xn", "xnz", "xnm", "ntz"], w=["nt"])
 
-    def spread(h, every=True):
+    def spread(h):
         a = 0 if h else 128
         quant("nq", a, a + 128, "nt", 0, ["nt", "ntz"], hk("nq", a))
-        if every:
+        if h == 0:
             mm(6, 128, "kq", KB, "nq", a, key=hk("nq", a))
         for k in ((), (0, 1))[h] if h < 2 else (h,):
             a = 0 if k else 128
             mm(7, 128, "kq", KG + 112 - 16 * k, "nq", a, k == 0, k == NG - 1, hk("nq", a), "kq%d" % KG)
-
-    def take_offsets():
-        ts(T.off[:], bank(6, 0, NM), 160.0, None, A.add, r=[ps(6)], w=["off"])
 
     EB, VB, SB, CB = {"A": 6, "B": 7}, {"A": 4, "B": 5}, {"A": 0, "B": 1}, {"A": 2, "B": 3}
     EARLY = tuple(m for m in BY_VECTOR if 16 * m < H)
@@ -402,17 +440,12 @@ def rank_program(g, core, T, topo):
     def scores(n, a):
         return (VB if a else EB)[n]
 
-    def span(a):
-        return (a, a + H) if SPLIT_P else (0, NC)
-
     def own_column(n, a):
-        k, (x, y) = scores(n, a), span(a)
-        tt(half("dg", n, x, y), bank(k, x, y), T.dpos[:, 0:y - x], A.min, r=[ps(k), "dpos"], w=[hk("dg" + n, a)])
+        k = scores(n, a)
+        tt(half("dg", n, a, a + H), bank(k, a, a + H), T.dpos[:, 0:H], A.min, r=[ps(k), "dpos"], w=[hk("dg" + n, a)])
 
     def carry(n, a):
-        x, y = span(a)
-        do("v", lambda: V.tensor_tensor_scan(half("sc", n, x, y), T.rstn[:, 0:y - x], half("dg", n, x, y), 0.0, A.min, A.max),
-           r=["rstn", hk("dg" + n, a)], w=[hk("sc" + n, a)])
+        run(half("sc", n, a, a + H), T.rstn[:, 0:H], half("dg", n, a, a + H), 0.0, A.min, A.max, r=["rstn", hk("dg" + n, a)], w=[hk("sc" + n, a)])
 
     def part(n, m):
         o, e = 4 * TILE[(NM - m) // 4][0], (NM - m) % 4
@@ -425,8 +458,8 @@ def rank_program(g, core, T, topo):
         return half("sc", n, 16 * m + 15, 16 * m + 16)
 
     def inside(n, a):
-        k, (x, y) = scores(n, a), span(a)
-        tt(T["mt" + n][:, 4 * x:4 * y:4], bank(k, x, y), half("sc", n, x, y), A.is_le,
+        k = scores(n, a)
+        tt(T["mt" + n][:, 4 * a:4 * (a + H):4], bank(k, a, a + H), half("sc", n, a, a + H), A.is_le,
            r=[ps(k), hk("sc" + n, a)] + ([zeros(n, NM)] if a else []), p=["mt%s%d" % (n, NM)])
 
     def inside_sums():
@@ -439,7 +472,7 @@ def rank_program(g, core, T, topo):
 
     def scalar_compare(rows, a):
         late = None
-        for n, m in [(n, m) for n in rows for m in BY_SCALAR if (16 * m >= H) == (a > 0) or not SPLIT_P] + [(None, None)]:
+        for n, m in [(n, m) for n in rows for m in BY_SCALAR if (16 * m >= H) == (a > 0)] + [(None, None)]:
             if m:
                 k = (SB if a else CB)[n]
                 j, jk = junk(16 * m)
@@ -466,8 +499,8 @@ def rank_program(g, core, T, topo):
         o, d = 4 * TILE[3][0], 4 * SHORT if n == "B" else 0
         for e in range(4):
             a = d + SHORT * (3 - e)
-            do("v", lambda: V.tensor_tensor_scan(T.ds[:, a:a + SHORT], T.rs2[:], T["mt" + n][:, o + e:o + 4 * SHORT:4], 0.0, A.mult, A.add),
-               r=["rs2"] + ["mt%s%d" % (n, m - e) for m in (8, 4)] + ["mz%s%d" % (n, u) for u in (3, 4)], p=["ds" + n])
+            run(T.ds[:, a:a + SHORT], T.rs2[:], T["mt" + n][:, o + e:o + 4 * SHORT:4], 0.0, A.mult, A.add,
+                r=["rs2"] + ["mt%s%d" % (n, m - e) for m in (8, 4)] + ["mz%s%d" % (n, u) for u in (3, 4)], p=["ds" + n])
 
     def row_part(n, k):
         ow, d = T["ow" + n], 4 * SHORT if n == "B" else 0
@@ -482,43 +515,23 @@ def rank_program(g, core, T, topo):
         else:
             tt(ow[:, 10:NM], old[:, 10:NM], T["acc" + n][:, 10:NM], A.subtract, r=["acc" + n, key], w=["ow10" + n])
 
-    def table(h):
-        mm(h % 4, NC, "kq", KW + 128 * h, "cq", 0)
+    def unpack(a, PX):
+        for b in (a, a + 1):
+            mm(4 + b % 2, NC, "kq", KE + 128 * b, PX, 0)
 
-    def copy_table(h):
-        scopy(plane("cw", h), bank(h % 4), r=[ps(h % 4)], w=["cw%d" % h])
-
-    def look_up(h, prev, a=0, b=NC):
-        new = "kr%d" % (h % 2)
-        tt(T[new][:, a:b], plane("cw", h).indirect(T.off[:, a // 16:b // 16]), T[prev][:, a:b], A.add, r=["cw%d" % h, "off", prev], p=[new])
-        return new
-
-    def count_teams(prev, c):
-        j, jk = junk(NC)
-        do("s", lambda: S.activation(j, T[prev][:], F.Sign, bias=T.pk[:, c:c + 1], scale=-1.0, accum_out=T.cnt[:, c:c + 1]),
-           r=[prev, "pk"], w=["cnt%d" % c, jk])
-
-    def own_totals(h):
-        tt(T.ogd[:], plane("cw", h).indirect(T.offo[:, 0:3]), T.diag[:, 0:48], A.mult, r=["cw%d" % h, "offo", "offo2", "diag"], w=["ogd"])
-
-    def own_totals_picked():
-        scan(T.os1[:], T.ogd[:], 48, r=["rst", "ogd"], w=["os1"])
-
-    def own_totals_added(old):
-        tt(T.pk[:, 0:3], T[old][:, 0:3], T.os1[:, 15:48:16], A.add, r=["os1", old], w=["pk"])
-
-    def unpack(b, PX):
-        mm(4 + b % 2, NC, "kq", KE + 128 * b, PX, 0)
+    def unpacked(a):
+        for b in (a, a + 1):
+            scopy(plane("fp", b), bank(4 + b % 2), r=[ps(4 + b % 2)], w=["fp%d" % b])
 
     def places(t, PX):
         UP = {"A": 0, "B": 128}
-        for banks in (EB, CB) if SPLIT_P else ():
+        for banks in (EB, CB):
             for n in "BA":
                 mm(banks[n], H, "up", UP[n], PX, 0, key=hk(PX, 0))
         for banks in (VB, SB):
             for n in ORDER:
                 mm(banks[n], NC, "up", UP[n], PX, 0)
-        for a in HALVES if SPLIT_P else (H,):
+        for a in HALVES:
             for step in (own_column, carry):
                 for n in ORDER if a else "BA":
                     step(n, a)
@@ -528,7 +541,7 @@ def rank_program(g, core, T, topo):
                     inside(n, 0)
         scalar_compare(ORDER, H)
         for n in "BA":
-            compare(n, EARLY, 0 if SPLIT_P else H)
+            compare(n, EARLY, 0)
         for n in "BA":
             inside(n, H)
             compare(n, LATE, H)
@@ -541,6 +554,7 @@ def rank_program(g, core, T, topo):
         short_sums("A")
         if t == 0:
             constants(KO, 128, "go", 0, ["go"])
+            quantise_row(*range(EARLY_ROWS))
         first_turns()
         for n in "AB":
             row_part(n, 1)
@@ -550,7 +564,7 @@ def rank_program(g, core, T, topo):
             if n == "B":
                 tt(T.rkd[:], bank(CB["A"]), T.diag[:], A.mult, r=[ps(CB["A"]), "diag"], w=["rkd"])
             column_sums(t, n, (1,))
-        do("v", lambda: V.tensor_tensor_scan(T.cs[:, 16:16 + NC], T.rkd[:], part("A", NM), 0.0, A.add, A.subtract), r=["rkd", "mtA%d" % NM], w=["cs"])
+        run(T.cs[:, 16:16 + NC], T.rkd[:], part("A", NM), 0.0, A.add, A.subtract, r=["rkd", "mtA%d" % NM], w=["cs"])
 
         def row_of_b(a):
             tt(T.bx[:, a:a + H], T.owB[:, 0:10 + a // 16].indirect(T.lm[:, a // 16:a // 16 + 10]), T.diag[:, 0:H], A.mult,
@@ -560,160 +574,263 @@ def rank_program(g, core, T, topo):
             tt(T.bt[:, a:a + H], bank(CB["B"], a, a + H), T.bx[:, a:a + H], A.add, r=[ps(CB["B"]), hk("bx", a)], w=[hk("bt", a)])
 
         row_of_b(0)
-        tt(T.df[:], T.cs[:, 31:NC + 16:16], T.cs[:, 15:NC:16], A.subtract, r=["cs", "csz"], w=["df"])
+        tt(T.plA[:, NM:2 * NM], T.cs[:, 31:NC + 16:16], T.cs[:, 15:NC:16], A.subtract, r=["cs", "csz"], w=["df"])
         whole_b(0)
-        tt(T.plA[:], T.owA[:], T.df[:], A.add, r=["ow0A", "ow1A", "ow5A", "ow9A", "df"], w=["plA", "pl10"])
+        tt(T.plA[:, 0:NM], T.owA[:], T.plA[:, NM:2 * NM], A.add, r=["ow0A", "ow1A", "ow5A", "ow9A", "df"], w=["plA", "pl10"])
         row_part("B", 3)
         vcopy(T.aoff[:, 0:10], T.plA[:, 0:10], r=["plA"], w=["aoff0"])
         row_of_b(H)
         for c in range(3):
             a, b, ma, mb = block_of(c)
-            scopy(slots(a, b), T.mask8[:, ma:mb], T.d0[:, c:c + 1], r=["mask8", "d0", "xnz"], p=["xn"])
+            scopy(slots(a, b), T.mask[:, ma:mb], T.a0[:, 8 + c:9 + c], r=["mask8", "d0", "xnz"], p=["xn"])
         if t == 0:
-            for h in range(1, NG):
-                row_to_all(h)
+            late_patterns()
+            row(*range(EARLY_ROWS, NBUF + EARLY_ROWS))
+        else:
+            for a in (0, 2):
+                unpack(a, PX)
+                unpacked(a)
         vcopy(T.cx[:, 0:NC].indirect(T.aoff[:, 0:10]), T.bt[:, 0:H], r=["aoff0", hk("bt", 0)], w=["cx"])
         tt(T.plA[:, 10:NM], T.plA[:, 10:NM], T.accA[:, 10:NM], A.subtract, r=["accA"], w=["pl10"])
         whole_b(H)
         vcopy(T.aoff[:, 10:NM], T.plA[:, 10:NM], r=["pl10"], w=["aoff"])
-        ts(T.offo[:, 0:3], T.d0[:, 0:3], 160.0, None, A.add, r=["d0"], w=["offo"])
+        ts(T.offo[:, 0:3], T.a0[:, 8:11], 160.0, None, A.add, r=["d0"], w=["offo"])
         digits()
         vcopy(T.cx[:, 0:NC].indirect(T.aoff[:, 10:NM]), T.bt[:, H:NC], r=["aoff", hk("bt", H)], w=["cx"])
+        if t == 0:
+            constants(KB, 128, "bd", 0, ["bd"])
         spread(0)
-
+        if t == 0:
+            quantise_row(*range(EARLY_ROWS, 3))
         for a in HALVES:
             ts(T.ct[:, 4 * a:4 * (a + H):4], T.cx[:, a:a + H], MG32, MG32, A.add, A.subtract, r=["cx"], w=["cthi%d" % a])
-        for a in HALVES:
-            tt(T.ct[:, 4 * a + 1:4 * (a + H):4], T.cx[:, a:a + H], T.ct[:, 4 * a:4 * (a + H):4], A.subtract, r=["cx", "cthi%d" % a], w=["ctlo%d" % a])
-        for a in HALVES:
-            quant("cq", a, a + H, "ct", 4 * a, ["cthi%d" % a, "ctlo%d" % a, "ct2", "ct3"], hk("cq", a))
-        take_offsets()
         if t == 0:
-            quantise_row_to_all(1)
-            vcopy(T.bg[:, 448:512], T.bd[:, 0:64], r=["bd", "bgz"], w=["bg"])
+            quantise_row(3)
+            row(*range(NBUF + EARLY_ROWS, 10))
+        for a in HALVES:
+            tt(T.ct[:, 4 * a + 2:4 * (a + H):4], T.cx[:, a:a + H], T.ct[:, 4 * a:4 * (a + H):4], A.subtract, r=["cx", "cthi%d" % a], w=["ctlo%d" % a])
+        for a in HALVES:
+            quant("cq", a, a + H, "ct", 4 * a, ["cthi%d" % a, "ctlo%d" % a, "ct1", "ct3"], hk("cq", a))
+        ts(T.off[:], bank(6, 0, NM), 160.0, None, A.add, r=[ps(6)], w=["off"])
+
+    KS, KV = 6, {0: 3, H: 1}
+
+    def table(h):
+        mm(int(h == 1), NC, "kq", KW + 128 * h, "cq", 0)
+
+    def copy_table(h):
+        scopy(plane("cw", h), bank(int(h == 1)), float(M), r=[ps(int(h == 1))], w=["cw%d" % h])
+
+    def digit_table(h):
+        mm(2, NC, "kq", KD + 128 * h, "cq", 0)
+
+    def copy_digits(h):
+        o = 2 * NC * (h % 2)
+        scopy(T.cd[:, o:o + 2 * NC:2], bank(2), r=[ps(2), "cdz"], w=["cd%d" % (h % 2)])
+
+    def first_keys(a):
+        tt(T.kr0[:, a:a + H], plane("cw", 0).indirect(T.off[:, a // 16:(a + H) // 16]), T.tier[:, a:a + H], A.add, r=["cw0", "off", "tier"], p=["kr0"])
+
+    def count_teams(h, c):
+        j, jk = junk(NC)
+        src, key, o, own = (T.kr0[:], "kr0", 4, "pkc") if h == 1 else (bank(KS), ps(KS), 0, "pk")
+        do("s", lambda: S.activation(j, src, F.Sign, bias=T.pk[:, o + c:o + c + 1], accum_out=T.cnt[:, c:c + 1]), r=[key, own], w=["cnt%d" % c, jk])
+
+    def own_totals(h):
+        tt(T.ogd[:], plane("cw", h).indirect(T.offo[:, 0:3]), T.diag[:, 0:48], A.mult, r=["cw%d" % h, "offo", "offo2", "diag"], w=["ogd"])
+
+    def own_totals_picked():
+        scan(T.os1[:], T.ogd[:], 48, r=["rst", "ogd"], w=["os1"])
+
+    def own_totals_added(old):
+        if old == "tiec":
+            tt(T.pk[:, 4:7], T.tiec[:, 4:7], T.os1[:, 15:48:16], A.subtract, r=["os1", "tiecc"], w=["pkc"])
+        tt(T.pk[:, 0:3], T[old][:, 0:3], T.os1[:, 15:48:16], A.subtract, r=["os1", old], w=["pk"])
+
+    def own_offsets(c, src, key):
+        a, b, ma, mb = block_of(c)
+        ts(T.offm[:, a:b], T.mask[:, OWN + ma:OWN + mb], src, float(NC), A.max, A.add, r=["zm", key], p=["offm"])
+
+    def grown(h):
+        return ("gt", "gq", h - 1) if h < 5 else ("gu", "zq", h - 5)
+
+    def keys_so_far(h):
+        for k, a, n in ((KV[0], 0, H), (KS, 0, NC), (KV[H], H, H)):
+            mm(k, n, "kq", K0, "g0", a, True, False)
+            if h > 4:
+                mm(k, n, "kq", KM, "gq", a, False, False)
+
+    def keys_grow(h):
+        o, (tile, _, e) = 2 * NC * (h % 2), grown(h)
+        for a, cp in ((H, scopy), (0, vcopy)):
+            cp(T[tile][:, 4 * a + e:4 * (a + H):4], T.cd[:, o:o + 2 * NC].indirect(T.offm[:, a // 16:(a + H) // 16]),
+               r=["cd%d" % (h % 2), "offm", tile + "z"], w=[hk(tile, a)])
+
+    def keys_added(h):
+        tile, q, _ = grown(h)
+        for a in HALVES:
+            quant(q, a, a + H, tile, 4 * a, [hk(tile, a)], hk(q, a))
+        mm(KV[0], H, "kq", KM, q, 0, False, True, hk(q, 0))
+        mm(KS, NC, "kq", KM, q, 0, False, True)
+        mm(KV[H], H, "kq", KM, q, H, False, True)
+
+    def turned(k):
+        if k == 0:
+            do("v", lambda: V.transpose(T.it[:, 0:NC], T.ir[:, 16:16 + NC]), r=["ir"], p=["it"])
+        else:
+            do("v", lambda: V.transpose(T.it[:, NC:2 * NC + 32], T.ir[:, 0:NC + 32]), r=["ir", "irz0", "irz"], p=["it"])
+
+    def beside(t, h, k):
+        for x in BESIDE[t].get((h, k), "").split():
+            n = int(x[1:] or 0)
+            if x[0] == "p":
+                vcopy(T.ir[:, 16:16 + NC].indirect(T.aoff[:, 10 * n:10 * n + 10]), T.iom[:, H * n:H * n + H], r=["aoff0", "aoff", "iom"], w=["ir"])
+            elif x[0] == "t":
+                turned(n)
+            elif x[0] == "l":
+                ts(T.inva[:], T.it[:, 0:2 * NC + 32].indirect(T.lt[:, 0:2]), 160.0, None, A.add, r=["it", "lt"], w=["inva"])
+            elif x[0] == "e":
+                ts(T.eb[:, 3:515:4], T.triv[:], 0.0, None, A.is_equal, r=["triv", "ebz"], w=["eb"])
+            elif x[0] == "u":
+                quantise_unpacking(n)
+            else:
+                quantise_row(n)
 
     def draft(t, PX):
         last = t == 1
         for n, a in enumerate(HALVES):
-            mm(2 * n, H, "kq", KW, "cq", a, key=hk("cq", a))
+            mm(2 * n, H, "kq", KW, "cq", a, True, False, key=hk("cq", a))
+            mm(2 * n, H, "kq", KD, "cq", a, False, True, key=hk("cq", a))
         table(1)
         for n, a in enumerate(HALVES):
             tt(plane("cw", 0, a, a + H), bank(2 * n, 0, H), T.tab0[:, a:a + H], A.add, r=[ps(2 * n), "tab0"], p=["cw0"])
         copy_table(1)
+        digit_table(1)
+        copy_digits(1)
         if t == 0:
-            quantise_row_to_all(2)
+            scopy(T.bg[:, 448:512], T.bd[:, 0:64], r=["bd", "bgz"], w=["bg"])
+            quantise_row(4)
         own_totals(0)
-        look_up(0, "tier", 0, H)
+        first_keys(0)
         own_totals_picked()
-        prev = look_up(0, "tier", H, NC)
+        first_keys(H)
         own_totals_added("tiec")
+        if t == 0:
+            quantise_row(5)
         small = [lambda k=k: list_of_turned_rows(k) for k in range(5)] if t == 0 else []
         for h in range(1, NG):
             own = h < NG - 1
-            if own:
+            if h + 1 < NG - 1 or own and last:
                 table(h + 1)
-            if h in (3, 4):
-                unpack(2 * h - 6, PX)
-                unpack(2 * h - 5, PX)
+            if h + 1 < NG - 1:
+                digit_table(h + 1)
+            if t == 0 and h in UNPACK:
+                unpack(2 * UNPACK.index(h), PX)
             ns = 3 if h == 1 else 2
             for c in range(ns):
-                count_teams(prev, c)
+                count_teams(h, c)
             if h == 1:
-                vcopy(T.ir[:, 16:16 + NC].indirect(T.aoff[:, 0:NM]), T.iom[:], r=["aoff0", "aoff", "iom"], w=["ir"])
+                for k in range(2):
+                    ts(plane("kd", k), T.kr0[:], col(RA + k), col(RA + k), A.add, A.subtract, r=["kr0", "mg"], w=["kd%d" % k])
+                own_offsets(0, T.cnt[:, 0:1], "cnt0")
+                if t == 0:
+                    quantise_row(6)
+                run(T.gt[:, 0:4 * NC:4], plane("kd", 0), plane("kd", 1), 0.0, A.max, A.subtract, r=["kd0", "kd1", "gtz"], w=both("gt"))
+                own_offsets(1, T.cnt[:, 1:2], "cnt1")
+                if t == 0:
+                    quantise_row(7)
+                quant("g0", 0, NC, "gt", 0, both("gt"), "g0")
             else:
-                ts(T.cb[:], T[prev][:], T.pk[:, 2:3], None, A.is_gt, r=[prev, "pk"], w=["cb"])
-                if h == 2:
-                    do("v", lambda: V.transpose(T.it[:, NC:2 * NC + 32], T.ir[:, 0:NC + 32]), r=["ir", "irz0", "irz"], p=["it"])
-                elif h == 3 and t == 0:
-                    quantise_unpacking(2)
-                do("v", lambda: V.tensor_tensor_scan(T.cbs[:], T.ones[:, 0:NC], T.cb[:], -160.0, A.mult, A.add), r=["cb", "ones"], w=["cbs"])
-                if h < 4 and t == 0:
-                    quantise_unpacking(3 * h - 6)
-                a, b, ma, mb = block_of(2)
-                ts(slots(a, b), T.mask8[:, ma:mb], T.cbs[:, NC - 1:NC], None, A.mult, r=["mask8", "cbs"], p=["xn"])
-                if h == 2 and t == 0:
-                    quantise_unpacking(1)
-            for c in range(ns):
+                for a in HALVES:
+                    ts(plane("cb", 0, a, a + H), bank(KV[a], 0, H), T.pk[:, 2:3], 0.0, A.add, A.is_gt, r=[ps(KV[a]), "pk"], p=["cb"])
+                beside(t, h, 0)
+                run(plane("cb", 1), plane("cb", 0), plane("cb", 0), -float(NC), A.add, A.add, r=["cb"], w=["cbs"])
+                if own:
+                    own_offsets(0, T.cnt[:, 0:1], "cnt0")
+                beside(t, h, 1)
+            third, key = (T.cnt[:, 2:3], "cnt2") if ns == 3 else (plane("cb", 1, NC - 1, NC), "cbs")
+            if own:
+                keys_so_far(h)
+                own_offsets(2, third, key)
+            a, b, ma, mb = block_of(2)
+            ts(slots(a, b), T.mask[:, HALF + ma:HALF + mb], third, None, A.mult, r=["mask8n", key], p=["xn"])
+            if ns == 2 and (own or last):
+                ts(T.offo[:, 2:3], third, 0.5, 160.0, A.mult, A.add, r=["cbs"], w=["offo2"])
+            if ns == 2 and own:
+                own_offsets(1, T.cnt[:, 1:2], "cnt1")
+            for c in range(2):
                 a, b, ma, mb = block_of(c)
-                if c < 2 < ns:
-                    ts(slots(a, b), T.mask8n[:, ma:mb], T.cnt[:, c:c + 1], None, A.mult, r=["mask8n", "cnt%d" % c], p=["xn"])
-                else:
-                    scopy(slots(a, b), T.mask8n[:, ma:mb], T.cnt[:, c:c + 1], r=["mask8n", "cnt%d" % c], p=["xn"])
-            if t == 0 and h == 1:
-                small.pop(0)()
-                constants(KG, 240, "bg", 0, ["bg"])
-                small.pop(0)()
-                ts(T.eb[:, 3:515:4], T.triv[:], 0.0, None, A.is_equal, r=["triv", "ebz"], w=["eb"])
-            digits()
+                scopy(slots(a, b), T.mask[:, HALF + ma:HALF + mb], T.cnt[:, c:c + 1], r=["mask8n", "cnt%d" % c], p=["xn"])
+                if c == 0 and (h + 1 < NG - 1 or own and last):
+                    copy_table(h + 1)
             if own or last:
-                ts(T.offo[:, 0:ns], T.cnt[:, 0:ns], -0.5, 160.0, A.mult, A.add, r=["cnt%d" % c for c in range(ns)], w=["offo"])
-                if ns == 2:
-                    ts(T.offo[:, 2:3], T.cbs[:, NC - 1:NC], 160.0, None, A.add, r=["cbs"], w=["offo2"])
-                elif small:
-                    small.pop(0)()
-            spread(h, own)
+                ts(T.offo[:, 0:ns], T.cnt[:, 0:ns], 0.5, 160.0, A.mult, A.add, r=["cnt%d" % c for c in range(ns)], w=["offo"])
             if own:
+                if small:
+                    small.pop(0)()
+                keys_grow(h)
                 own_totals(h)
-                if h == 1:
-                    do("v", lambda: V.transpose(T.it[:, 0:NC], T.ir[:, 16:16 + NC]), r=["ir"], p=["it"])
-                elif h == 2:
-                    ts(T.inva[:], T.it[:, 0:2 * NC + 32].indirect(T.lt[:, 0:2]), 160.0, None, A.add, r=["it", "lt"], w=["inva"])
+                digits()
+                keys_added(h)
                 own_totals_picked()
-                take_offsets()
+                if t == 0 and h == 1:
+                    constants(KG, 240, "bg", 0, ["bg"])
+                else:
+                    spread(h)
                 own_totals_added("pk")
+                if t == 0 and h == 1:
+                    spread(h)
                 if small:
                     small.pop(0)()
-                prev = look_up(h, prev)
-                if small:
-                    small.pop(0)()
-            if t == 0 and h + 2 < NG:
-                quantise_row_to_all(h + 2)
-            if own:
-                copy_table(h + 1)
-            if h in (3, 4):
-                for b in (2 * h - 6, 2 * h - 5):
-                    scopy(plane("fp", b), bank(4 + b % 2), r=[ps(4 + b % 2)], w=["fp%d" % b])
-            if h >= 4:
-                scopy(plane("fs", h - 4), plane("fp", h - 4).indirect(T.inva[:, 0:NM]), r=["fp%d" % (h - 4), "inva"], w=["fs%d" % (h - 4)])
-        return prev
+                beside(t, h, 2)
+            else:
+                digits()
+                spread(h)
+            if h + 1 < NG - 1:
+                copy_digits(h + 1)
+            if t == 0:
+                row(2 * h + 8, 2 * h + 9)
+            if t == 0 and h in UNPACK:
+                unpacked(2 * UNPACK.index(h))
+            for k in SORT[t].get(h, ()):
+                scopy(plane("fs", k), plane("fp", k).indirect(T.inva[:, 0:NM]), r=["fp%d" % k, "inva"], w=["fs%d" % k])
 
-    def layer(t, prev):
+    def layer(t):
         X, PY, YQ = "xq%d" % t, "py%d" % t, "yq%d" % t
         last = t == 1
         ts(T.noff[:], bank(7, 0, NM), 160.0, None, A.add, r=[ps(7)], w=["noff"])
         for k in range(4):
-            cp = scopy if k else vcopy
-            cp(T.zt[:, k:4 * NC:4], plane("fs", k).indirect(T.noff[:, 0:NM]), r=["fs%d" % k, "noff"], p=["zt"])
-        vcopy(T.sr[:, 0:NC].indirect(T.noff[:, 0:NM]), T.iot[:], r=["noff", "iot"], w=["sr"])
-        quant("zq", 0, NC, "zt", 0, ["zt"])
+            for cp, a, b in ((vcopy, 0, ZS[k]), (scopy, ZS[k], NM)):
+                if a < b:
+                    cp(T.zt[:, 64 * a + k:64 * b:4], plane("fs", k).indirect(T.noff[:, a:b]), r=["fs%d" % k, "noff"], p=["zt"])
+        vcopy(T.sr[:, 0:NC].indirect(T.noff[:, 0:NM]), T.iom[:], r=["noff", "iom"], w=["sr"])
+        quant("zq", 0, NC, "zt", 0, ["zt"], both("zq"))
         for b in (4, 5, 0, 6, 1, 7, 2, 3):
             mm(b, NC, "ww", 128 * b, "zq", 0)
             if b >= 4:
                 scopy(plane("cc", b - 4), bank(b), r=[ps(b)], w=["cc%d" % (b - 4)])
-        tt(T.rkd[:], T.sr[:, 0:NC].indirect(T.aoff[:, 0:NM]), T.diag[:], A.mult, r=["sr", "aoff0", "aoff", "diag"], w=["rkd"])
-        scan(T.rks[:], T.rkd[:], r=["rst", "rkd"], w=["rks"])
+        tt(plane("rk", 0), T.sr[:, 0:NC].indirect(T.aoff[:, 0:NM]), T.diag[:], A.mult, r=["sr", "aoff0", "aoff", "diag"], w=["rk0"])
+        scan(plane("rk", 1), plane("rk", 0), r=["rst", "rk0"], w=["rk1"])
         for b in range(4):
             tt(plane("yp", b), bank(b), plane("cc", b), A.max, r=[ps(b), "cc%d" % b], w=["yp%d" % b])
             if b == 0:
-                vcopy(T.koff[:], T.rks[:, 15:NC:16], r=["rks"], w=["koff"])
+                ts(T.koff[:], T.rk[:, NC + 15:2 * NC:16], 160.0, None, A.add, r=["rk1"], w=["koff"])
         for a in HALVES:
             for k in range(4):
                 out, src = T.yt[:, 4 * a + k:4 * (a + H):4], plane("yp", k).indirect(T.koff[:, a // 16:(a + H) // 16])
-                if k < (3 if a else 2):
+                if k < YS[a > 0]:
                     scopy(out, src, 0.03125, r=["yp%d" % k, "koff"], p=["yt%d" % a])
                 else:
                     ts(out, src, 0.03125, None, A.mult, r=["yp%d" % k, "koff"], p=["yt%d" % a])
             quant(YQ, a, a + H, "yt", 4 * a, ["yt%d" % a], hk(YQ, a))
-            if SPLIT_Y:
-                send_tile(t, PY, YQ, (a,))
-        if not SPLIT_Y:
-            send_tile(t, PY, YQ, HALVES)
+            send_half(t, PY, YQ, a)
         if last:
             own_totals(NG - 1)
             own_totals_picked()
             own_totals_added("pk")
-            tt(T.tsb[:, 0:3], T.pk[:, 0:3], T.tiec[:, 0:3], A.subtract, r=["pk", "tiec"], w=["tsb"])
-            scopy(T.tsb[:, 4:7], T.tsb[:, 0:3], 1.0 / 512, r=["tsb"], w=["tot"])
+            tt(T.tsb[:, 0:3], T.tiec[:, 0:3], T.pk[:, 0:3], A.subtract, r=["pk", "tiec"], w=["tsb"])
+            ts(T.tsb[:, 8:11], T.tsb[:, 0:3], 1.0 / M, MG1, A.mult, A.add, r=["tsb"], w=["tsm"])
+            sline(T.tsb[:, 4:7], T.tsb[:, 8:11], 1.0, -MG1, r=["tsm"], w=["tot"])
             for c in range(3):
                 a = 128 * c - PIECE[c]
                 dma("sy", T.tot[:, 128 * c:128 * c + 128 - a], T.tsb[a:128, 4 + c:5 + c], r=["tot"] + both(PY))
@@ -730,15 +847,13 @@ def rank_program(g, core, T, topo):
             for b in range(4):
                 cp = scopy if b % 2 else vcopy
                 cp(T.xt1[:, 4 * a + b:4 * (a + H):4], bank(4 * n + b, 0, H), r=[ps(4 * n + b)], p=["xt1%d" % a])
+            quant(NX, a, a + H, "xt1", 4 * a, ["xt1%d" % a], hk(NX, a))
             if last and n:
                 store_y(0, 0)
-            quant(NX, a, a + H, "xt1", 4 * a, ["xt1%d" % a], hk(NX, a))
             if last:
                 store(n, a)
-            elif SPLIT_X:
-                send_tile(1, "px1", NX, (a,))
-        if not last and not SPLIT_X:
-            send_tile(1, "px1", NX, HALVES)
+            else:
+                send_half(1, "px1", NX, a)
 
     def store(n, a):
         key = hk("xq2", a)
@@ -749,22 +864,19 @@ def rank_program(g, core, T, topo):
         vcopy(T.ysb[:, a:a + H], bank(4 * n, 0, H), r=[ps(4 * n)], w=["ysb%d" % a])
         dma("s" if n else "sy", T.y[:, a:a + H], T.ysb[:, a:a + H], r=["ysb%d" % a])
 
-    for a in HALVES:
-        dma("sy", T.xt0[:, 4 * a:4 * (a + H)], T.x[:, 4 * a:4 * (a + H)], w=["xt0%d" % a])
+    dma("sy", T.xt0[:, 0:4 * H], T.x[:, 0:4 * H], w=["xt0%d" % 0])
     dma("sy", T.ut[:, :], T.u[:, :], w=["ut"])
+    dma("sy", T.xt0[:, 4 * H:4 * NC], T.x[:, 4 * H:4 * NC], w=["xt0%d" % H])
     while_x_comes()
-    for a in HALVES:
-        quant("xq0", a, a + H, "xt0", 4 * a, ["xt0%d" % a], hk("xq0", a))
-        if SPLIT_0:
-            send_tile(0, "px0", "xq0", (a,))
-        if a == 0:
-            between_halves_of_x()
-    if not SPLIT_0:
-        send_tile(0, "px0", "xq0", HALVES)
+    quant("xq0", 0, H, "xt0", 0, ["xt0%d" % 0], hk("xq0", 0))
+    send_half(0, "px0", "xq0", 0)
     while_u_comes()
     quant("uq", 0, 128, "ut", 0, ["ut"])
+    before_u_is_picked()
     do("v", lambda: V.tensor_copy(T.upc[:, 0:384].bitcast(dt.uint32), T.uqc[:, 0:128].bitcast(dt.uint32).indirect(T.lu[:, 0:24])), r=["uq", "lu"], p=["up"])
     do("s", lambda: S.activation(T.ups[:, 0:384], T.uqs[:, 0:128].indirect(T.lu[:, 0:24]), F.Copy), r=["uq", "lu"], p=["up"])
+    quant("xq0", H, NC, "xt0", 4 * H, ["xt0%d" % H], hk("xq0", H))
+    send_half(0, "px0", "xq0", H)
     behind_the_first_writes()
     dma("sy", codes("ww", 0, 1024), T.wc[:, :], r=both("px0"), p=["ww"])
     dma("sy", T.wws[:, :], T.ws[:, :], p=["ww"])
@@ -774,12 +886,13 @@ def rank_program(g, core, T, topo):
         own_scores("xq%d" % t)
         if t == 0:
             while_own_scores_come()
+        else:
+            before_the_second_draft()
         own_places()
         own_sums()
-        if t == 0:
-            unfilled("A", FILL_V, "v")
         places(t, PX)
-        layer(t, draft(t, PX))
+        draft(t, PX)
+        layer(t)
     for k in range(4):
         dma("sy", T.osc[4 * k:4 * k + 4, :], T.xq2s[32 * k:32 * k + 4, 0:NC], r=both("xq2"))
     store_y(1, H)

from concourse.mybir import dt, AluOpType as A, ActivationFunctionType as F

NC = 320
NG = 8
NM = 20
TILE = ((0, 320), (320, 320), (640, 192), (832, 128), (960, 128))
MT = 1088
SHORT = 192
ORDER = "AB"
BY_SCALAR = (19, 18, 17, 16, 15, 9)
BY_VECTOR = tuple(m for m in range(NM - 1, 0, -1) if m not in BY_SCALAR)
PIECE = (0, 128, 192)
M = NC + 1
NBUF = 6
BESIDE = ({(1, 2): "r8 r9", (2, 0): "e", (2, 2): "r10 r11 p0", (3, 0): "u0", (3, 1): "u1", (3, 2): "r12 r13 p1", (4, 0): "u2", (4, 1): "u3",
           (4, 2): "r14 r15 t0 t1", (5, 0): "l", (5, 2): "r16"},
          {(1, 2): "p0", (2, 2): "p1", (3, 2): "t0 t1", (4, 0): "l"})
UNPACK = (4, 5)
SORT = ({6: (0, 1), 7: (2, 3)}, {4: (0,), 5: (1,), 6: (2,), 7: (3,)})
ZS = (20, 0, 0, 10)
YS = (2, 3)
EARLY_ROWS = 0

F32, BF, I32, U16, FP8, U8 = "float32", "bfloat16", "int32", "uint16", "float8_e4m3fn_x4", "uint8"
SCRATCH = {"ps": ("psum", [128, 4096], F32)}


def _sb(name, cols, dtype):
    SCRATCH[name] = ("sbuf", [128, cols], dtype)


def _mx(name, cols):
    _sb(name + "c", cols, FP8)
    _sb(name + "s", cols, U8)


for _n, _c in (("tab0", NC), ("tier", NC), ("col", 12), ("ramp", NM), ("mask", 32), ("tiec", 8), ("triv", 128), ("lf", 56),
               ("a0", 12), ("r1", NC), ("dg", 2 * NC), ("sc", 2 * NC), ("cs", NC + 16),
               ("accA", NM), ("accB", NM), ("owA", NM), ("owB", NM), ("plA", 2 * NM),
               ("bx", NC), ("bt", NC), ("cx", NC),
               ("xn", 84), ("kr0", NC), ("pk", 8), ("cnt", 4), ("ogd", 48), ("os1", 48),
               ("sr", NC), ("rkd", NC), ("kd", 2 * NC), ("cc", 4 * NC), ("ysb", NC), ("tsb", 12), ("cw", NG * NC)):
    _sb(_n, _c, F32)
for _n, _c in (("ipr", NC), ("diag", NC), ("rst", NC), ("dpos", NC), ("rstn", NC), ("go", 512), ("go0", 512), ("xt0", 4 * NC), ("xt1", 4 * NC),
               ("ut", 512), ("vt", 512), ("ones", 512), ("eb", 516), ("wg", NBUF * 512), ("rr", 512), ("bd", 512), ("bg", 960), ("tri", NC),
               ("tpos", NC), ("a0c", 3 * 448), ("dd", NC), ("rs2", SHORT), ("ds", 8 * SHORT), ("mtA", 4 * MT), ("mtB", 4 * MT),
               ("junk", 16 * 448), ("cb", 2 * NC), ("rk", 2 * NC), ("ct", 4 * NC), ("nt", 512), ("cd", 4 * NC), ("gt", 4 * NC), ("gu", 4 * NC), ("zt", 4 * NC),
               ("yt", 4 * NC), ("fp", 4 * NC), ("fs", 4 * NC), ("yp", 4 * NC), ("iom", NC), ("ir", NC + 32), ("it", 2 * NC + 32)):
    _sb(_n, _c, BF)
_sb("pi_i", 8, I32)
for _n, _c in (("lm", NM), ("lu", 24), ("aoff", NM), ("inva", 32), ("lt", 2), ("off", NM), ("offo", 4), ("offm", NM), ("noff", NM), ("koff", NM)):
    _sb(_n, _c, U16)
KE, KW, KB, KG, KO, KF, K0, KM, KD = 0, 512, 1536, 1664, 1904, 2032, 2160, 2288, 2416
for _n, _c in (("xq0", NC), ("xq1", NC), ("xq2", NC), ("px0", NC), ("px1", NC), ("py0", NC), ("py1", NC), ("uq", 128), ("up", 384), ("vq", 128),
               ("kq", KD + 7 * 128), ("mq", 2 * MT), ("nq", 256), ("cq", NC), ("gq", NC), ("g0", NC), ("zq", NC), ("yq0", NC), ("yq1", NC), ("ww", 1024)):
    _mx(_n, _c)

SEMAPHORES = ["v", "s", "t", "gp", "ls"] + ["d%d" % k for k in range(20)] + ["rx%d" % k for k in range(16)]
H = NC // 2
HALVES = (0, H)

MG1 = 1.5 * 2.0 ** 23
MG16 = 16 * MG1
MG32 = 32 * MG1
LIFT = 2.0 ** 21
FAR = 1e29


def rank_program(g, core, T, topo):
    rank = T.rank_of(core)
    if rank is None:
        return
    V, S, PE = g.vector, g.scalar, g.tensor
    queues = {"v": V, "s": S, "t": PE, "gp": g, "sy": g.sync}
    known = {q: {} for q in queues}
    count = {"v": 0, "s": 0, "t": 0, "gp": 0}
    state = {}
    tally = {"dma": 0, "ls": 0, "junk": 0}
    arrivals = []

    def st(k):
        if k not in state:
            state[k] = {"w": [], "r": [], "b": []}
        return state[k]

    def waits(eng, r, w, p):
        deps = []
        for k in r:
            x = st(k)
            deps += x["w"] + x["b"]
            if k[:2] == "ps":
                deps += [d for d in x["r"] if d[0] != eng]
        for k in w:
            x = st(k)
            deps += x["w"] + x["r"] + x["b"]
        for k in p:
            x = st(k)
            if x["r"]:
                x["b"] = x["w"] + x["r"] + x["b"]
                x["w"], x["r"] = [], []
            deps += [d for d in x["b"] if not (eng == "t" and d[0] == "t")]
        kn = known[eng]
        best = {}
        for d in deps:
            if kn.get(d[0], 0) < d[1] and (d[0] not in best or best[d[0]][1] < d[1]):
                best[d[0]] = d
        items = list(best.values())
        for d in items:
            if any(o is not d and o[2].get(d[0], 0) >= d[1] for o in items):
                continue
            if kn.get(d[0], 0) < d[1]:
                queues[eng].wait_ge(T.sem[d[0]], d[1])
            for s, n in list(d[2].items()) + [(d[0], d[1])]:
                if kn.get(s, 0) < n:
                    kn[s] = n

    def record(ev, r, w, p):
        for k in r:
            st(k)["r"].append(ev)
        for k in w:
            x = st(k)
            x["w"], x["r"], x["b"] = [ev], [], [ev]
        for k in p:
            st(k)["w"].append(ev)

    def do(eng, fn, r=(), w=(), p=()):
        waits(eng, r, w, p)
        count[eng] += 1
        fn().then_inc(T.sem[eng], 1)
        record((eng, count[eng], dict(known[eng])), r, w, p)

    def dma(eng, out, in_, r=(), w=(), p=()):
        waits(eng, r, w, p)
        s = "d%d" % tally["dma"]
        tally["dma"] += 1
        queues[eng].dma_start(out, in_).then_inc(T.sem[s], 16)
        record((s, 16, dict(known[eng])), r, w, p)

    def engines_between(a, b):
        return len(topo.engines(a, b))

    def send(dst, out, in_, r):
        waits("gp", r, (), ())
        rid, pid, _ = topo.addr(dst)
        rx = "rx%d" % len(arrivals)
        g.remote_dma(out, in_, T.sem[rx], T.sem["ls"], pid, rid, topo.mask(core, dst))
        tally["ls"] += engines_between(core, dst)
        arrivals.append((rx, engines_between(dst, core)))
        return arrivals[-1] + ({},)

    def hk(name, a):
        return "%s@%d" % (name, a)

    def both(name):
        return [hk(name, a) for a in HALVES]

    def send_half(t, land, name, a):
        r = [hk(name, a)]
        st(hk(land, a))["w"] = [send(partner(t), codes(land, a, a + H), codes(name, a, a + H), r),
                                send(partner(t), T[land + "s"][:, a:a + H], T[name + "s"][:, a:a + H], r)]

    def partner(t):
        return T.cores[rank ^ (1 << t)]

    def codes(name, a, b):
        return T[name + "c"][:, a:b].bitcast(dt.uint8)

    def bank(k, a=0, b=NC):
        return T.ps[:, 512 * k + a:512 * k + b]

    def ps(k):
        return "ps%d" % k

    def plane(name, k, a=0, b=NC):
        return T[name][:, k * NC + a:k * NC + b]

    def half(name, n, a=0, b=NC, step=1):
        o = NC if n == "B" else 0
        return T[name][:, o + a:o + b:step]

    def col(k):
        return T.col[:, k:k + 1]

    def junk(n):
        k = tally["junk"] % 16
        tally["junk"] += 1
        return T.junk[:, 448 * k:448 * k + n], "junk%d" % k

    def quant(name, a, b, tile, ta, r, key=None):
        kw = {"w": key if isinstance(key, list) else [key]} if key else {"p": [name]}
        do("v", lambda: V.quantize_mx(T[name + "c"][:, a:b], T[name + "s"][:, a:b], T[tile][:, ta:ta + 4 * (b - a)]), r=r, **kw)

    def constants(a, n, tile, ta, r):
        quant("kq", a, a + n, tile, ta, r, "kq%d" % a)

    def mm(k, n, left, la, right, ra, start=True, stop=True, key=None, lkey=None):
        kw = {"w": [ps(k)]} if start else {"p": [ps(k)]}
        lkey = lkey or ("kq%d" % la if left == "kq" else left)
        r = [x for side in (lkey, key or right) for x in (both(side) if side[:2] in ("xq", "px", "cq", "gq", "zq") and "@" not in side else [side])]
        do("t", lambda: PE.matmul_mx(bank(k, 0, n), T[left + "c"][:, la:la + 128], T[left + "s"][:, la:la + 128],
                                     T[right + "c"][:, ra:ra + n], T[right + "s"][:, ra:ra + n], start, stop), r=r, **kw)

    def ts(out, in0, s1, s2, op0, op1=None, **k):
        if op1 is None:
            do("v", lambda: V.tensor_scalar(out, in0, s1, s2, op0), **k)
        else:
            do("v", lambda: V.tensor_scalar(out, in0, s1, s2, op0, op1), **k)

    def tt(out, a, b, op, **k):
        do("v", lambda: V.tensor_tensor(out, a, b, op), **k)

    def vcopy(out, in_, **k):
        do("v", lambda: V.tensor_copy(out, in_), **k)

    def scopy(out, in_, scale=1.0, **k):
        do("s", lambda: S.activation(out, in_, F.Copy, scale=scale), **k)

    def sline(out, in_, scale, bias, **k):
        do("s", lambda: S.activation(out, in_, F.Identity, bias=bias, scale=scale), **k)

    def ssum(in_, n, acc, key, r):
        j, jk = junk(n)
        do("s", lambda: S.activation(j, in_, F.Copy, accum_out=acc), r=r, w=[jk], p=[key])

    def run(out, d0, d1, first, op0, op1, **k):
        do("v", lambda: V.tensor_tensor_scan(out, d0, d1, first, op0, op1), **k)

    def scan(out, d1, n=NC, **k):
        run(out, T.rst[:, 0:n], d1, 0.0, A.mult, A.add, **k)

    def fill(ap, c, key, r=()):
        do("v", lambda: V.memset(ap, c), r=r, w=[key])

    def iota(name, a, b, pattern, base, cm, key=None):
        ap = T[name][:, a:b]
        if name == "pi_i":
            do("gp", lambda: g.iota(ap, pattern, base, cm), w=[name])
        else:
            do("gp", lambda: g.iota(ap, pattern, base, cm, allow_small_or_imprecise_dtypes=True), w=[key or name])

    def clear(name, a, b, key, step=1):
        do("gp", lambda: g.iota(T[name][:, a:b:step], [[0, (b - a + step - 1) // step]], 0, 0, allow_small_or_imprecise_dtypes=True), w=[key])

    def unfilled(n, us, eng):
        for u in us:
            a, b, key = 4 * TILE[u][0] + 64 * (17 - 4 * u), 4 * sum(TILE[u]), "mz%s%d" % (n, u)
            if eng == "s":
                scopy(T["mt" + n][:, a:b], T.ones[:, 0:b - a], 0.0, r=["ones"], w=[key])
            else:
                clear("mt" + n, a, b, key)

    PG, PI, FIRST, REST, RA, RB, W0 = range(7)
    PLAIN, W320, WK0, WKM, HALF, OWN = 0, 8, 9, 10, 16, 24
    ROWS = [(KW, "ones", 0), (KD, "ones", W320), (KW + 128, "ones", 1), (KD + 128, "rr", 1), (KW + 256, "ones", 2), (KD + 256, "rr", 2),
            (K0, "ones", WK0), (KM, "ones", WKM)]
    for h in range(3, NG):
        ROWS += [(KW + 128 * h, "ones", h)] + ([(KD + 128 * h, "rr", h)] if h < NG - 1 else [])

    def row(*ks):
        for k in ks:
            if k < len(ROWS):
                o, (_, name, c), step = 512 * (k % NBUF), ROWS[k], 1 if k < NBUF or ROWS[k][0] == KM else 2
                scopy(T.wg[:, o:o + 512:step], T[name][:, 0:512:step], T.mask[:, c:c + 1],
                      r=[name, "mask8", "maskw"] + (["maskk"] if k > 1 else []), w=["wg%d" % (k % NBUF)])

    def quantise_row(*ks):
        for k in ks:
            if k < len(ROWS):
                constants(ROWS[k][0], 128, "wg", 512 * (k % NBUF), ["wg%d" % (k % NBUF)])

    def quantise_unpacking(*bs):
        for b in bs:
            constants(KE + 128 * b, 128, "eb", 3 - b, ["eb", "ebz"])

    def while_x_comes():
        iota("pi_i", 0, 1, [[0, 1]], 0, 1)
        iota("lf", 48, 56, [[1, 8]], 0, 0, "h8")
        iota("triv", 0, 128, [[1, 128]], 0, -1)
        iota("ipr", 0, NC, [[0, NM], [1, 16]], 0, 0)
        iota("lf", 0, 16, [[1, 2], [16, 8]], 0, 0, "lf0")
        iota("lf", 24, 44, [[16, NM]], 15, 0, "lf1")
        iota("tiec", 0, 2, [[128, 2]], 1 - M, 1, "tiec0")
        iota("tiec", 2, 3, [[0, 1]], 1 - M + PIECE[2], 1, "tiec1")
        fill(T.ones[:], 1.0, "ones")
        ts(T.pi_i[:, 1:2], T.pi_i[:, 0:1], 15, None, A.bitwise_and, r=["pi_i"], w=["pi1"])
        ts(T.pi_i[:, 2:3], T.pi_i[:, 0:1], 4, None, A.arith_shift_right, r=["pi_i"], w=["pi2"])
        fill(T.go0[:], 0.0, "go0z")
        vcopy(col(PG), T.pi_i[:, 2:3], r=["pi2"], w=["hcol"])
        vcopy(col(PI), T.pi_i[:, 1:2], r=["pi1"], w=["pif"])
        do("v", lambda: V.memset(T.lu[:, 16:24], 0), p=["lu"])
        ts(T.mask[:, 0:8], T.lf[:, 48:56], col(PG), None, A.is_equal, r=["h8", "hcol"], w=["mask8"])
        ts(T.mask[:, W320:W320 + 1], col(PG), 0.0, float(NC), A.is_equal, A.mult, r=["hcol"], w=["maskw"])
        for c in range(3):
            o = 128 * c - PIECE[c]
            ts(T.tri[:, 128 * c:128 * c + 128 - o], T.triv[:, o:128], 0.0, None, A.is_lt, r=["triv"], p=["tri"])
        ts(T.pi_i[:, 4:5], T.pi_i[:, 0:1], 31, None, A.bitwise_and, r=["pi_i"], w=["pi4"])
        ts(T.pi_i[:, 5:6], T.pi_i[:, 0:1], 12, None, A.bitwise_and, r=["pi_i"], w=["pi5"])
        ts(T.mask[:, OWN:OWN + 8], T.mask[:, 0:8], -2000.0, NC - 1.0, A.mult, A.add, r=["mask8"], w=["zm"])
        ts(col(FIRST), col(PI), 0.0, None, A.is_equal, r=["pif"], p=["wk2"])
        ts(col(REST), col(PI), 0.0, None, A.is_gt, r=["pif"], p=["wk2"])
        for q in range(4):
            do("v", lambda: V.memset(T.col[32 * q:32 * q + 32, RA:RA + 1], MG1 * 32 ** q), p=["mg0"])
        ts(T.diag[:], T.ipr[:], col(PI), None, A.is_equal, r=["ipr", "pif"], w=["diag"])
        unfilled("B", range(5), "s")
        sline(T.tpos[:], T.tri[:], 2 * FAR, -FAR, r=["tri"], w=["tpos"])
        sline(T.rstn[:], T.ipr[:], 2 * FAR, -FAR, r=["ipr"], w=["rstn"])

    def while_u_comes():
        vcopy(T.lu[:, 0:16], T.lf[:, 0:16], r=["lf0"], p=["lu"])
        ts(T.mask[:, WK0:WK0 + 1], T.pi_i[:, 4:5], 0.0, None, A.is_equal, r=["pi4"], p=["maskk"])
        ts(col(W0), T.pi_i[:, 5:6], 0.0, M - 1.0, A.is_equal, A.mult, r=["pi5"], w=["wk0"])
        ts(col(RB), col(RA), 32.0, None, A.mult, r=["mg0"], w=["mg"])
        ts(T.rst[:], T.ipr[:], 0.0, None, A.is_gt, r=["ipr"], w=["rst"])
        sline(T.dpos[:], T.diag[:], 2 * FAR, -FAR, r=["diag"], w=["dpos"])

    def before_u_is_picked():
        for e in range(4):
            vcopy(T.go0[:, e:512:64], T.mask[:, 0:8], r=["mask8", "go0z"], p=["go0"])
        fill(T.rs2[:], 1.0, "rs2")

    def behind_the_first_writes():
        unfilled("A", (0, 2, 1, 3, 4), "gp")
        iota("go", 0, 512, [[1, 8], [0, 64]], 0, 0)
        clear("bd", 0, 512, "bdz")
        clear("rr", 0, 512, "rrz")
        clear("nt", 4 * NM, 512, "ntz")
        clear("ct", 1, 4 * NC, "ct1", 4)
        clear("ct", 3, 4 * NC, "ct3", 4)
        iota("tab0", 0, NC, [[-M, NC]], M * (NC - 1), 0)
        iota("tier", 0, NC, [[-1, NC]], M - 1 + int(LIFT), 0)
        clear("cd", 1, 4 * NC, "cdz", 2)
        clear("gt", 0, 4 * NC, "gtz")
        clear("bg", 0, 960, "bgz")
        clear("eb", 0, 516, "ebz")
        iota("iom", 0, NC, [[1, NC]], -160, 0)
        clear("ir", 0, 16, "irz0")
        clear("ir", NC + 16, NC + 32, "irz")
        clear("gu", 0, 4 * NC, "guz")

    def before_the_second_draft():
        for name, es in (("gt", (1, 2, 3)), ("gu", (1,))):
            for e in es:
                do("gp", lambda: g.iota(T[name][:, e:4 * NC:4], [[0, NC]], 0, 0, allow_small_or_imprecise_dtypes=True), w=both(name))

    def while_own_scores_come():
        ts(T.tiec[:, 0:3], T.tiec[:, 0:3], -0.5, None, A.add, r=["tiec0", "tiec1"], w=["tiec"])
        ts(T.lm[:], T.lf[:, 24:44], -15.0, 0.0625, A.add, A.mult, r=["lf1"], w=["lm"])
        ts(T.ramp[:], T.lf[:, 24:44], col(PI), None, A.subtract, r=["lf1", "pif"], w=["ramp"])
        fill(T.xn[:, 0:84:2], 0.0, "xnz")
        fill(T.xn[:, 1:84:2], MG16, "xnm")
        fill(T.rs2[:, 128:129], 0.0, "rs2")
        fill(T.tiec[0:64, 2:3], -2.0 ** 22, "tiec")
        fill(T.a0c[:, 3 * 448 - 64:3 * 448], 1.0, "a0z")
        constants(KF, 128, "go0", 0, ["go0"])
        ts(T.mask[:, WKM:WKM + 1], T.pi_i[:, 5:6], 4.0, col(W0), A.is_equal, A.add, r=["pi5", "wk0"], p=["maskk"])
        row(*range(EARLY_ROWS))
        ts(T.mask[:, HALF:HALF + 8], T.lf[:, 48:56], col(PG), 0.5, A.is_equal, A.mult, r=["h8", "hcol"], w=["mask8n"])
        vcopy(T.owA[:], T.ramp[:], r=["ramp"], w=["ow0A", "ow1A", "ow5A", "ow9A"])
        fill(T.cs[:, 15:16], 0.0, "csz")
        ts(T.tiec[:, 4:7], T.tiec[:, 0:3], -LIFT, None, A.add, r=["tiec"], w=["tiecc"])

    def adding_up_by_group():
        ts(T.go[:], T.go[:], col(PG), None, A.is_equal, r=["hcol"], w=["go"])

    def late_patterns():
        scopy(T.bd[:, 1:512:4], T.diag[:, 0:128], r=["diag", "bdz"], p=["bd"])
        scopy(T.bd[:, 2:512:4], T.diag[:, 0:128], -1.0, r=["diag", "bdz"], p=["bd"])
        for e, c in ((0, 1.0), (6, col(FIRST)), (10, col(REST))):
            scopy(T.rr[:, e:512:16], T.ones[:, 0:32], c, r=["ones", "wk2", "rrz"], p=["rr"])

    def list_of_turned_rows(k):
        if k == 0:
            tt(T.pi_i[:, 3:4], T.pi_i[:, 0:1], T.pi_i[:, 2:3], A.add, r=["pi_i", "pi2"], w=["pi3"])
        elif k == 1:
            ts(T.pi_i[:, 3:4], T.pi_i[:, 3:4], 1, None, A.bitwise_and, w=["pi3"])
        elif k == 2:
            ts(T.lf[:, 16:17], T.pi_i[:, 3:4], NC + 16.0, None, A.mult, r=["pi3"], w=["lf2"])
        elif k == 3:
            ts(T.lt[:, 0:1], col(PI), 16.0, T.lf[:, 16:17], A.mult, A.add, r=["pif", "lf2"], w=["lt0"])
        else:
            ts(T.lt[:, 1:2], T.lt[:, 0:1], 256.0, 2.0 * NC, A.add, A.min, r=["lt0"], w=["lt"])

    OB = (1, 3, 2)

    def own_scores(X):
        mm(0, NC, "up", 256, X, 0)
        for c in (0, 2, 1):
            mm(OB[c], 128, X, PIECE[c], "uq", 0)
        mm(4, NC, "up", 256, X, 0)

    def own_places():
        long = ((0, NC), (2, 256))
        scopy(T.a0[:, 4:6], T.ps[:, 512:1025:512], r=[ps(1), ps(2)], w=["own"])
        for c, n in long:
            do("s", lambda: S.activation(T.a0c[:, 448 * c:448 * c + n], bank(4, 0, n), F.Sign, bias=T.a0[:, 4 + c // 2:5 + c // 2], scale=-1.0),
               r=[ps(4), "own"], p=["a0c%d" % c])
        tt(T.r1[:], bank(0), T.tpos[:], A.min, r=[ps(0), "tpos"], w=["r1"])
        for c in (1, 0, 2):
            o, sc, k, rr, key = 128 * c, bank(OB[c], 0, 1), 448 * c, [ps(0), ps(OB[c])], "a0c%d" % c
            if c == 1:
                ts(T.a0c[:, k:k + o], bank(0, 0, o), sc, -1.0, A.is_ge, A.mult, r=rr, p=[key])
                ts(T.a0c[:, k + o:k + NC], bank(0, o, NC), sc, -1.0, A.is_gt, A.mult, r=rr, p=[key])
            if c < 2:
                ts(T.a0c[:, k + NC:k + 448], T.r1[:, o:o + 128], sc, -1.0, A.is_equal, A.mult, r=["r1", ps(OB[c])], p=[key])
            else:
                ts(T.a0c[:, k + o:k + NC], bank(0, o, NC), sc, None, A.is_le, r=rr, p=[key])
                ts(T.a0c[:, k + NC:k + 384], T.r1[:, o:NC], sc, None, A.not_equal, r=["r1", ps(OB[c])], p=[key])

    def own_sums():
        for c in (1, 0, 2):
            j, jk = junk(448)
            do("s", lambda: S.activation(j, T.a0c[:, 448 * c:448 * c + 448], F.Sign, bias=0.5 if c == 2 else -0.5, scale=-1.0, accum_out=T.a0[:, c:c + 1]),
               r=["a0c%d" % c, "a0z"], w=[jk], p=["a0"])

    def first_turns():
        ts(T.a0[:, 8:11], T.a0[:, 0:3], -0.5, -65.0, A.mult, A.add, r=["a0"], w=["d0"])

    def block_of(c):
        return (8 * c, 8 * c + 8, 0, 8) if c < 2 else (16, 20, 4, 8)

    def slots(a, b):
        return T.xn[:, 2 + 4 * a:2 + 4 * b:4]

    def digits():
        run(T.nt[:, 0:4 * NM], T.xn[:, 2:2 + 4 * NM], T.xn[:, 0:4 * NM], 0.0, A.add, A.subtract, r=["xn", "xnz", "xnm", "ntz"], w=["nt"])

    def spread(h):
        a = 0 if h else 128
        quant("nq", a, a + 128, "nt", 0, ["nt", "ntz"], hk("nq", a))
        if h == 0:
            mm(6, 128, "kq", KB, "nq", a, key=hk("nq", a))
        for k in ((), (0, 1))[h] if h < 2 else (h,):
            a = 0 if k else 128
            mm(7, 128, "kq", KG + 112 - 16 * k, "nq", a, k == 0, k == NG - 1, hk("nq", a), "kq%d" % KG)

    EB, VB, SB, CB = {"A": 6, "B": 7}, {"A": 4, "B": 5}, {"A": 0, "B": 1}, {"A": 2, "B": 3}
    EARLY = tuple(m for m in BY_VECTOR if 16 * m < H)
    LATE = tuple(m for m in BY_VECTOR if 16 * m >= H)

    def scores(n, a):
        return (VB if a else EB)[n]

    def own_column(n, a):
        k = scores(n, a)
        tt(half("dg", n, a, a + H), bank(k, a, a + H), T.dpos[:, 0:H], A.min, r=[ps(k), "dpos"], w=[hk("dg" + n, a)])

    def carry(n, a):
        run(half("sc", n, a, a + H), T.rstn[:, 0:H], half("dg", n, a, a + H), 0.0, A.min, A.max, r=["rstn", hk("dg" + n, a)], w=[hk("sc" + n, a)])

    def part(n, m):
        o, e = 4 * TILE[(NM - m) // 4][0], (NM - m) % 4
        return T["mt" + n][:, o + e:o + 64 * m:4]

    def zeros(n, m):
        return "mz%s%d" % (n, (NM - m) // 4)

    def score(n, m):
        return half("sc", n, 16 * m + 15, 16 * m + 16)

    def inside(n, a):
        k = scores(n, a)
        tt(T["mt" + n][:, 4 * a:4 * (a + H):4], bank(k, a, a + H), half("sc", n, a, a + H), A.is_le,
           r=[ps(k), hk("sc" + n, a)] + ([zeros(n, NM)] if a else []), p=["mt%s%d" % (n, NM)])

    def inside_sums():
        scan(T.dd[:], part("B", NM), r=["rst", "mtB%d" % NM], w=["dd"])

    def compare(n, ms, a):
        k = scores(n, a)
        for m in ms:
            ts(part(n, m), bank(k, 0, 16 * m), score(n, m), None, A.is_lt, r=[ps(k), hk("sc" + n, a), zeros(n, m)], w=["mt%s%d" % (n, m)])

    def scalar_compare(rows, a):
        late = None
        for n, m in [(n, m) for n in rows for m in BY_SCALAR if (16 * m >= H) == (a > 0)] + [(None, None)]:
            if m:
                k = (SB if a else CB)[n]
                j, jk = junk(16 * m)
                do("s", lambda: S.activation(j, bank(k, 0, 16 * m), F.Sign, bias=score(n, m), scale=-1.0), r=[ps(k), hk("sc" + n, a)], w=[jk])
            if late:
                o, q, i, ik = late
                do("s", lambda: S.activation(part(o, q), i, F.Relu, accum_out=T["acc" + o][:, q:q + 1]),
                   r=[ik, zeros(o, q)], w=["mt%s%d" % (o, q)], p=["acc9" + o if q == 9 else "acc" + o])
            late = m and (n, m, j, jk)

    def add_up(n, ms):
        for m in [m for m in ms if m > 8]:
            ssum(part(n, m), 16 * m, T["acc" + n][:, m:m + 1], "acc" + n, ["mt%s%d" % (n, m)])

    def column_sums(t, n, us):
        o, c, key = TILE[us[0]][0], TILE[us[0]][0] + (MT if n == "B" else 0), "mq%s%d" % (n, us[0])
        w = sum(TILE[u][1] for u in us) - (64 if t and us[0] else 0)
        r = ["mz%s%d" % (n, u) for u in us] + ["mt%s%d" % (n, NM - 4 * u - e) for u in us for e in range(4)]
        quant("mq", c, c + w, "mt" + n, 4 * o, r, key)
        for u in us:
            mm(CB[n], TILE[u][1], "kq", KO if n == "A" else KF, "mq", c + TILE[u][0] - o, u == 0, u == 1, key)

    def short_sums(n):
        o, d = 4 * TILE[3][0], 4 * SHORT if n == "B" else 0
        for e in range(4):
            a = d + SHORT * (3 - e)
            run(T.ds[:, a:a + SHORT], T.rs2[:], T["mt" + n][:, o + e:o + 4 * SHORT:4], 0.0, A.mult, A.add,
                r=["rs2"] + ["mt%s%d" % (n, m - e) for m in (8, 4)] + ["mz%s%d" % (n, u) for u in (3, 4)], p=["ds" + n])

    def row_part(n, k):
        ow, d = T["ow" + n], 4 * SHORT if n == "B" else 0
        old, key = (ow, "owB") if n == "B" else (T.ramp, "ramp")
        if k == 0:
            tt(ow[:], T.ramp[:], T.dd[:, 15:NC:16], A.subtract, r=["ramp", "dd"], w=["owB", "ow1B", "ow5B", "ow9B", "ow10B"])
        elif k == 1:
            for m, end in ((5, 127), (1, 191)):
                tt(ow[:, m:m + 4], old[:, m:m + 4], T.ds[:, d + end:d + 4 * SHORT:SHORT], A.subtract, r=["ds" + n, key], w=["ow%d%s" % (m, n)])
        elif k == 2:
            tt(ow[:, 9:10], old[:, 9:10], T["acc" + n][:, 9:10], A.subtract, r=["acc9" + n, key], w=["ow9" + n])
        else:
            tt(ow[:, 10:NM], old[:, 10:NM], T["acc" + n][:, 10:NM], A.subtract, r=["acc" + n, key], w=["ow10" + n])

    def unpack(a, PX):
        for b in (a, a + 1):
            mm(4 + b % 2, NC, "kq", KE + 128 * b, PX, 0)

    def unpacked(a):
        for b in (a, a + 1):
            scopy(plane("fp", b), bank(4 + b % 2), r=[ps(4 + b % 2)], w=["fp%d" % b])

    def places(t, PX):
        UP = {"A": 0, "B": 128}
        for banks in (EB, CB):
            for n in "BA":
                mm(banks[n], H, "up", UP[n], PX, 0, key=hk(PX, 0))
        for banks in (VB, SB):
            for n in ORDER:
                mm(banks[n], NC, "up", UP[n], PX, 0)
        for a in HALVES:
            for step in (own_column, carry):
                for n in ORDER if a else "BA":
                    step(n, a)
            if a == 0:
                scalar_compare("BA", 0)
                for n in "BA":
                    inside(n, 0)
        scalar_compare(ORDER, H)
        for n in "BA":
            compare(n, EARLY, 0)
        for n in "BA":
            inside(n, H)
            compare(n, LATE, H)
            add_up(n, LATE + EARLY)
        if t == 0:
            adding_up_by_group()
        inside_sums()
        short_sums("B")
        row_part("B", 0)
        short_sums("A")
        if t == 0:
            constants(KO, 128, "go", 0, ["go"])
            quantise_row(*range(EARLY_ROWS))
        first_turns()
        for n in "AB":
            row_part(n, 1)
            row_part(n, 2)
            column_sums(t, n, (0,))
            column_sums(t, n, (2, 3, 4))
            if n == "B":
                tt(T.rkd[:], bank(CB["A"]), T.diag[:], A.mult, r=[ps(CB["A"]), "diag"], w=["rkd"])
            column_sums(t, n, (1,))
        run(T.cs[:, 16:16 + NC], T.rkd[:], part("A", NM), 0.0, A.add, A.subtract, r=["rkd", "mtA%d" % NM], w=["cs"])

        def row_of_b(a):
            tt(T.bx[:, a:a + H], T.owB[:, 0:10 + a // 16].indirect(T.lm[:, a // 16:a // 16 + 10]), T.diag[:, 0:H], A.mult,
               r=["owB", "ow1B", "ow5B", "ow9B", "lm", "diag"] + (["ow10B"] if a else []), w=[hk("bx", a)])

        def whole_b(a):
            tt(T.bt[:, a:a + H], bank(CB["B"], a, a + H), T.bx[:, a:a + H], A.add, r=[ps(CB["B"]), hk("bx", a)], w=[hk("bt", a)])

        row_of_b(0)
        tt(T.plA[:, NM:2 * NM], T.cs[:, 31:NC + 16:16], T.cs[:, 15:NC:16], A.subtract, r=["cs", "csz"], w=["df"])
        whole_b(0)
        tt(T.plA[:, 0:NM], T.owA[:], T.plA[:, NM:2 * NM], A.add, r=["ow0A", "ow1A", "ow5A", "ow9A", "df"], w=["plA", "pl10"])
        row_part("B", 3)
        vcopy(T.aoff[:, 0:10], T.plA[:, 0:10], r=["plA"], w=["aoff0"])
        row_of_b(H)
        for c in range(3):
            a, b, ma, mb = block_of(c)
            scopy(slots(a, b), T.mask[:, ma:mb], T.a0[:, 8 + c:9 + c], r=["mask8", "d0", "xnz"], p=["xn"])
        if t == 0:
            late_patterns()
            row(*range(EARLY_ROWS, NBUF + EARLY_ROWS))
        else:
            for a in (0, 2):
                unpack(a, PX)
                unpacked(a)
        vcopy(T.cx[:, 0:NC].indirect(T.aoff[:, 0:10]), T.bt[:, 0:H], r=["aoff0", hk("bt", 0)], w=["cx"])
        tt(T.plA[:, 10:NM], T.plA[:, 10:NM], T.accA[:, 10:NM], A.subtract, r=["accA"], w=["pl10"])
        whole_b(H)
        vcopy(T.aoff[:, 10:NM], T.plA[:, 10:NM], r=["pl10"], w=["aoff"])
        ts(T.offo[:, 0:3], T.a0[:, 8:11], 160.0, None, A.add, r=["d0"], w=["offo"])
        digits()
        vcopy(T.cx[:, 0:NC].indirect(T.aoff[:, 10:NM]), T.bt[:, H:NC], r=["aoff", hk("bt", H)], w=["cx"])
        if t == 0:
            constants(KB, 128, "bd", 0, ["bd"])
        spread(0)
        if t == 0:
            quantise_row(*range(EARLY_ROWS, 3))
        for a in HALVES:
            ts(T.ct[:, 4 * a:4 * (a + H):4], T.cx[:, a:a + H], MG32, MG32, A.add, A.subtract, r=["cx"], w=["cthi%d" % a])
        if t == 0:
            quantise_row(3)
            row(*range(NBUF + EARLY_ROWS, 10))
        for a in HALVES:
            tt(T.ct[:, 4 * a + 2:4 * (a + H):4], T.cx[:, a:a + H], T.ct[:, 4 * a:4 * (a + H):4], A.subtract, r=["cx", "cthi%d" % a], w=["ctlo%d" % a])
        for a in HALVES:
            quant("cq", a, a + H, "ct", 4 * a, ["cthi%d" % a, "ctlo%d" % a, "ct1", "ct3"], hk("cq", a))
        ts(T.off[:], bank(6, 0, NM), 160.0, None, A.add, r=[ps(6)], w=["off"])

    KS, KV = 6, {0: 3, H: 1}

    def table(h):
        mm(int(h == 1), NC, "kq", KW + 128 * h, "cq", 0)

    def copy_table(h):
        scopy(plane("cw", h), bank(int(h == 1)), float(M), r=[ps(int(h == 1))], w=["cw%d" % h])

    def digit_table(h):
        mm(2, NC, "kq", KD + 128 * h, "cq", 0)

    def copy_digits(h):
        o = 2 * NC * (h % 2)
        scopy(T.cd[:, o:o + 2 * NC:2], bank(2), r=[ps(2), "cdz"], w=["cd%d" % (h % 2)])

    def first_keys(a):
        tt(T.kr0[:, a:a + H], plane("cw", 0).indirect(T.off[:, a // 16:(a + H) // 16]), T.tier[:, a:a + H], A.add, r=["cw0", "off", "tier"], p=["kr0"])

    def count_teams(h, c):
        j, jk = junk(NC)
        src, key, o, own = (T.kr0[:], "kr0", 4, "pkc") if h == 1 else (bank(KS), ps(KS), 0, "pk")
        do("s", lambda: S.activation(j, src, F.Sign, bias=T.pk[:, o + c:o + c + 1], accum_out=T.cnt[:, c:c + 1]), r=[key, own], w=["cnt%d" % c, jk])

    def own_totals(h):
        tt(T.ogd[:], plane("cw", h).indirect(T.offo[:, 0:3]), T.diag[:, 0:48], A.mult, r=["cw%d" % h, "offo", "offo2", "diag"], w=["ogd"])

    def own_totals_picked():
        scan(T.os1[:], T.ogd[:], 48, r=["rst", "ogd"], w=["os1"])

    def own_totals_added(old):
        if old == "tiec":
            tt(T.pk[:, 4:7], T.tiec[:, 4:7], T.os1[:, 15:48:16], A.subtract, r=["os1", "tiecc"], w=["pkc"])
        tt(T.pk[:, 0:3], T[old][:, 0:3], T.os1[:, 15:48:16], A.subtract, r=["os1", old], w=["pk"])

    def own_offsets(c, src, key):
        a, b, ma, mb = block_of(c)
        ts(T.offm[:, a:b], T.mask[:, OWN + ma:OWN + mb], src, float(NC), A.max, A.add, r=["zm", key], p=["offm"])

    def grown(h):
        return ("gt", "gq", h - 1) if h < 5 else ("gu", "zq", h - 5)

    def keys_so_far(h):
        for k, a, n in ((KV[0], 0, H), (KS, 0, NC), (KV[H], H, H)):
            mm(k, n, "kq", K0, "g0", a, True, False)
            if h > 4:
                mm(k, n, "kq", KM, "gq", a, False, False)

    def keys_grow(h):
        o, (tile, _, e) = 2 * NC * (h % 2), grown(h)
        for a, cp in ((H, scopy), (0, vcopy)):
            cp(T[tile][:, 4 * a + e:4 * (a + H):4], T.cd[:, o:o + 2 * NC].indirect(T.offm[:, a // 16:(a + H) // 16]),
               r=["cd%d" % (h % 2), "offm", tile + "z"], w=[hk(tile, a)])

    def keys_added(h):
        tile, q, _ = grown(h)
        for a in HALVES:
            quant(q, a, a + H, tile, 4 * a, [hk(tile, a)], hk(q, a))
        mm(KV[0], H, "kq", KM, q, 0, False, True, hk(q, 0))
        mm(KS, NC, "kq", KM, q, 0, False, True)
        mm(KV[H], H, "kq", KM, q, H, False, True)

    def turned(k):
        if k == 0:
            do("v", lambda: V.transpose(T.it[:, 0:NC], T.ir[:, 16:16 + NC]), r=["ir"], p=["it"])
        else:
            do("v", lambda: V.transpose(T.it[:, NC:2 * NC + 32], T.ir[:, 0:NC + 32]), r=["ir", "irz0", "irz"], p=["it"])

    def beside(t, h, k):
        for x in BESIDE[t].get((h, k), "").split():
            n = int(x[1:] or 0)
            if x[0] == "p":
                vcopy(T.ir[:, 16:16 + NC].indirect(T.aoff[:, 10 * n:10 * n + 10]), T.iom[:, H * n:H * n + H], r=["aoff0", "aoff", "iom"], w=["ir"])
            elif x[0] == "t":
                turned(n)
            elif x[0] == "l":
                ts(T.inva[:], T.it[:, 0:2 * NC + 32].indirect(T.lt[:, 0:2]), 160.0, None, A.add, r=["it", "lt"], w=["inva"])
            elif x[0] == "e":
                ts(T.eb[:, 3:515:4], T.triv[:], 0.0, None, A.is_equal, r=["triv", "ebz"], w=["eb"])
            elif x[0] == "u":
                quantise_unpacking(n)
            else:
                quantise_row(n)

    def draft(t, PX):
        last = t == 1
        for n, a in enumerate(HALVES):
            mm(2 * n, H, "kq", KW, "cq", a, True, False, key=hk("cq", a))
            mm(2 * n, H, "kq", KD, "cq", a, False, True, key=hk("cq", a))
        table(1)
        for n, a in enumerate(HALVES):
            tt(plane("cw", 0, a, a + H), bank(2 * n, 0, H), T.tab0[:, a:a + H], A.add, r=[ps(2 * n), "tab0"], p=["cw0"])
        copy_table(1)
        digit_table(1)
        copy_digits(1)
        if t == 0:
            scopy(T.bg[:, 448:512], T.bd[:, 0:64], r=["bd", "bgz"], w=["bg"])
            quantise_row(4)
        own_totals(0)
        first_keys(0)
        own_totals_picked()
        first_keys(H)
        own_totals_added("tiec")
        if t == 0:
            quantise_row(5)
        small = [lambda k=k: list_of_turned_rows(k) for k in range(5)] if t == 0 else []
        for h in range(1, NG):
            own = h < NG - 1
            if h + 1 < NG - 1 or own and last:
                table(h + 1)
            if h + 1 < NG - 1:
                digit_table(h + 1)
            if t == 0 and h in UNPACK:
                unpack(2 * UNPACK.index(h), PX)
            ns = 3 if h == 1 else 2
            for c in range(ns):
                count_teams(h, c)
            if h == 1:
                for k in range(2):
                    ts(plane("kd", k), T.kr0[:], col(RA + k), col(RA + k), A.add, A.subtract, r=["kr0", "mg"], w=["kd%d" % k])
                own_offsets(0, T.cnt[:, 0:1], "cnt0")
                if t == 0:
                    quantise_row(6)
                run(T.gt[:, 0:4 * NC:4], plane("kd", 0), plane("kd", 1), 0.0, A.max, A.subtract, r=["kd0", "kd1", "gtz"], w=both("gt"))
                own_offsets(1, T.cnt[:, 1:2], "cnt1")
                if t == 0:
                    quantise_row(7)
                quant("g0", 0, NC, "gt", 0, both("gt"), "g0")
            else:
                for a in HALVES:
                    ts(plane("cb", 0, a, a + H), bank(KV[a], 0, H), T.pk[:, 2:3], 0.0, A.add, A.is_gt, r=[ps(KV[a]), "pk"], p=["cb"])
                beside(t, h, 0)
                run(plane("cb", 1), plane("cb", 0), plane("cb", 0), -float(NC), A.add, A.add, r=["cb"], w=["cbs"])
                if own:
                    own_offsets(0, T.cnt[:, 0:1], "cnt0")
                beside(t, h, 1)
            third, key = (T.cnt[:, 2:3], "cnt2") if ns == 3 else (plane("cb", 1, NC - 1, NC), "cbs")
            if own:
                keys_so_far(h)
                own_offsets(2, third, key)
            a, b, ma, mb = block_of(2)
            ts(slots(a, b), T.mask[:, HALF + ma:HALF + mb], third, None, A.mult, r=["mask8n", key], p=["xn"])
            if ns == 2 and (own or last):
                ts(T.offo[:, 2:3], third, 0.5, 160.0, A.mult, A.add, r=["cbs"], w=["offo2"])
            if ns == 2 and own:
                own_offsets(1, T.cnt[:, 1:2], "cnt1")
            for c in range(2):
                a, b, ma, mb = block_of(c)
                scopy(slots(a, b), T.mask[:, HALF + ma:HALF + mb], T.cnt[:, c:c + 1], r=["mask8n", "cnt%d" % c], p=["xn"])
                if c == 0 and (h + 1 < NG - 1 or own and last):
                    copy_table(h + 1)
            if own or last:
                ts(T.offo[:, 0:ns], T.cnt[:, 0:ns], 0.5, 160.0, A.mult, A.add, r=["cnt%d" % c for c in range(ns)], w=["offo"])
            if own:
                if small:
                    small.pop(0)()
                keys_grow(h)
                own_totals(h)
                digits()
                keys_added(h)
                own_totals_picked()
                if t == 0 and h == 1:
                    constants(KG, 240, "bg", 0, ["bg"])
                else:
                    spread(h)
                own_totals_added("pk")
                if t == 0 and h == 1:
                    spread(h)
                if small:
                    small.pop(0)()
                beside(t, h, 2)
            else:
                digits()
                spread(h)
            if h + 1 < NG - 1:
                copy_digits(h + 1)
            if t == 0:
                row(2 * h + 8, 2 * h + 9)
            if t == 0 and h in UNPACK:
                unpacked(2 * UNPACK.index(h))
            for k in SORT[t].get(h, ()):
                scopy(plane("fs", k), plane("fp", k).indirect(T.inva[:, 0:NM]), r=["fp%d" % k, "inva"], w=["fs%d" % k])

    def layer(t):
        X, PY, YQ = "xq%d" % t, "py%d" % t, "yq%d" % t
        last = t == 1
        ts(T.noff[:], bank(7, 0, NM), 160.0, None, A.add, r=[ps(7)], w=["noff"])
        for k in range(4):
            for cp, a, b in ((vcopy, 0, ZS[k]), (scopy, ZS[k], NM)):
                if a < b:
                    cp(T.zt[:, 64 * a + k:64 * b:4], plane("fs", k).indirect(T.noff[:, a:b]), r=["fs%d" % k, "noff"], p=["zt"])
        vcopy(T.sr[:, 0:NC].indirect(T.noff[:, 0:NM]), T.iom[:], r=["noff", "iom"], w=["sr"])
        quant("zq", 0, NC, "zt", 0, ["zt"], both("zq"))
        for b in (4, 5, 0, 6, 1, 7, 2, 3):
            mm(b, NC, "ww", 128 * b, "zq", 0)
            if b >= 4:
                scopy(plane("cc", b - 4), bank(b), r=[ps(b)], w=["cc%d" % (b - 4)])
        tt(plane("rk", 0), T.sr[:, 0:NC].indirect(T.aoff[:, 0:NM]), T.diag[:], A.mult, r=["sr", "aoff0", "aoff", "diag"], w=["rk0"])
        scan(plane("rk", 1), plane("rk", 0), r=["rst", "rk0"], w=["rk1"])
        for b in range(4):
            tt(plane("yp", b), bank(b), plane("cc", b), A.max, r=[ps(b), "cc%d" % b], w=["yp%d" % b])
            if b == 0:
                ts(T.koff[:], T.rk[:, NC + 15:2 * NC:16], 160.0, None, A.add, r=["rk1"], w=["koff"])
        for a in HALVES:
            for k in range(4):
                out, src = T.yt[:, 4 * a + k:4 * (a + H):4], plane("yp", k).indirect(T.koff[:, a // 16:(a + H) // 16])
                if k < YS[a > 0]:
                    scopy(out, src, 0.03125, r=["yp%d" % k, "koff"], p=["yt%d" % a])
                else:
                    ts(out, src, 0.03125, None, A.mult, r=["yp%d" % k, "koff"], p=["yt%d" % a])
            quant(YQ, a, a + H, "yt", 4 * a, ["yt%d" % a], hk(YQ, a))
            send_half(t, PY, YQ, a)
        if last:
            own_totals(NG - 1)
            own_totals_picked()
            own_totals_added("pk")
            tt(T.tsb[:, 0:3], T.tiec[:, 0:3], T.pk[:, 0:3], A.subtract, r=["pk", "tiec"], w=["tsb"])
            ts(T.tsb[:, 8:11], T.tsb[:, 0:3], 1.0 / M, MG1, A.mult, A.add, r=["tsb"], w=["tsm"])
            sline(T.tsb[:, 4:7], T.tsb[:, 8:11], 1.0, -MG1, r=["tsm"], w=["tot"])
            for c in range(3):
                a = 128 * c - PIECE[c]
                dma("sy", T.tot[:, 128 * c:128 * c + 128 - a], T.tsb[a:128, 4 + c:5 + c], r=["tot"] + both(PY))
        else:
            quant("vq", 0, 128, "vt", 0, ["vt"])
        NX = "xq%d" % (t + 1)
        for n, a in enumerate(HALVES):
            for b in range(4):
                mm(4 * n + b, H, "kq", KE + 128 * b, X, a, True, False, hk(X, a))
        for n, a in enumerate(HALVES):
            for b in range(4):
                mm(4 * n + b, H, "kq", KE + 128 * b, PY, a, False, True, hk(PY, a))
        for n, a in enumerate(HALVES):
            for b in range(4):
                cp = scopy if b % 2 else vcopy
                cp(T.xt1[:, 4 * a + b:4 * (a + H):4], bank(4 * n + b, 0, H), r=[ps(4 * n + b)], p=["xt1%d" % a])
            quant(NX, a, a + H, "xt1", 4 * a, ["xt1%d" % a], hk(NX, a))
            if last and n:
                store_y(0, 0)
            if last:
                store(n, a)
            else:
                send_half(1, "px1", NX, a)

    def store(n, a):
        key = hk("xq2", a)
        mm(4 * n, H, "vq", 0, "xq2", a, key=key)
        dma("sy", T.oc[:, 4 * a:4 * (a + H)], codes("xq2", a, a + H), r=[key])

    def store_y(n, a):
        vcopy(T.ysb[:, a:a + H], bank(4 * n, 0, H), r=[ps(4 * n)], w=["ysb%d" % a])
        dma("s" if n else "sy", T.y[:, a:a + H], T.ysb[:, a:a + H], r=["ysb%d" % a])

    dma("sy", T.xt0[:, 0:4 * H], T.x[:, 0:4 * H], w=["xt0%d" % 0])
    dma("sy", T.ut[:, :], T.u[:, :], w=["ut"])
    dma("sy", T.xt0[:, 4 * H:4 * NC], T.x[:, 4 * H:4 * NC], w=["xt0%d" % H])
    while_x_comes()
    quant("xq0", 0, H, "xt0", 0, ["xt0%d" % 0], hk("xq0", 0))
    send_half(0, "px0", "xq0", 0)
    while_u_comes()
    quant("uq", 0, 128, "ut", 0, ["ut"])
    before_u_is_picked()
    do("v", lambda: V.tensor_copy(T.upc[:, 0:384].bitcast(dt.uint32), T.uqc[:, 0:128].bitcast(dt.uint32).indirect(T.lu[:, 0:24])), r=["uq", "lu"], p=["up"])
    do("s", lambda: S.activation(T.ups[:, 0:384], T.uqs[:, 0:128].indirect(T.lu[:, 0:24]), F.Copy), r=["uq", "lu"], p=["up"])
    quant("xq0", H, NC, "xt0", 4 * H, ["xt0%d" % H], hk("xq0", H))
    send_half(0, "px0", "xq0", H)
    behind_the_first_writes()
    dma("sy", codes("ww", 0, 1024), T.wc[:, :], r=both("px0"), p=["ww"])
    dma("sy", T.wws[:, :], T.ws[:, :], p=["ww"])
    dma("sy", T.vt[:, :], T.v[:, :], w=["vt"])
    for t in range(2):
        PX = "px%d" % t
        own_scores("xq%d" % t)
        if t == 0:
            while_own_scores_come()
        else:
            before_the_second_draft()
        own_places()
        own_sums()
        places(t, PX)
        draft(t, PX)
        layer(t)
    for k in range(4):
        dma("sy", T.osc[4 * k:4 * k + 4, :], T.xq2s[32 * k:32 * k + 4, 0:NC], r=both("xq2"))
    store_y(1, H)

    for s in ("v", "s", "t", "gp"):
        g.sync.wait_ge(T.sem[s], count[s])
    for k in range(tally["dma"]):
        g.sync.wait_ge(T.sem["d%d" % k], 16)
    for s, n in arrivals:
        g.sync.wait_ge(T.sem[s], n)
    g.sync.wait_ge(T.sem["ls"], tally["ls"])
